import numpy as np, ml_dtypes
CORES = [35,38,43,46]
N = 4
import mx_ref
BF = ml_dtypes.bfloat16
def entries(a):
    return np.ascontiguousarray(a.T).reshape(-1)
def table(e):
    return np.ascontiguousarray(np.reshape(e, (-1, 16)).T).astype(np.int32)
def pick(q, e):
    c = np.concatenate([q[0].reshape(128, -1, 4), np.zeros((128, 1, 4), np.uint8)], axis=1); s = np.concatenate([q[1], np.ones((16, 1), np.uint8)], axis=1)
    return (np.ascontiguousarray(c[:, e].reshape(128, -1)), np.ascontiguousarray(s[:, e]))
def join(*qs):
    return (np.concatenate([q[0] for q in qs], axis=1), np.concatenate([q[1] for q in qs], axis=1))
def put(q, e, v):
    c, s = q[0].reshape(128, -1, 4).copy(), q[1].copy(); c[:, e] = v[0].reshape(128, -1, 4); s[:, e] = v[1]
    return (c.reshape(128, -1), s)
def pk(c, s):
    return (np.ascontiguousarray(c), mx_ref.live(s))
def emit(q):
    return q[0], q[1]
def decode(q):
    o = []
    for b in range(4):
        e = np.zeros((128, 128, 4), np.float32); e[np.arange(128), np.arange(128), b] = 1
        o.append(mx_ref.matmul(mx_ref.quantize(e.reshape(128, 512).astype(BF)), q))
    return np.stack(o, axis=2).reshape(128, -1)
def f(rng, *shape):
    return mx_ref.flush((rng.standard_normal(shape, dtype=np.float32) * np.exp2(rng.integers(-2, 3, shape[:-1] + (1,)))).astype(BF))
def wide(rng, *shape, cols=0):
    v = rng.standard_normal(shape, dtype=np.float32) * np.exp2(rng.integers(-12, 13, shape)).astype(np.float32)
    if cols: v *= np.repeat(np.exp2(rng.integers(-cols, cols + 1, shape[:-2] + (1, shape[-1] // 4))) * (rng.random(shape[:-2] + (1, shape[-1] // 4)) > 0.0625), 4, axis=-1).astype(np.float32)
    return mx_ref.flush(v.astype(BF))
P, F, R = 256, 48, 3
def big(v):
    v = np.array(v, np.float32)
    v[np.abs(v) < np.float32(2.0 ** -16)] = 0
    return v.astype(BF)
def share(v):
    return big(np.ascontiguousarray(v.reshape(128, N, 4 * P).transpose(1, 0, 2)))
def links(nb):
    return np.concatenate([entries(nb[r]).reshape(P, 3) for r in range(N)])
def graph(rng, ends=False):
    to, far, n = np.zeros((N * P, 3), int), [], P - (N - 1) * F
    for r in range(N):
        a, i = P * r + rng.permutation(P), 0
        while i < P:
            m = min(2 * int(rng.integers(2, 17)), P - i)
            if P - i - m < 4: m = P - i
            for k in range(2):
                c = np.roll(a[i:i + m], -k)
                to[c[0::2], k], to[c[1::2], k] = c[1::2], c[0::2]
            i += m
        if ends:
            h = rng.permutation(a[a < to[a, 0]])[:n]
            e = np.where(rng.random(n) < 0.5, h, to[h, 0])
        else: e = rng.permutation(a)[:n]
        far.append(rng.permutation(np.setdiff1d(a, e)).reshape(N - 1, F))
        for i in range(0, n, 2):
            if e[i + 1] in to[e[i], :2]:
                for j in range(0, n, 2):
                    if j != i and e[j + 1] not in to[e[i], :2] and e[i + 1] not in to[e[j], :2]:
                        e[i + 1], e[j + 1] = e[j + 1], e[i + 1]
                        break
        to[e[0::2], 2], to[e[1::2], 2] = e[1::2], e[0::2]
    for r in range(N):
        for q in range(r + 1, N):
            u, v = far[r][q - 1], far[q][r]
            to[u, 2], to[v, 2] = v, u
    return to
def inputs(rng, x, to):
    return {"x": x, "nb": np.stack([table(to[P * r:P * r + P].reshape(-1)) for r in range(N)]), "w": f(rng, N, 128, 512)}
def setup_inputs(rng):
    return inputs(rng, big(f(rng, N, 128, 4 * P)), graph(rng))
def setup_inputs_far(rng):
    to, n = graph(rng), np.arange(N * P)
    v = (1 + 0.5 * rng.random((128, N * P, 4))) * rng.choice([-1.0, 1.0], (128, N * P, 4))
    a = n[(to[:, 2] // P != n // P) & (n < to[:, 2])]
    b = to[a, 2]
    v[:, b] = np.abs(v[:, b]) * np.sign(v[:, a]) * np.where(rng.random((128, a.size, 4)) < 0.125, -1.0, 1.0)
    return inputs(rng, share(v), to)
def setup_inputs_none(rng):
    to, n, z = graph(rng, ends=True), np.arange(N * P), int(rng.integers(0, N))
    own = n // P == z
    size = np.where(own & (to[:, 2] // P == z), 0.125, 1.0)
    color = np.full(N * P, -1)
    for a in n[n < to[:, 0]]:
        both = np.array([a, to[a, 0]])
        near = color[to[both, 1:]].reshape(-1).tolist()
        color[both] = next(int(c) for c in rng.permutation(5) if c not in near)
    v = rng.choice([-1.0, 1.0], (128, N * P, 4))
    a = n[(to[:, 2] // P != n // P) & (n < to[:, 2])]
    v[:, to[a, 2]] = v[:, a]
    v[:40] = np.where((np.arange(40) // 8)[:, None, None] == color[None, :, None], 8.0, 0.0)
    v[40:48] = 64.0
    v = np.where(own[None, :, None], (1 + 0.5 * rng.random((128, N * P, 4))) * size[None, :, None], 16.0 * v)
    return inputs(rng, share(v), to)
def setup_inputs_spread(rng):
    return inputs(rng, big(wide(rng, N, 128, 4 * P, cols=6)), graph(rng))
def setup_inputs_ties(rng):
    to = graph(rng)
    t = f(rng, 128, 12).astype(np.float32).reshape(128, 3, 4)
    five = np.concatenate([t, 0 - t[:, :1], np.zeros((128, 1, 4), np.float32)], axis=1)
    e = rng.integers(0, 5, N * P)
    for r in range(N):
        j = P * r + int(rng.integers(0, P))
        e[to[j]] = 0
        e[to[to[j]].reshape(-1)] = 0
    return inputs(rng, share(five[:, e]), to)
def setup_inputs_twice(rng):
    to, large = graph(rng), np.zeros(N * P, bool)
    v = np.abs(rng.standard_normal((128, N * P, 4))) * np.exp2(rng.integers(-1, 2, (1, N * P, 1)))
    for i in range(P // 32):
        for r in rng.permutation(N):
            for j in rng.permutation(P):
                n1 = P * r + j
                n2 = to[n1, 1]
                p = np.array([to[n1, 0], n1, n2, to[n2, 0]])
                if i == 0:
                    m = to[[n1, n2], 2]
                    q = np.concatenate([p, m])
                    if large[q].any() or large[to[q]].any() or np.count_nonzero(np.isin(to[q], q)) != 10: continue
                    size = np.concatenate([rng.choice([1.0, 1.25], (128, 4, 4)), rng.choice([3.5, 4.0], (128, 2, 4))], axis=1) * 2.0 ** 26
                    v[:, q] = size * rng.choice([-1.0, 1.0], (128, 1, 4)) * np.array([1.0, 1.0, -1.0, -1.0, -1.0, 1.0])[None, :, None]
                    large[q] = True
                    large[to[m]] = True
                    break
                if large[p].any() or large[to[p]].any() or np.isin(to[p, 2], p).any() or to[p[0], 1] == p[3]: continue
                large[p] = True
                v[:, p] = (1 + 0.5 * rng.random((128, 4, 4))) * np.array([256.0, 64.0, 64.0, 256.0])[None, :, None]
                break
    return inputs(rng, share(v), to)
def check_inputs(d):
    b = []
    for k, low, high in (("x", -16, 28), ("w", -30, 30)):
        v = np.abs(d[k].astype(np.float32))
        if not (np.isfinite(v).all() and ((v == 0) | (v >= 2.0 ** low) & (v <= 2.0 ** high)).all()): b.append("a value of " + k)
    to, n = links(d["nb"]), np.arange(N * P)
    if to.min() < 0 or to.max() >= N * P: return b + ["range of nb"]
    for k in range(3):
        if (to[to[:, k], k] != n).any() or (to[:, k] == n).any(): b.append("edges k = %d are no pairs" % k)
    if (to[:, :2] // P != n[:, None] // P).any(): b.append("an edge k = 0 or 1 leaves its rank")
    if (to[:, 0] == to[:, 1]).any() or (to[:, 0] == to[:, 2]).any() or (to[:, 1] == to[:, 2]).any(): b.append("two edges of a node lead to the same node")
    c = np.zeros((N, N), int)
    np.add.at(c, (n // P, to[:, 2] // P), 1)
    if (c[~np.eye(N, dtype=bool)] != F).any(): b.append("number of edges between two ranks")
    return b
def scores(h, to):
    s = np.zeros((N * P, 3), np.float32)
    for i in range(0, N * P, 128):
        a = pick(h, np.arange(i, i + 128))
        for k in range(3): s[i:i + 128, k] = np.diagonal(mx_ref.matmul(a, pick(h, to[i:i + 128, k]))) + np.float32(0)
    return s
def reference(x, nb, w):
    to, n = links(nb), np.arange(N * P)
    h = join(*[mx_ref.quantize(np.ascontiguousarray(x[r])) for r in range(N)])
    merged, pr = np.zeros((N * P, 3), bool), np.zeros((N, R, P), np.float32)
    for t in range(R):
        s = scores(h, to)
        s[merged] = -np.inf
        c = np.argmax(s, axis=1)
        v = to[n, c]
        met = c[v] == c
        merged[n[met], c[met]] = True
        pr[:, t] = np.where(met, v, -1).reshape(N, P)
        d = decode(h).reshape(128, N * P, 4)
        m = np.float32(0.5) * d + np.float32(0.5) * d[:, np.where(met, v, n)]
        new = mx_ref.quantize(np.ascontiguousarray(m.reshape(128, -1).astype(BF)))
        h = pick(join(h, new), np.where(met, N * P + n, n))
    oc, osc, y = np.zeros((N, 128, 4 * P), np.uint8), np.zeros((N, 16, P), np.uint8), np.zeros((N, 128, P), np.float32)
    for r in range(N):
        own = pick(h, np.arange(P * r, P * r + P))
        oc[r], osc[r] = emit(own)
        y[r] = mx_ref.matmul(mx_ref.quantize(np.ascontiguousarray(w[r])), own)
    return {"oc": oc, "osc": osc, "pr": pr, "y": y}

@@ -1,0 +1,488 @@
+from concourse.bass import DstId, RemoteDMATransfer
+from concourse.mybir import dt, AluOpType as A, AxisListType, ActivationFunctionType as AF
+
+P, F, R = 256, 48, 3
+FAR = {1: (0, 48), 3: (160, 208), 2: (208, 256)}
+LOC = (48, 160)
+BIG = 1e29
+BANKS = ((4, 5, 6, 7), (4, 5, 6, 7), (2, 3, 0, 1))
+CODE = (0.25, 0.5, 5.0)
+
+
+def _bufs():
+    b = {}
+    def sb(name, n, d="float32"): b[name] = ("sbuf", [128, n], d)
+    def mx(name, n):
+        sb(name + "c", n, "float8_e4m3fn_x4")
+        sb(name + "s", n, "uint8")
+    sb("nbT", 48, "int32"); sb("xb", 1024, "bfloat16"); sb("wb", 512, "bfloat16")
+    mx("X", 256); mx("wq", 128); mx("E", 512); mx("Z", 256)
+    for t in range(R):
+        mx("W%d" % t, 1024); mx("N%d" % t, 512); mx("M%d" % t, 256)
+        sb("fl%d" % t, 4); sb("m01_%d" % t, 2); sb("RC%d" % t, 256, "bfloat16"); sb("CD%d" % t, 1024, "bfloat16"); sb("CT%d" % t, 1024, "bfloat16")
+        sb("S%d" % t, 48); sb("Eq%d" % t, 48); sb("Fd%d" % t, 64); sb("F2%d" % t, 32); sb("L%d" % t, 16); sb("U%d" % t, 16, "uint16")
+        sb("pt%d" % t, 32); sb("pu%d" % t, 32); sb("e6_%d" % t, 6)
+    for k in range(3): sb("h%d" % k, 1024, "bfloat16")
+    sb("half", 512, "bfloat16"); sb("hE", 2048, "bfloat16")
+    for name, n in (("pI", 1), ("rI", 1), ("gI", 1), ("uI", 1), ("yI", 256), ("wI", 256), ("rhoI", 1), ("zI", 48),
+                    ("vI", 64), ("aI", 64), ("nbI", 48), ("vN", 64), ("aN", 64), ("kI", 16), ("kA", 16), ("kL", 16), ("kB", 16), ("pv", 16), ("pv0", 16), ("pv1", 16)): sb(name, n, "int32")
+    for name, n in (("one", 128), ("I", 128), ("mF", 256), ("ju", 256), ("rF", 1), ("gF", 1), ("gG", 1), ("me", 1), ("mo", 1), ("pF", 1), ("rho", 1), ("c16", 16), ("cd", 16), ("o48", 48), ("z48", 48), ("z3", 48), ("M48", 48), ("jR", 256),
+                    ("Fw", 1024), ("mk", 48), ("t2a", 16), ("T2", 16), ("RK", 256), ("dk", 256), ("nK", 2), ("sg", 2), ("jk", 512), ("Tn", 16), ("nd0", 16), ("nd", 16), ("md", 16), ("mn", 16),
+                    ("kh", 16), ("k1", 16), ("kap", 16), ("kapn", 16), ("kh2", 16), ("k12", 16), ("kap2", 16), ("u0", 8), ("u1", 8), ("p3", 16), ("hP", 48), ("kP", 48), ("lP", 48), ("lQ", 48), ("xP", 24), ("yP", 24), ("dP", 48),
+                    ("hN", 64), ("kN", 64), ("lN", 64), ("lO", 64), ("xN", 32), ("yN", 32), ("dN2", 64), ("posF", 16), ("lo", 16), ("lo1", 16), ("lo2", 16), ("df", 16), ("df2", 16), ("Dp", 64), ("Dn", 64), ("K2", 48), ("Bm", 48), ("c8", 48),
+                    ("MK", 4), ("mk0", 4), ("mk1", 4), ("mk2", 4), ("CP", 6), ("dg", 768), ("dh", 512), ("Sc", 6), ("sm", 4), ("ge", 2), ("c01", 2), ("m01c", 2), ("ncp", 2), ("mxa", 1), ("mxc", 2), ("Af", 2), ("Bf", 2),
+                    ("EB", 48), ("e24", 24), ("e12", 12), ("cpn", 6), ("io", 1024), ("Rn", 768), ("dR", 768), ("tR", 768), ("NB1", 48),
+                    ("fp", 48), ("f1", 16), ("f2", 16), ("yo", 256), ("En0", 48), ("En1", 48), ("q4", 6), ("q6", 6), ("qa", 2), ("qb", 2), ("qc", 2)): sb(name, n)
+    for name, n in (("TS", 64), ("TT", 64), ("Rp", 256), ("dA", 256), ("tA", 256), ("iJ", 256), ("Rpi", 256), ("dB", 256), ("tB", 256), ("Rpn", 256), ("Rq", 768), ("d2", 768), ("t2", 768),
+                    ("dn", 768), ("tn", 768), ("TC", 64), ("TD", 64), ("TP", 64), ("TQ", 64), ("RP", 256), ("dPr", 256), ("tPr", 256)): sb(name, n, "bfloat16")
+    for name, n in (("T2u", 16), ("lA", 16), ("lB", 16), ("lM", 16), ("posU", 16), ("piU", 16), ("nbL", 48), ("nbU", 48), ("lG", 48), ("lH", 48), ("nU", 32), ("n2U", 8), ("CLp", 64), ("CLn", 64)): sb(name, n, "uint16")
+    for i in range(8): b["ps%d" % i] = ("psum", [128, 512], "float32")
+    return b
+
+
+def _pack(b):
+    out, place, fill = {}, {}, {"float32": 0, "int32": 0, "uint16": 0, "bfloat16": 0}
+    fixed = ("nbT", "xb", "wb", "hE", "half", "h0", "h1", "h2", "fl0", "fl1", "fl2", "m01_0", "m01_1", "m01_2")
+    for name, (where, shape, d) in b.items():
+        place[name] = (name, 0)
+        if where != "sbuf" or d not in fill or name in fixed: out[name] = (where, shape, d)
+        else:
+            place[name] = ("pool_" + d, fill[d])
+            fill[d] += (shape[1] + 31) // 32 * 32
+    for d, n in fill.items(): out["pool_" + d] = ("sbuf", [128, n], d)
+    return out, place
+
+
+SCRATCH, PLACE = _pack(_bufs())
+WIDTH = {k: v[1][1] for k, v in _bufs().items()}
+SEMAPHORES = ["qv", "qs", "qt", "qg", "ldn", "ldx", "ldw", "ls", "st", "pst"] + ["x%s%d" % (k, t) for k in "csm" for t in range(R)]
+
+
+def shares(T, topo, core):
+    peer = {d: T.cores[T.rank_of(core) ^ d] for d in FAR}
+    may = {d: topo.engines(core, c) for d, c in peer.items()}
+    away = [d for d in FAR if topo.chip(peer[d]) != topo.chip(core)]
+    eng, used = {}, []
+    for d in sorted(FAR, key=lambda d: (d not in away, d)):
+        free = [e for e in may[d] if e not in used]
+        eng[d] = free[:len(may[d]) // len(away)] if d in away else free[::2][:4]
+        used += eng[d]
+    return peer, eng
+
+
+def rank_program(g, core, T, topo):
+    rank = T.rank_of(core)
+    if rank is None: return
+    queues = {"v": g.vector, "s": g.scalar, "t": g.tensor, "g": g, "y": g.sync}
+    qsem = {"v": "qv", "s": "qs", "t": "qt", "g": "qg"}
+    count = {k: 0 for k in qsem.values()}
+    known = {q: {} for q in queues}
+    writes, reads = {}, {}
+
+    def norm(r): return (r[0], r[1], r[2], r[3] if len(r) > 3 else 1)
+
+    def clash(x, y):
+        if x[2] <= y[1] or y[2] <= x[1]: return False
+        return not (x[3] == y[3] and x[3] > 1 and (x[1] - y[1]) % x[3])
+
+    def need(q, rd, wr, acc=False):
+        evs = []
+        for r in map(norm, rd): evs += [e for w, e in writes.get(r[0], []) if clash(w, r)]
+        for r in map(norm, wr):
+            evs += [e for w, e in writes.get(r[0], []) if clash(w, r) and not (acc and e[3] == "t")]
+            evs += [e for w, e in reads.get(r[0], []) if clash(w, r)]
+        evs.sort(key=lambda e: -e[1])
+        for sem, val, snap, _q in evs:
+            if known[q].get(sem, 0) >= val: continue
+            queues[q].wait_ge(T.sem[sem], val)
+            known[q][sem] = val
+            for k, v in snap.items(): known[q][k] = max(known[q].get(k, 0), v)
+
+    def note(ev, rd, wr):
+        for r in rd: reads.setdefault(r[0], []).append((norm(r), ev))
+        for r in map(norm, wr):
+            inside = lambda w: w[1] >= r[1] and w[2] <= r[2] and r[3] == 1
+            writes[r[0]] = [(w, e) for w, e in writes.get(r[0], []) if not inside(w)] + [(r, ev)]
+            reads[r[0]] = [(w, e) for w, e in reads.get(r[0], []) if not inside(w)]
+
+    def run(q, fn, rd, wr, acc=False):
+        need(q, rd, wr, acc)
+        sem = qsem[q]
+        count[sem] += 1
+        fn(queues[q]).then_inc(T.sem[sem], 1)
+        note((sem, count[sem], dict(known[q]), q), rd, wr)
+
+    def arrives(sem, val, wr): note((sem, val, {}, "d"), [], wr)
+
+    def ap(r, p=None):
+        name, a, b, st = norm(r)
+        buf, o = PLACE[name]
+        rows = slice(p[0], p[1]) if p else slice(None)
+        return T[buf][rows, o + a:o + b:st] if st != 1 else T[buf][rows, o + a:o + b]
+
+    def words(r): return ap(r).bitcast(dt.uint32)
+    def octets(r): return ap(r).bitcast(dt.uint8)
+    def W(n): return (n, 0, WIDTH[n])
+    def sc(s): return ap(s) if isinstance(s, tuple) else s
+    def tt(out, in0, in1, op): run("v", lambda e: e.tensor_tensor(ap(out), ap(in0), ap(in1), op), [in0, in1], [out])
+    def ts(out, in0, s1, op0, s2=None, op1=None):
+        rd = [in0] + [s for s in (s1, s2) if isinstance(s, tuple)]
+        if op1 is None: run("v", lambda e: e.tensor_scalar(ap(out), ap(in0), sc(s1), None, op0), rd, [out])
+        else: run("v", lambda e: e.tensor_scalar(ap(out), ap(in0), sc(s1), sc(s2), op0, op1), rd, [out])
+    def cp(out, in_, q="v"):
+        if q == "v": run("v", lambda e: e.tensor_copy(ap(out), ap(in_)), [in_], [out])
+        else: run("s", lambda e: e.activation(ap(out), ap(in_), AF.Copy), [in_], [out])
+    def ms(out, c): run("v", lambda e: e.memset(ap(out), c), [], [out])
+    def rsum(out, in_, negate=False): run("v", lambda e: e.tensor_reduce(ap(out), ap(in_), AxisListType.X, A.add, negate=negate), [in_], [out])
+    def tp(out, in_, p=None): run("v", lambda e: e.transpose(ap(out, p), ap(in_, p)), [in_], [out])
+    def gather(out, win, off, q="v"):
+        if q == "v": run("v", lambda e: e.tensor_copy(ap(out), ap(win).indirect(ap(off))), [win, off], [out])
+        else: run("s", lambda e: e.activation(ap(out), ap(win).indirect(ap(off)), AF.Copy), [win, off], [out])
+    def pick(out, win, off):
+        oc, wc, os_, ws = [(r[0] + x, r[1], r[2]) for x in "cs" for r in (out, win)]
+        run("v", lambda e: e.tensor_copy(words(oc), words(wc).indirect(ap(off))), [wc, off], [oc])
+        run("s", lambda e: e.activation(ap(os_), ap(ws).indirect(ap(off)), AF.Copy), [ws, off], [os_])
+    def quant(out, in_):
+        c, s = (out[0] + "c", out[1], out[2]), (out[0] + "s", out[1], out[2])
+        run("v", lambda e: e.quantize_mx(ap(c), ap(s), ap(in_)), [in_], [c, s])
+    def mm(bank, n, w, x, start=True, stop=True):
+        wc, ws, xc, xs = (w[0] + "c", w[1], w[2]), (w[0] + "s", w[1], w[2]), (x[0] + "c", x[1], x[2]), (x[0] + "s", x[1], x[2])
+        run("t", lambda e: e.matmul_mx(ap(("ps%d" % bank, 0, n)), ap(wc), ap(ws), ap(xc), ap(xs), start, stop), [wc, ws, xc, xs], [("ps%d" % bank, 0, 512)], acc=not start)
+    def iota(out, pattern, base, cm):
+        if PLACE[out[0]][0] == "pool_int32": run("g", lambda e: e.iota(ap(out), pattern, base, cm), [], [out])
+        else: run("g", lambda e: e.iota(ap(out), pattern, base, cm, allow_small_or_imprecise_dtypes=True), [], [out])
+    def settle():
+        if known["g"].get("qg", 0) < count["qg"]: g.wait_ge(T.sem.qg, count["qg"])
+        known["g"]["qg"] = count["qg"]
+    def pb(out, in_, p): run("g", lambda e: e.partition_broadcast(ap(out), ap(in_, (p, p + 1)), 128), [in_], [out])
+    def spread(row, col):
+        settle()
+        for a in range(4): pb((row, 64 * a, 64 * a + 64), (col, 0, 64), 32 * a)
+
+    peer, eng = shares(T, topo, core)
+    incoming = sum(len(shares(T, topo, c)[1][d]) for d, c in peer.items())
+    sent = [0]
+
+    def send(what, sem):
+        tr = []
+        for d in eng:
+            src, dst, region = what(d)
+            need("g", [region], [])
+            rid, pid, _s = topo.addr(peer[d])
+            tr.append(RemoteDMATransfer(dst_ids=[DstId(rid=rid, pnc=pid)], dma_engine_mask=sum(1 << e for e in eng[d]), remote_sem=T.sem[sem], src=src, dst=dst))
+            sent[0] += len(eng[d])
+        g.remote_dma_fused(tr, local_sem=T.sem.ls)
+
+    for i in range(8):
+        q = g.sync if i % 2 == 0 else g.scalar
+        q.dma_start(T.nbT[16 * i:16 * i + 16, :], T.nb[:, :]).then_inc(T.sem.ldn, 16)
+    arrives("ldn", 128, [W("nbT")])
+    g.sync.dma_start(T.xb[:, :], T.x[:, :]).then_inc(T.sem.ldx, 16)
+    arrives("ldx", 16, [W("xb")])
+    g.sync.dma_start(T.wb[:, :], T.w[:, :]).then_inc(T.sem.ldw, 16)
+    arrives("ldw", 16, [W("wb")])
+
+    iota(W("pI"), [[0, 1]], 0, 1)
+    iota(W("o48"), [[0, 16], [1, 3]], 0, 0)
+    iota(W("yI"), [[0, 16], [11, 16]], 10, 0)
+    iota(W("ju"), [[16, 16], [0, 16]], 0, 0)
+    iota(W("mF"), [[1, 256]], 0, 0)
+    ms(W("one"), 1.0)
+    for q in range(4):
+        c, r = q ^ rank ^ 1, ("Fw", 256 * q, 256 * q + 256)
+        if q < rank: run("s", lambda e: e.activation(ap(r), ap(W("mF")), AF.Identity, bias=65536.0 * c, scale=256.0), [W("mF")], [r])
+        else: ms(r, 65536.0 * c)
+    cp(W("iJ"), W("mF"), "s")
+    ms(W("TS"), 0.0)
+    ms(W("half"), 0.5)
+    run("g", lambda e: e.affine_select(ap(W("I")), ap(W("one")), [[-1, 128]], A.is_equal, 0.0, 0, 1), [W("one")], [W("I")])
+    iota(W("cd"), [[2, 8], [0, 2]], 0, 0)
+    iota(W("c16"), [[16, 16]], 0, 0)
+    def etile(b):
+        out = ("hE", 512 * b, 512 * b + 512)
+        settle()
+        run("g", lambda e: e.affine_select(ap(out), ap(W("half")), [[1, 512]], A.is_equal, 0.0, -b, -4), [W("half")], [out])
+    for b in range(2): etile(b)
+    ts(W("rI"), W("pI"), 15, A.bitwise_and)
+    ts(W("gI"), W("pI"), 4, A.logical_shift_right)
+    cp(W("rF"), W("rI"))
+    ts(W("uI"), W("gI"), 1, A.bitwise_and)
+    ts(W("z48"), W("o48"), W("rF"), A.add, 1.0, A.add)
+    ts(W("zI"), W("z48"), 1.0 / 3.0, A.mult)
+    ts(W("z3"), W("zI"), 3.0, A.mult)
+    tt(W("M48"), W("z3"), W("z48"), A.is_equal)
+    ts(W("wI"), W("yI"), 15, A.bitwise_and)
+    tt(W("jR"), W("wI"), W("ju"), A.add)
+
+    tt(W("mk"), W("nbT"), W("M48"), A.mult)
+    tt(W("t2a"), ("mk", 0, 48, 3), ("mk", 1, 48, 3), A.add)
+    tt(W("T2"), W("t2a"), ("mk", 2, 48, 3), A.add)
+    cp(W("T2u"), W("T2"))
+    run("v", lambda e: e.tensor_tensor(ap(W("RK")), ap(W("Fw")).indirect(ap(W("T2u"))), ap(W("jR")), A.add), [W("Fw"), W("T2u"), W("jR")], [W("RK")])
+    for h in range(2):
+        d = ("dk", 128 * h, 128 * h + 128)
+        tt(d, ("RK", 128 * h, 128 * h + 128), W("I"), A.mult)
+        rsum(("nK", h, h + 1), d, negate=True)
+        jk, b, o = ("jk", 256 * h, 256 * h + 256), ("nK", h, h + 1), ("sg", h, h + 1)
+        run("s", lambda e: e.activation(ap(jk), ap(W("RK")), AF.Sign, bias=ap(b), accum_out=ap(o)), [W("RK"), b], [jk, o])
+    ts(W("rhoI"), W("rF"), 3.0, A.mult, 2.0, A.add)
+    ts(W("rhoI"), W("rhoI"), 15, A.bitwise_and)
+    cp(W("gF"), W("uI"))
+    ts(W("nbI"), W("nbT"), 255, A.bitwise_and)
+    ts(("TS", 0, 64, 32), W("sg"), -0.5, A.mult, 127.5, A.add)
+    tp(W("TT"), W("TS"))
+    spread("Rp", "TT")
+    for b in range(2, 4): etile(b)
+
+    def kappa(v, vi, ai, h, s, out):
+        cp(vi, v)
+        ts(ai, vi, 96, A.bitwise_and)
+        ts(h, v, 128.0, A.is_ge, 96.0, A.mult)
+        tt(s, v, ai, A.add)
+        tt(out, s, h, A.subtract)
+    cp(W("rho"), W("rhoI"))
+    ts(W("nd0"), W("cd"), W("gF"), A.add, 16.0, A.mult)
+    ts(W("md"), W("nd0"), W("rho"), A.add)
+    kappa(W("md"), W("kI"), W("kA"), W("kh"), W("k1"), W("kap"))
+    cp(W("lA"), W("kap"))
+    ts(W("mn"), W("c16"), W("rho"), A.add)
+    kappa(W("mn"), W("kL"), W("kB"), W("kh2"), W("k12"), W("kap2"))
+    cp(W("lM"), W("kap2"))
+    cp(W("nbL"), W("nbI"))
+    ts(W("nd"), W("nd0"), W("rF"), A.add)
+    cp(W("lB"), W("nd"))
+    quant(("X", 0, 256), W("xb"))
+
+    gather(W("dA"), W("Rp"), W("lA"))
+    tp(W("tA"), W("dA"))
+    cp(W("posU"), ("tA", 0, 256, 16))
+    run("v", lambda e: e.tensor_copy(ap(W("Rpi")).indirect(ap(W("posU"))), ap(W("iJ"))), [W("posU"), W("iJ")], [W("Rpi")])
+    gather(W("Rpn"), W("Rp"), W("lM"), "s")
+    gather(W("Rq"), W("Rpn"), W("nbL"), "s")
+    gather(W("dB"), W("Rpi"), W("lB"))
+    tp(W("tB"), W("dB"))
+    cp(W("piU"), ("tB", 0, 256, 16))
+    pick(("W0", 0, 256), ("X", 0, 256), W("piU"))
+
+    def exchange(t):
+        for kind in "cs":
+            def what(d):
+                own, far = [("%s%d%s" % (n, t, kind),) + FAR[d] for n in "WM"]
+                return (octets(own), octets(far), own) if kind == "c" else (ap(own), ap(far), own)
+            send(what, "x%s%d" % (kind, t))
+            arrives("x%s%d" % (kind, t), incoming, [("M%d%s" % (t, kind), a, b) for a, b in FAR.values()])
+
+    def neighbours(t):
+        for k in range(2): pick(("N%d" % t, 256 * k, 256 * k + 256), ("W%d" % t, 0, 256), ("nU", 16 * k, 16 * k + 16))
+
+    def neighbours2(t): pick(("M%d" % t,) + LOC, ("W%d" % t, 0, 256), ("n2U", 0, 7))
+
+    def score(t, k, h, bank):
+        mov = ("N%d" % t, 256 * k + 128 * h, 256 * k + 128 * h + 128) if k < 2 else ("M%d" % t, 128 * h, 128 * h + 128)
+        mm(bank, 128, ("W%d" % t, 128 * h, 128 * h + 128), mov)
+        d = ("dg", 128 * (2 * k + h), 128 * (2 * k + h) + 128)
+        tt(d, ("ps%d" % bank, 0, 128), W("I"), A.mult)
+        return d, ("Sc", 2 * k + h, 2 * k + h + 1)
+
+    def local(t):
+        for k in range(2):
+            for h in range(2):
+                d, s = score(t, k, h, 2 * k + h)
+                j = ("dh", 128 * h, 128 * h + 128)
+                if k == 0: run("s", lambda e: e.activation(ap(j), ap(d), AF.Copy, accum_out=ap(s)), [d], [j, s])
+                else: rsum(s, d)
+        tt(W("sm"), ("Sc", 0, 4), ("CP", 0, 4), A.min)
+        m, fl = "m01_%d" % t, "fl%d" % t
+        tt(W(m), ("sm", 0, 2), ("sm", 2, 4), A.max)
+        def what(d):
+            r = (m, FAR[d][0] // 128, FAR[d][0] // 128 + 1)
+            return ap(r), ap((fl, d, d + 1)), r
+        send(what, "xm%d" % t)
+        arrives("xm%d" % t, incoming, [W(fl)])
+        tt(W("ge"), ("sm", 0, 2), ("sm", 2, 4), A.is_ge)
+        ts(W("c01"), W("ge"), CODE[0] - CODE[1], A.mult, CODE[1], A.add)
+        ts(W("ncp"), ("CP", 4, 6), -1.0, A.mult)
+        tt(W("m01c"), W(m), W("ncp"), A.max)
+
+    def unpack(t, k):
+        mov = ("N%d" % t, 256 * k, 256 * k + 256) if k < 2 else ("M%d" % t, 0, 256)
+        for b in range(4):
+            e = ("E", 128 * b, 128 * b + 128)
+            mm(BANKS[k][b], 256, e, ("W%d" % t, 0, 256), True, False)
+            mm(BANKS[k][b], 256, e, mov, False, True)
+        for b in range(4): cp(("h%d" % k, b, 1024, 4), ("ps%d" % BANKS[k][b], 0, 256), "s")
+
+    def candidate(t, k): quant(("W%d" % t, 256 * (k + 1), 256 * (k + 2)), W("h%d" % k))
+
+    def choose(t):
+        fl = "fl%d" % t
+        for d, s in [score(t, 2, h, h) for h in range(2)]: rsum(s, d)
+        for h in range(2): ts(("Af", h, h + 1), ("Sc", 4 + h, 5 + h), ("m01c", h, h + 1), A.is_gt, ("c01", h, h + 1), A.max)
+        ts(("mxc", 0, 1), (fl, 1, 2), ("MK", 0, 1), A.min, ("m01c", 0, 1), A.max)
+        ts(W("mxa"), (fl, 3, 4), ("MK", 1, 2), A.min, ("m01c", 1, 2), A.max)
+        ts(("mxc", 1, 2), (fl, 2, 3), ("MK", 2, 3), A.min, W("mxa"), A.max)
+        for h in range(2): ts(("Bf", h, h + 1), ("Sc", 4 + h, 5 + h), ("mxc", h, h + 1), A.is_gt, CODE[2] - 1.0, A.mult)
+        tt(("TC", 0, 64, 32), W("Af"), W("Bf"), A.add)
+        tp(W("TD"), W("TC"))
+        spread("RC%d" % t, "TD")
+        candidate(t, 0)
+
+    def decide(t, cl):
+        cd, ct, s = "CD%d" % t, "CT%d" % t, "S%d" % t
+        for i in range(4): gather((cd, 256 * i, 256 * i + 256), W("RC%d" % t), (cl, 16 * i, 16 * i + 16), "vvss"[i])
+        for i in range(4): tp((ct, 256 * i, 256 * i + 256), (cd, 256 * i, 256 * i + 256))
+        for k in range(3): tt((s, 16 * k, 16 * k + 16), (ct, 0, 256, 16), (ct, 256 * (k + 1), 256 * (k + 2), 16), A.add)
+        tt(W("Eq%d" % t), W(s), W("K2"), A.is_equal)
+
+    def newlist(t, d):
+        f, f2, l = "Fd%d" % t, "F2%d" % t, "L%d" % t
+        tt((f, 0, 48), W("Eq%d" % t), (d, 0, 48), A.mult)
+        tt(W(f2), (f, 0, 32), (f, 32, 64), A.max)
+        tt(W(l), (f2, 0, 16), (f2, 16, 32), A.max)
+        cp(W("U%d" % t), W(l))
+
+    def caps(t):
+        tt(W("EB"), W("Eq%d" % t), W("Bm"), A.mult)
+        tt(W("e24"), ("EB", 0, 48, 2), ("EB", 1, 48, 2), A.add)
+        tt(W("e12"), ("e24", 0, 24, 2), ("e24", 1, 24, 2), A.add)
+        tt(W("e6_%d" % t), ("e12", 0, 12, 2), ("e12", 1, 12, 2), A.add)
+        ts(W("cpn"), W("e6_%d" % t), -2 * BIG, A.mult, BIG, A.add)
+        tt(W("CP"), W("CP"), W("cpn"), A.min)
+
+    def pairs(t, e):
+        tt(W("fp"), W(e), W("NB1"), A.mult)
+        tt(W("f1"), ("fp", 0, 16), ("fp", 16, 32), A.add)
+        tt(W("f2"), W("f1"), ("fp", 32, 48), A.add)
+        ts(("pt%d" % t, 0, 16), W("f2"), -1.0, A.add)
+        tp(W("pu%d" % t), W("pt%d" % t), (0, 32))
+        need("y", [W("pu%d" % t)], [])
+        g.sync.dma_start(T.pr[t:t + 1, :], ap(("pu%d" % t, 0, 16), (0, 16))).then_inc(T.sem.pst, 16)
+
+    def dup(v, x, y, out, n):
+        ts(x, (v, 0, n, 2), W("me"), A.mult)
+        ts(y, (v, 1, n, 2), W("mo"), A.mult)
+        for i in range(2): tt((out, i, n, 2), x, y, A.add)
+
+    exchange(0)
+    cp(W("mo"), W("gF"))
+    ts(W("me"), W("gF"), -1.0, A.mult, 1.0, A.add)
+    ts(W("u0"), ("tB", 0, 256, 32), 3.0, A.mult, W("me"), A.mult)
+    ts(W("u1"), ("tB", 16, 256, 32), 3.0, A.mult, W("mo"), A.mult)
+    for i in range(2): tt(("p3", i, 16, 2), W("u0"), W("u1"), A.add)
+    for k in range(3): ts(("lG", 16 * k, 16 * k + 16), W("p3"), float(k), A.add)
+    for k in (0, 1, 2): gather(("d2", 256 * k, 256 * k + 256), W("Rq"), ("lG", 16 * k, 16 * k + 16), "vsv"[k])
+    for k in (0, 1):
+        tp(("t2", 256 * k, 256 * k + 256), ("d2", 256 * k, 256 * k + 256))
+        cp(("nU", 16 * k, 16 * k + 16), ("t2", 256 * k, 256 * k + 256, 16))
+    neighbours(0)
+    ms(W("CP"), BIG)
+    ms(W("TC"), 0.0)
+    for k in range(3): ts(("lH", 16 * k, 16 * k + 16), W("nd"), 3.0, A.mult, float(k), A.add)
+    local(0)
+    quant(("E", 0, 512), W("hE"))
+    tp(("t2", 512, 768), ("d2", 512, 768))
+    cp(("n2U", 0, 7), ("t2", 512 + LOC[0], 512 + LOC[1], 16))
+    neighbours2(0)
+    iota(W("io"), [[1, 1024]], 0, 0)
+    iota(W("c8"), [[0, 6], [1, 8]], 0, 0)
+    cp(W("pF"), W("pI"))
+    for i, (lo, hi) in enumerate(((0, 48), (32, 80), (80, 128))):
+        ts(("mk0", i, i + 1), W("pF"), float(lo), A.is_ge)
+        ts(("mk1", i, i + 1), W("pF"), float(hi), A.is_lt)
+    tt(("mk2", 0, 3), ("mk0", 0, 3), ("mk1", 0, 3), A.mult)
+    ts(("MK", 0, 3), ("mk2", 0, 3), 8e29, A.mult, -4e29, A.add)
+    for k in range(3): ms(("K2", 16 * k, 16 * k + 16), 2 * CODE[k])
+    for k in range(3): gather(("dn", 256 * k, 256 * k + 256), W("Rq"), ("lH", 16 * k, 16 * k + 16), "s")
+    unpack(0, 0)
+    choose(0)
+    kappa(W("nd"), W("kI"), W("kA"), W("kh"), W("k1"), W("kapn"))
+    cp(("CLp", 0, 16), W("kapn"))
+    ts(W("Tn"), W("c16"), W("rF"), A.add)
+    cp(W("lP"), ("t2", 0, 768, 16))
+    for a, b in ((0, LOC[0] // 16), (LOC[1] // 16, 16)): cp(("lP", 32 + a, 32 + b), ("Tn", a, b))
+    kappa(W("lP"), ("vI", 0, 48), ("aI", 0, 48), W("hP"), W("kP"), W("lQ"))
+    dup("lQ", W("xP"), W("yP"), "dP", 48)
+    cp(("CLp", 16, 64), W("dP"))
+    for k in range(3): ts(("Dp", 16 * k, 16 * k + 16), W("Tn"), 256.0 * (k + 1), A.add)
+    for t in range(2): cp(("Fd%d" % t, 48, 64), W("Tn"))
+
+    for t in range(R):
+        last = t == R - 1
+        unpack(t, 1)
+        decide(t, "CLn" if last else "CLp")
+        unpack(t, 2)
+        candidate(t, 1)
+        newlist(t, "Dn" if last else "Dp")
+        candidate(t, 2)
+        if last: break
+        u = t + 1
+        pick(("W%d" % u, 0, 256), ("W%d" % t, 0, 1024), W("U%d" % t))
+        exchange(u)
+        if t == 0:
+            cp(W("gG"), W("gI"))
+            ts(W("Bm"), W("c8"), W("gG"), A.is_equal)
+        neighbours(u)
+        caps(t)
+        local(u)
+        neighbours2(u)
+        unpack(u, 0)
+        if u == 1:
+            for i in range(R): ms(("pt%d" % i, 16, 32), 0.0)
+            cp(W("nbU"), W("nbT"))
+            gather(W("Rn"), W("io"), W("nbU"), "s")
+            for k in range(3): gather(("dR", 256 * k, 256 * k + 256), W("Rn"), ("lH", 16 * k, 16 * k + 16), "s")
+            for k in range(3): tp(("tn", 256 * k, 256 * k + 256), ("dn", 256 * k, 256 * k + 256))
+            cp(W("posF"), ("tA", 0, 256, 16))
+            cp(("lN", 0, 16), W("posF"))
+            cp(("lN", 16, 48), ("tn", 0, 512, 16))
+            ts(W("lo1"), W("posF"), float(LOC[0]), A.is_ge)
+            ts(W("lo2"), W("posF"), float(LOC[1]), A.is_lt)
+            tt(W("df"), ("tn", 512, 768, 16), W("posF"), A.subtract)
+            tt(W("lo"), W("lo1"), W("lo2"), A.mult)
+            tt(W("df2"), W("df"), W("lo"), A.mult)
+            tt(("lN", 48, 64), W("df2"), W("posF"), A.add)
+            kappa(W("lN"), W("vN"), W("aN"), W("hN"), W("kN"), W("lO"))
+            dup("lO", W("xN"), W("yN"), "dN2", 64)
+            cp(W("CLn"), W("dN2"))
+            choose(u)
+            for k in range(3): ts(("Dn", 16 * k, 16 * k + 16), W("posF"), 256.0 * (k + 1), A.add)
+            cp(("Fd2", 48, 64), W("posF"))
+            ms(W("TP"), 0.0)
+            quant(("wq", 0, 128), W("wb"))
+            for k in range(3): tp(("tR", 256 * k, 256 * k + 256), ("dR", 256 * k, 256 * k + 256))
+            ts(W("NB1"), ("tR", 0, 768, 16), 1.0, A.add)
+        else:
+            ts(W("q4"), W("e6_1"), 4.0, A.mult)
+            tt(W("q6"), W("q4"), W("e6_0"), A.add)
+            ts(W("qa"), ("q6", 2, 4), 2.0, A.mult)
+            ts(W("qc"), ("q6", 4, 6), 3.0, A.mult)
+            tt(W("qb"), ("q6", 0, 2), W("qa"), A.add)
+            tt(("TP", 0, 64, 32), W("qb"), W("qc"), A.add)
+            tp(W("TQ"), W("TP"))
+            spread("RP", "TQ")
+            choose(u)
+            gather(W("dPr"), W("RP"), ("CLn", 0, 16))
+            tp(W("tPr"), W("dPr"))
+            cp(W("pv"), ("tPr", 0, 256, 16))
+            ts(W("pv0"), W("pv"), 3, A.bitwise_and)
+            ts(W("pv1"), W("pv"), 2, A.logical_shift_right)
+            for i in range(2):
+                for k in range(3): ts(("En%d" % i, 16 * k, 16 * k + 16), W("pv%d" % i), float(k + 1), A.is_equal)
+                pairs(i, "En%d" % i)
+
+    t = R - 1
+    pick(("Z", 0, 256), ("W%d" % t, 0, 1024), W("U%d" % t))
+    need("y", [("Zc", 0, 256)], [])
+    g.sync.dma_start(T.oc[:, :], octets(("Zc", 0, 256))).then_inc(T.sem.st, 16)
+    pairs(t, "Eq%d" % t)
+    mm(0, 256, ("wq", 0, 128), ("Z", 0, 256))
+    need("s", [("Zs", 0, 256)], [])
+    for k in range(4): g.scalar.dma_start(T.osc[4 * k:4 * k + 4, :], T.Zs[32 * k:32 * k + 4, 0:256]).then_inc(T.sem.st, 16)
+    cp(W("yo"), ("ps0", 0, 256))
+    need("y", [W("yo")], [])
+    g.sync.dma_start(T.y[:, :], ap(W("yo"))).then_inc(T.sem.st, 16)
+    g.sync.wait_ge(T.sem.st, 16 * 6)
+    g.sync.wait_ge(T.sem.pst, 16 * R)
+    g.wait_ge(T.sem.ls, sent[0])
+    for q, sem in qsem.items():
+        if known["g"].get(sem, 0) < count[sem]: g.wait_ge(T.sem[sem], count[sem])

@@ -6,6 +6,8 @@ FAR = {1: (0, 48), 3: (160, 208), 2: (208, 256)}
 LOC = (48, 160)
 BIG = 1e29
 BANKS = ((4, 5, 6, 7), (4, 5, 6, 7), (2, 3, 0, 1))
+AHEAD = ((0, 0), (0, 1))
+NB = 2
 CODE = (0.25, 0.5, 5.0)
 
 
@@ -20,19 +22,19 @@ def _bufs():
     for t in range(R):
         mx("W%d" % t, 1024); mx("N%d" % t, 512); mx("M%d" % t, 256)
         sb("fl%d" % t, 4); sb("m01_%d" % t, 2); sb("RC%d" % t, 256, "bfloat16"); sb("CD%d" % t, 1024, "bfloat16"); sb("CT%d" % t, 1024, "bfloat16")
-        sb("S%d" % t, 48); sb("Eq%d" % t, 48); sb("Fd%d" % t, 64); sb("F2%d" % t, 32); sb("L%d" % t, 16); sb("U%d" % t, 16, "uint16")
+        sb("S%d" % t, 48); sb("Eq%d" % t, 48); sb("Fd%d" % t, 48); sb("F2%d" % t, 32); sb("L%d" % t, 16); sb("U%d" % t, 16, "uint16")
         sb("pt%d" % t, 32); sb("pu%d" % t, 32); sb("e6_%d" % t, 6)
     for k in range(3): sb("h%d" % k, 1024, "bfloat16")
     sb("half", 512, "bfloat16"); sb("hE", 2048, "bfloat16")
-    for name, n in (("pI", 1), ("rI", 1), ("gI", 1), ("uI", 1), ("yI", 256), ("wI", 256), ("rhoI", 1), ("zI", 48),
+    for name, n in (("pI", 1), ("rI", 1), ("gI", 1), ("uI", 1), ("yI", 256), ("wI", 256), ("rhoI", 1), ("zI", 48), ("vI0", 16), ("aI0", 16),
                     ("vI", 64), ("aI", 64), ("nbI", 48), ("vN", 64), ("aN", 64), ("kI", 16), ("kA", 16), ("kL", 16), ("kB", 16), ("pv", 16), ("pv0", 16), ("pv1", 16)): sb(name, n, "int32")
-    for name, n in (("one", 128), ("I", 128), ("mF", 256), ("ju", 256), ("rF", 1), ("gF", 1), ("gG", 1), ("me", 1), ("mo", 1), ("pF", 1), ("rho", 1), ("c16", 16), ("cd", 16), ("o48", 48), ("z48", 48), ("z3", 48), ("M48", 48), ("jR", 256),
+    for name, n in (("one", 128), ("I", 128), ("mF", 256), ("ju", 256), ("rF", 1), ("g16", 1), ("gG", 1), ("me", 1), ("mo", 1), ("rho", 1), ("o48", 48), ("z48", 48), ("z3", 48), ("M48", 48), ("jR", 256),
                     ("Fw", 1024), ("mk", 48), ("t2a", 16), ("T2", 16), ("RK", 256), ("dk", 256), ("nK", 2), ("sg", 2), ("jk", 512), ("Tn", 16), ("nd0", 16), ("nd", 16), ("md", 16), ("mn", 16),
-                    ("kh", 16), ("k1", 16), ("kap", 16), ("kapn", 16), ("kh2", 16), ("k12", 16), ("kap2", 16), ("u0", 8), ("u1", 8), ("p3", 16), ("hP", 48), ("kP", 48), ("lP", 48), ("lQ", 48), ("xP", 24), ("yP", 24), ("dP", 48),
-                    ("hN", 64), ("kN", 64), ("lN", 64), ("lO", 64), ("xN", 32), ("yN", 32), ("dN2", 64), ("posF", 16), ("lo", 16), ("lo1", 16), ("lo2", 16), ("df", 16), ("df2", 16), ("Dp", 64), ("Dn", 64), ("K2", 48), ("Bm", 48), ("c8", 48),
-                    ("MK", 4), ("mk0", 4), ("mk1", 4), ("mk2", 4), ("CP", 6), ("dg", 768), ("dh", 512), ("Sc", 6), ("sm", 4), ("ge", 2), ("c01", 2), ("m01c", 2), ("ncp", 2), ("mxa", 1), ("mxc", 2), ("Af", 2), ("Bf", 2),
-                    ("EB", 48), ("e24", 24), ("e12", 12), ("cpn", 6), ("io", 1024), ("Rn", 768), ("dR", 768), ("tR", 768), ("NB1", 48),
-                    ("fp", 48), ("f1", 16), ("f2", 16), ("yo", 256), ("En0", 48), ("En1", 48), ("q4", 6), ("q6", 6), ("qa", 2), ("qb", 2), ("qc", 2)): sb(name, n)
+                    ("kh", 16), ("k1", 16), ("kap", 16), ("kapn", 16), ("kh2", 16), ("k12", 16), ("kap2", 16), ("hh", 16), ("hk", 16), ("u0", 8), ("u1", 8), ("p3", 16), ("hP", 48), ("kP", 48), ("lP", 48), ("lQ", 48), ("xP", 24), ("yP", 24), ("dP", 48),
+                    ("hN", 64), ("kN", 64), ("lN", 64), ("lO", 64), ("xN", 32), ("yN", 32), ("dN2", 64), ("posF", 16), ("lo", 16), ("lo1", 16), ("lo2", 16), ("df", 16), ("df2", 16), ("K2", 48), ("Bm", 48), ("c8", 48),
+                    ("MK", 4), ("mk0", 4), ("CP", 6), ("dg", 768), ("dh", 512), ("Sc", 6), ("sm", 4), ("ge", 2), ("c01", 2), ("m01c", 2), ("ncp", 2), ("mxa", 1), ("mxc", 2), ("Af", 2), ("Bf", 2),
+                    ("EB", 48), ("e24", 24), ("e12", 12), ("cpn", 6), ("io", 1024), ("Rn", 768), ("dR", 768), ("tR", 768), ("NB1", 48), ("NB2", 96), ("En", 96), ("fq", 96), ("g1", 32), ("g2", 32),
+                    ("fp", 48), ("f1", 16), ("f2", 16), ("yo", 256), ("q4", 6), ("q6", 6), ("qa", 2), ("qb", 2), ("qc", 2)): sb(name, n)
     for name, n in (("TS", 64), ("TT", 64), ("Rp", 256), ("dA", 256), ("tA", 256), ("iJ", 256), ("Rpi", 256), ("dB", 256), ("tB", 256), ("Rpn", 256), ("Rq", 768), ("d2", 768), ("t2", 768),
                     ("dn", 768), ("tn", 768), ("TC", 64), ("TD", 64), ("TP", 64), ("TQ", 64), ("RP", 256), ("dPr", 256), ("tPr", 256)): sb(name, n, "bfloat16")
     for name, n in (("T2u", 16), ("lA", 16), ("lB", 16), ("lM", 16), ("posU", 16), ("piU", 16), ("nbL", 48), ("nbU", 48), ("lG", 48), ("lH", 48), ("nU", 32), ("n2U", 8), ("CLp", 64), ("CLn", 64)): sb(name, n, "uint16")
@@ -158,6 +160,11 @@ def rank_program(g, core, T, topo):
     def spread(row, col):
         settle()
         for a in range(4): pb((row, 64 * a, 64 * a + 64), (col, 0, 64), 32 * a)
+    def D(f, *a): return lambda: f(*a)
+    def weave(*chains):
+        for i in range(max(map(len, chains))):
+            for c in chains:
+                if i < len(c): c[i]()
 
     peer, eng = shares(T, topo, core)
     incoming = sum(len(shares(T, topo, c)[1][d]) for d, c in peer.items())
@@ -184,9 +191,9 @@ def rank_program(g, core, T, topo):
 
     iota(W("pI"), [[0, 1]], 0, 1)
     iota(W("o48"), [[0, 16], [1, 3]], 0, 0)
+    iota(W("mF"), [[1, 256]], 0, 0)
     iota(W("yI"), [[0, 16], [11, 16]], 10, 0)
     iota(W("ju"), [[16, 16], [0, 16]], 0, 0)
-    iota(W("mF"), [[1, 256]], 0, 0)
     ms(W("one"), 1.0)
     for q in range(4):
         c, r = q ^ rank ^ 1, ("Fw", 256 * q, 256 * q + 256)
@@ -196,28 +203,35 @@ def rank_program(g, core, T, topo):
     ms(W("TS"), 0.0)
     ms(W("half"), 0.5)
     run("g", lambda e: e.affine_select(ap(W("I")), ap(W("one")), [[-1, 128]], A.is_equal, 0.0, 0, 1), [W("one")], [W("I")])
-    iota(W("cd"), [[2, 8], [0, 2]], 0, 0)
-    iota(W("c16"), [[16, 16]], 0, 0)
     def etile(b):
         out = ("hE", 512 * b, 512 * b + 512)
         settle()
         run("g", lambda e: e.affine_select(ap(out), ap(W("half")), [[1, 512]], A.is_equal, 0.0, -b, -4), [W("half")], [out])
     for b in range(2): etile(b)
+    ms(W("mk0"), 4e29)
+    def within(i, src, cm, base):
+        a, b = (src, i, i + 1), ("MK", i, i + 1)
+        run("g", lambda e: e.affine_select(ap(b), ap(a), [[0, 1]], A.is_ge, -4e29, base, cm), [a], [b])
+    within(0, "mk0", -1, 47)
+    within(2, "mk0", 1, -80)
+    within(1, "mk0", 1, -32)
+    settle()
+    within(1, "MK", -1, 79)
+
+    def kappa(v, vi, ai, h, s, out):
+        return [D(cp, vi, v), D(ts, h, v, 128.0, A.is_ge, 96.0, A.mult), D(ts, ai, vi, 96, A.bitwise_and), D(tt, s, v, ai, A.add), D(tt, out, s, h, A.subtract)]
+
     ts(W("rI"), W("pI"), 15, A.bitwise_and)
     ts(W("gI"), W("pI"), 4, A.logical_shift_right)
     cp(W("rF"), W("rI"))
     ts(W("uI"), W("gI"), 1, A.bitwise_and)
-    ts(W("z48"), W("o48"), W("rF"), A.add, 1.0, A.add)
-    ts(W("zI"), W("z48"), 1.0 / 3.0, A.mult)
-    ts(W("z3"), W("zI"), 3.0, A.mult)
-    tt(W("M48"), W("z3"), W("z48"), A.is_equal)
-    ts(W("wI"), W("yI"), 15, A.bitwise_and)
-    tt(W("jR"), W("wI"), W("ju"), A.add)
+    weave([D(ts, W("z48"), W("o48"), W("rF"), A.add, 1.0, A.add), D(ts, W("zI"), W("z48"), 1.0 / 3.0, A.mult), D(ts, W("z3"), W("zI"), 3.0, A.mult), D(tt, W("M48"), W("z3"), W("z48"), A.is_equal)],
+          [D(ts, W("rhoI"), W("rF"), 3.0, A.mult, 2.0, A.add), D(ts, W("rhoI"), W("rhoI"), 15, A.bitwise_and), D(cp, W("rho"), W("rhoI"))],
+          [D(ts, W("g16"), W("uI"), 16.0, A.mult)] + [D(ts, ("nd0", i, 16, 2), ("mF", 0, 256, 32), W("g16"), A.add) for i in range(2)] + [D(ts, W("md"), W("nd0"), W("rho"), A.add)]
+          + kappa(W("md"), W("kI"), W("kA"), W("kh"), W("k1"), W("kap")))
 
-    tt(W("mk"), W("nbT"), W("M48"), A.mult)
-    tt(W("t2a"), ("mk", 0, 48, 3), ("mk", 1, 48, 3), A.add)
-    tt(W("T2"), W("t2a"), ("mk", 2, 48, 3), A.add)
-    cp(W("T2u"), W("T2"))
+    weave([D(tt, W("mk"), W("nbT"), W("M48"), A.mult), D(tt, W("t2a"), ("mk", 0, 48, 3), ("mk", 1, 48, 3), A.add), D(tt, W("T2"), W("t2a"), ("mk", 2, 48, 3), A.add), D(cp, W("T2u"), W("T2"))],
+          [D(ts, W("wI"), W("yI"), 15, A.bitwise_and), D(tt, W("jR"), W("wI"), W("ju"), A.add)])
     run("v", lambda e: e.tensor_tensor(ap(W("RK")), ap(W("Fw")).indirect(ap(W("T2u"))), ap(W("jR")), A.add), [W("Fw"), W("T2u"), W("jR")], [W("RK")])
     for h in range(2):
         d = ("dk", 128 * h, 128 * h + 128)
@@ -225,33 +239,15 @@ def rank_program(g, core, T, topo):
         rsum(("nK", h, h + 1), d, negate=True)
         jk, b, o = ("jk", 256 * h, 256 * h + 256), ("nK", h, h + 1), ("sg", h, h + 1)
         run("s", lambda e: e.activation(ap(jk), ap(W("RK")), AF.Sign, bias=ap(b), accum_out=ap(o)), [W("RK"), b], [jk, o])
-    ts(W("rhoI"), W("rF"), 3.0, A.mult, 2.0, A.add)
-    ts(W("rhoI"), W("rhoI"), 15, A.bitwise_and)
-    cp(W("gF"), W("uI"))
     ts(W("nbI"), W("nbT"), 255, A.bitwise_and)
     ts(("TS", 0, 64, 32), W("sg"), -0.5, A.mult, 127.5, A.add)
     tp(W("TT"), W("TS"))
     spread("Rp", "TT")
     for b in range(2, 4): etile(b)
-
-    def kappa(v, vi, ai, h, s, out):
-        cp(vi, v)
-        ts(ai, vi, 96, A.bitwise_and)
-        ts(h, v, 128.0, A.is_ge, 96.0, A.mult)
-        tt(s, v, ai, A.add)
-        tt(out, s, h, A.subtract)
-    cp(W("rho"), W("rhoI"))
-    ts(W("nd0"), W("cd"), W("gF"), A.add, 16.0, A.mult)
-    ts(W("md"), W("nd0"), W("rho"), A.add)
-    kappa(W("md"), W("kI"), W("kA"), W("kh"), W("k1"), W("kap"))
-    cp(W("lA"), W("kap"))
-    ts(W("mn"), W("c16"), W("rho"), A.add)
-    kappa(W("mn"), W("kL"), W("kB"), W("kh2"), W("k12"), W("kap2"))
-    cp(W("lM"), W("kap2"))
-    cp(W("nbL"), W("nbI"))
-    ts(W("nd"), W("nd0"), W("rF"), A.add)
-    cp(W("lB"), W("nd"))
-    quant(("X", 0, 256), W("xb"))
+    weave([D(ts, W("mn"), ("mF", 0, 256, 16), W("rho"), A.add)] + kappa(W("mn"), W("kL"), W("kB"), W("kh2"), W("k12"), W("kap2")) + [D(cp, W("lM"), W("kap2"))],
+          [D(cp, W("lA"), W("kap")), D(ts, W("nd"), W("nd0"), W("rF"), A.add), D(cp, W("nbL"), W("nbI")), D(cp, W("lB"), W("nd")), D(quant, ("X", 0, 256), W("xb")), D(cp, W("mo"), W("uI")), D(ts, W("me"), W("mo"), -1.0, A.mult, 1.0, A.add)])
+    weave(kappa(W("nd"), W("vI0"), W("aI0"), W("hh"), W("hk"), W("kapn")) + [D(cp, ("CLp", 0, 16), W("kapn"))],
+          [D(ms, ("K2", 16 * k, 16 * k + 16), 2 * CODE[k]) for k in range(3)] + [D(ms, W("CP"), BIG), D(ms, W("TC"), 0.0), D(ts, W("Tn"), ("mF", 0, 256, 16), W("rF"), A.add)])
 
     gather(W("dA"), W("Rp"), W("lA"))
     tp(W("tA"), W("dA"))
@@ -272,8 +268,7 @@ def rank_program(g, core, T, topo):
             send(what, "x%s%d" % (kind, t))
             arrives("x%s%d" % (kind, t), incoming, [("M%d%s" % (t, kind), a, b) for a, b in FAR.values()])
 
-    def neighbours(t):
-        for k in range(2): pick(("N%d" % t, 256 * k, 256 * k + 256), ("W%d" % t, 0, 256), ("nU", 16 * k, 16 * k + 16))
+    def neighbours(t, k): pick(("N%d" % t, 256 * k, 256 * k + 256), ("W%d" % t, 0, 256), ("nU", 16 * k, 16 * k + 16))
 
     def neighbours2(t): pick(("M%d" % t,) + LOC, ("W%d" % t, 0, 256), ("n2U", 0, 7))
 
@@ -300,26 +295,26 @@ def rank_program(g, core, T, topo):
         send(what, "xm%d" % t)
         arrives("xm%d" % t, incoming, [W(fl)])
         tt(W("ge"), ("sm", 0, 2), ("sm", 2, 4), A.is_ge)
-        ts(W("c01"), W("ge"), CODE[0] - CODE[1], A.mult, CODE[1], A.add)
         ts(W("ncp"), ("CP", 4, 6), -1.0, A.mult)
+        ts(W("c01"), W("ge"), CODE[0] - CODE[1], A.mult, CODE[1], A.add)
         tt(W("m01c"), W(m), W("ncp"), A.max)
 
-    def unpack(t, k):
+    def unpack(t, k, parts=(0, 1, 2, 3)):
         mov = ("N%d" % t, 256 * k, 256 * k + 256) if k < 2 else ("M%d" % t, 0, 256)
-        for b in range(4):
+        for b in parts:
             e = ("E", 128 * b, 128 * b + 128)
-            mm(BANKS[k][b], 256, e, ("W%d" % t, 0, 256), True, False)
+            if (k, b) not in AHEAD or t == 0: mm(BANKS[k][b], 256, e, ("W%d" % t, 0, 256), True, False)
             mm(BANKS[k][b], 256, e, mov, False, True)
-        for b in range(4): cp(("h%d" % k, b, 1024, 4), ("ps%d" % BANKS[k][b], 0, 256), "s")
+        for b in parts: cp(("h%d" % k, b, 1024, 4), ("ps%d" % BANKS[k][b], 0, 256), "s")
 
     def candidate(t, k): quant(("W%d" % t, 256 * (k + 1), 256 * (k + 2)), W("h%d" % k))
 
     def choose(t):
         fl = "fl%d" % t
         for d, s in [score(t, 2, h, h) for h in range(2)]: rsum(s, d)
-        for h in range(2): ts(("Af", h, h + 1), ("Sc", 4 + h, 5 + h), ("m01c", h, h + 1), A.is_gt, ("c01", h, h + 1), A.max)
         ts(("mxc", 0, 1), (fl, 1, 2), ("MK", 0, 1), A.min, ("m01c", 0, 1), A.max)
         ts(W("mxa"), (fl, 3, 4), ("MK", 1, 2), A.min, ("m01c", 1, 2), A.max)
+        for h in range(2): ts(("Af", h, h + 1), ("Sc", 4 + h, 5 + h), ("m01c", h, h + 1), A.is_gt, ("c01", h, h + 1), A.max)
         ts(("mxc", 1, 2), (fl, 2, 3), ("MK", 2, 3), A.min, W("mxa"), A.max)
         for h in range(2): ts(("Bf", h, h + 1), ("Sc", 4 + h, 5 + h), ("mxc", h, h + 1), A.is_gt, CODE[2] - 1.0, A.mult)
         tt(("TC", 0, 64, 32), W("Af"), W("Bf"), A.add)
@@ -327,27 +322,23 @@ def rank_program(g, core, T, topo):
         spread("RC%d" % t, "TD")
         candidate(t, 0)
 
-    def decide(t, cl):
-        cd, ct, s = "CD%d" % t, "CT%d" % t, "S%d" % t
+    def decide(t, cl, base):
+        cd, ct, s, f, f2, l = ["%s%d" % (n, t) for n in ("CD", "CT", "S", "Fd", "F2", "L")]
         for i in range(4): gather((cd, 256 * i, 256 * i + 256), W("RC%d" % t), (cl, 16 * i, 16 * i + 16), "vvss"[i])
         for i in range(4): tp((ct, 256 * i, 256 * i + 256), (cd, 256 * i, 256 * i + 256))
         for k in range(3): tt((s, 16 * k, 16 * k + 16), (ct, 0, 256, 16), (ct, 256 * (k + 1), 256 * (k + 2), 16), A.add)
-        tt(W("Eq%d" % t), W(s), W("K2"), A.is_equal)
-
-    def newlist(t, d):
-        f, f2, l = "Fd%d" % t, "F2%d" % t, "L%d" % t
-        tt((f, 0, 48), W("Eq%d" % t), (d, 0, 48), A.mult)
-        tt(W(f2), (f, 0, 32), (f, 32, 64), A.max)
-        tt(W(l), (f2, 0, 16), (f2, 16, 32), A.max)
+        for k in range(3): ts((f, 16 * k, 16 * k + 16), (s, 16 * k, 16 * k + 16), 2 * CODE[k], A.is_equal, 256.0 * (k + 1), A.mult)
+        candidate(t, 1)
+        tt((f2, 0, 16), (f, 0, 16), (f, 16, 32), A.add)
+        tt((f2, 16, 32), (f, 32, 48), W(base), A.add)
+        tt(W(l), (f2, 0, 16), (f2, 16, 32), A.add)
         cp(W("U%d" % t), W(l))
 
     def caps(t):
-        tt(W("EB"), W("Eq%d" % t), W("Bm"), A.mult)
-        tt(W("e24"), ("EB", 0, 48, 2), ("EB", 1, 48, 2), A.add)
-        tt(W("e12"), ("e24", 0, 24, 2), ("e24", 1, 24, 2), A.add)
-        tt(W("e6_%d" % t), ("e12", 0, 12, 2), ("e12", 1, 12, 2), A.add)
-        ts(W("cpn"), W("e6_%d" % t), -2 * BIG, A.mult, BIG, A.add)
-        tt(W("CP"), W("CP"), W("cpn"), A.min)
+        e6 = W("e6_%d" % t)
+        return [D(tt, W("Eq%d" % t), W("S%d" % t), W("K2"), A.is_equal), D(tt, W("EB"), W("Eq%d" % t), W("Bm"), A.mult), D(tt, W("e24"), ("EB", 0, 48, 2), ("EB", 1, 48, 2), A.add),
+                D(tt, W("e12"), ("e24", 0, 24, 2), ("e24", 1, 24, 2), A.add), D(tt, e6, ("e12", 0, 12, 2), ("e12", 1, 12, 2), A.add),
+                D(ts, W("cpn"), e6, -2 * BIG, A.mult, BIG, A.add), D(tt, W("CP"), W("CP"), W("cpn"), A.min)]
 
     def pairs(t, e):
         tt(W("fp"), W(e), W("NB1"), A.mult)
@@ -359,99 +350,68 @@ def rank_program(g, core, T, topo):
         g.sync.dma_start(T.pr[t:t + 1, :], ap(("pu%d" % t, 0, 16), (0, 16))).then_inc(T.sem.pst, 16)
 
     def dup(v, x, y, out, n):
-        ts(x, (v, 0, n, 2), W("me"), A.mult)
-        ts(y, (v, 1, n, 2), W("mo"), A.mult)
-        for i in range(2): tt((out, i, n, 2), x, y, A.add)
+        return [D(ts, x, (v, 0, n, 2), W("me"), A.mult), D(ts, y, (v, 1, n, 2), W("mo"), A.mult)] + [D(tt, (out, i, n, 2), x, y, A.add) for i in range(2)]
 
     exchange(0)
-    cp(W("mo"), W("gF"))
-    ts(W("me"), W("gF"), -1.0, A.mult, 1.0, A.add)
     ts(W("u0"), ("tB", 0, 256, 32), 3.0, A.mult, W("me"), A.mult)
     ts(W("u1"), ("tB", 16, 256, 32), 3.0, A.mult, W("mo"), A.mult)
     for i in range(2): tt(("p3", i, 16, 2), W("u0"), W("u1"), A.add)
-    for k in range(3): ts(("lG", 16 * k, 16 * k + 16), W("p3"), float(k), A.add)
-    for k in (0, 1, 2): gather(("d2", 256 * k, 256 * k + 256), W("Rq"), ("lG", 16 * k, 16 * k + 16), "vsv"[k])
+    def where(k, q):
+        ts(("lG", 16 * k, 16 * k + 16), W("p3"), float(k), A.add)
+        gather(("d2", 256 * k, 256 * k + 256), W("Rq"), ("lG", 16 * k, 16 * k + 16), q)
+    where(1, "s")
+    where(0, "v")
     for k in (0, 1):
         tp(("t2", 256 * k, 256 * k + 256), ("d2", 256 * k, 256 * k + 256))
         cp(("nU", 16 * k, 16 * k + 16), ("t2", 256 * k, 256 * k + 256, 16))
-    neighbours(0)
-    ms(W("CP"), BIG)
-    ms(W("TC"), 0.0)
-    for k in range(3): ts(("lH", 16 * k, 16 * k + 16), W("nd"), 3.0, A.mult, float(k), A.add)
-    local(0)
+        neighbours(0, k)
+    where(2, "s")
     quant(("E", 0, 512), W("hE"))
+    local(0)
     tp(("t2", 512, 768), ("d2", 512, 768))
-    cp(("n2U", 0, 7), ("t2", 512 + LOC[0], 512 + LOC[1], 16))
-    neighbours2(0)
+    weave([D(cp, ("n2U", 0, 7), ("t2", 512 + LOC[0], 512 + LOC[1], 16)), D(neighbours2, 0)] + [D(ts, ("lH", 16 * k, 16 * k + 16), W("nd"), 3.0, A.mult, float(k), A.add) for k in range(3)],
+          [D(cp, W("lP"), ("t2", 0, 768, 16))] + [D(cp, ("lP", 32 + a, 32 + b), ("Tn", a, b)) for a, b in ((0, LOC[0] // 16), (LOC[1] // 16, 16))]
+          + kappa(W("lP"), ("vI", 0, 48), ("aI", 0, 48), W("hP"), W("kP"), W("lQ")) + dup("lQ", W("xP"), W("yP"), "dP", 48) + [D(cp, ("CLp", 16, 64), W("dP"))])
     iota(W("io"), [[1, 1024]], 0, 0)
     iota(W("c8"), [[0, 6], [1, 8]], 0, 0)
-    cp(W("pF"), W("pI"))
-    for i, (lo, hi) in enumerate(((0, 48), (32, 80), (80, 128))):
-        ts(("mk0", i, i + 1), W("pF"), float(lo), A.is_ge)
-        ts(("mk1", i, i + 1), W("pF"), float(hi), A.is_lt)
-    tt(("mk2", 0, 3), ("mk0", 0, 3), ("mk1", 0, 3), A.mult)
-    ts(("MK", 0, 3), ("mk2", 0, 3), 8e29, A.mult, -4e29, A.add)
-    for k in range(3): ms(("K2", 16 * k, 16 * k + 16), 2 * CODE[k])
     for k in range(3): gather(("dn", 256 * k, 256 * k + 256), W("Rq"), ("lH", 16 * k, 16 * k + 16), "s")
     unpack(0, 0)
     choose(0)
-    kappa(W("nd"), W("kI"), W("kA"), W("kh"), W("k1"), W("kapn"))
-    cp(("CLp", 0, 16), W("kapn"))
-    ts(W("Tn"), W("c16"), W("rF"), A.add)
-    cp(W("lP"), ("t2", 0, 768, 16))
-    for a, b in ((0, LOC[0] // 16), (LOC[1] // 16, 16)): cp(("lP", 32 + a, 32 + b), ("Tn", a, b))
-    kappa(W("lP"), ("vI", 0, 48), ("aI", 0, 48), W("hP"), W("kP"), W("lQ"))
-    dup("lQ", W("xP"), W("yP"), "dP", 48)
-    cp(("CLp", 16, 64), W("dP"))
-    for k in range(3): ts(("Dp", 16 * k, 16 * k + 16), W("Tn"), 256.0 * (k + 1), A.add)
-    for t in range(2): cp(("Fd%d" % t, 48, 64), W("Tn"))
+    cp(W("gG"), W("gI"))
+    ts(W("Bm"), W("c8"), W("gG"), A.is_equal)
 
     for t in range(R):
         last = t == R - 1
-        unpack(t, 1)
-        decide(t, "CLn" if last else "CLp")
+        unpack(t, 1, range(NB if t else 0, 4))
+        decide(t, "CLn" if last else "CLp", "posF" if last else "Tn")
         unpack(t, 2)
-        candidate(t, 1)
-        newlist(t, "Dn" if last else "Dp")
         candidate(t, 2)
         if last: break
         u = t + 1
         pick(("W%d" % u, 0, 256), ("W%d" % t, 0, 1024), W("U%d" % t))
         exchange(u)
-        if t == 0:
-            cp(W("gG"), W("gI"))
-            ts(W("Bm"), W("c8"), W("gG"), A.is_equal)
-        neighbours(u)
-        caps(t)
+        for k, b in AHEAD: mm(BANKS[k][b], 256, ("E", 128 * b, 128 * b + 128), ("W%d" % u, 0, 256), True, False)
+        weave([D(neighbours, u, 0), D(neighbours, u, 1)], caps(t))
         local(u)
         neighbours2(u)
         unpack(u, 0)
+        unpack(u, 1, range(NB))
         if u == 1:
             for i in range(R): ms(("pt%d" % i, 16, 32), 0.0)
             cp(W("nbU"), W("nbT"))
             gather(W("Rn"), W("io"), W("nbU"), "s")
             for k in range(3): gather(("dR", 256 * k, 256 * k + 256), W("Rn"), ("lH", 16 * k, 16 * k + 16), "s")
-            for k in range(3): tp(("tn", 256 * k, 256 * k + 256), ("dn", 256 * k, 256 * k + 256))
-            cp(W("posF"), ("tA", 0, 256, 16))
-            cp(("lN", 0, 16), W("posF"))
-            cp(("lN", 16, 48), ("tn", 0, 512, 16))
-            ts(W("lo1"), W("posF"), float(LOC[0]), A.is_ge)
-            ts(W("lo2"), W("posF"), float(LOC[1]), A.is_lt)
-            tt(W("df"), ("tn", 512, 768, 16), W("posF"), A.subtract)
-            tt(W("lo"), W("lo1"), W("lo2"), A.mult)
-            tt(W("df2"), W("df"), W("lo"), A.mult)
-            tt(("lN", 48, 64), W("df2"), W("posF"), A.add)
-            kappa(W("lN"), W("vN"), W("aN"), W("hN"), W("kN"), W("lO"))
-            dup("lO", W("xN"), W("yN"), "dN2", 64)
-            cp(W("CLn"), W("dN2"))
+            weave([D(tp, ("tn", 256 * k, 256 * k + 256), ("dn", 256 * k, 256 * k + 256)) for k in range(3)] + [D(cp, ("lN", 16, 48), ("tn", 0, 512, 16)), D(tt, W("df"), ("tn", 512, 768, 16), W("posF"), A.subtract),
+                  D(tt, W("df2"), W("df"), W("lo"), A.mult), D(tt, ("lN", 48, 64), W("df2"), W("posF"), A.add)] + kappa(W("lN"), W("vN"), W("aN"), W("hN"), W("kN"), W("lO")) + dup("lO", W("xN"), W("yN"), "dN2", 64) + [D(cp, W("CLn"), W("dN2"))],
+                  [D(cp, W("posF"), ("tA", 0, 256, 16)), D(cp, ("lN", 0, 16), W("posF")), D(ts, W("lo1"), W("posF"), float(LOC[0]), A.is_ge), D(ts, W("lo2"), W("posF"), float(LOC[1]), A.is_lt), D(tt, W("lo"), W("lo1"), W("lo2"), A.mult)])
             choose(u)
-            for k in range(3): ts(("Dn", 16 * k, 16 * k + 16), W("posF"), 256.0 * (k + 1), A.add)
-            cp(("Fd2", 48, 64), W("posF"))
             ms(W("TP"), 0.0)
             quant(("wq", 0, 128), W("wb"))
             for k in range(3): tp(("tR", 256 * k, 256 * k + 256), ("dR", 256 * k, 256 * k + 256))
             ts(W("NB1"), ("tR", 0, 768, 16), 1.0, A.add)
         else:
+            for k in range(3):
+                for i in range(2): cp(("NB2", 32 * k + 16 * i, 32 * k + 16 * i + 16), ("NB1", 16 * k, 16 * k + 16), "s")
             ts(W("q4"), W("e6_1"), 4.0, A.mult)
             tt(W("q6"), W("q4"), W("e6_0"), A.add)
             ts(W("qa"), ("q6", 2, 4), 2.0, A.mult)
@@ -467,22 +427,29 @@ def rank_program(g, core, T, topo):
             ts(W("pv0"), W("pv"), 3, A.bitwise_and)
             ts(W("pv1"), W("pv"), 2, A.logical_shift_right)
             for i in range(2):
-                for k in range(3): ts(("En%d" % i, 16 * k, 16 * k + 16), W("pv%d" % i), float(k + 1), A.is_equal)
-                pairs(i, "En%d" % i)
+                for k in range(3): ts(("En", 32 * k + 16 * i, 32 * k + 16 * i + 16), W("pv%d" % i), float(k + 1), A.is_equal)
 
     t = R - 1
     pick(("Z", 0, 256), ("W%d" % t, 0, 1024), W("U%d" % t))
     need("y", [("Zc", 0, 256)], [])
     g.sync.dma_start(T.oc[:, :], octets(("Zc", 0, 256))).then_inc(T.sem.st, 16)
+    tt(W("Eq%d" % t), W("S%d" % t), W("K2"), A.is_equal)
     pairs(t, "Eq%d" % t)
     mm(0, 256, ("wq", 0, 128), ("Z", 0, 256))
     need("s", [("Zs", 0, 256)], [])
     for k in range(4): g.scalar.dma_start(T.osc[4 * k:4 * k + 4, :], T.Zs[32 * k:32 * k + 4, 0:256]).then_inc(T.sem.st, 16)
     cp(W("yo"), ("ps0", 0, 256))
+    tt(W("fq"), W("En"), W("NB2"), A.mult)
+    tt(W("g1"), ("fq", 0, 32), ("fq", 32, 64), A.add)
+    tt(W("g2"), W("g1"), ("fq", 64, 96), A.add)
+    ts(W("pt0"), W("g2"), -1.0, A.add)
+    tp(W("pu0"), W("pt0"), (0, 32))
+    need("s", [W("pu0")], [])
+    g.scalar.dma_start(T.pr[0:2, :], ap(("pu0", 0, 16), (0, 32))).then_inc(T.sem.pst, 16)
     need("y", [W("yo")], [])
     g.sync.dma_start(T.y[:, :], ap(W("yo"))).then_inc(T.sem.st, 16)
     g.sync.wait_ge(T.sem.st, 16 * 6)
-    g.sync.wait_ge(T.sem.pst, 16 * R)
+    g.sync.wait_ge(T.sem.pst, 32)
     g.wait_ge(T.sem.ls, sent[0])
     for q, sem in qsem.items():
         if known["g"].get(sem, 0) < count[sem]: g.wait_ge(T.sem[sem], count[sem])

@@ -6,9 +6,8 @@ FAR = {1: (0, 48), 3: (160, 208), 2: (208, 256)}
 LOC = (48, 160)
 BIG = 1e29
 BANKS = ((4, 5, 6, 7), (4, 5, 6, 7), (2, 3, 0, 1))
-AHEAD = ((0, 0), (0, 1))
 NB = 2
-CODE = (0.25, 0.5, 5.0)
+VPARTS = (0, 1)
 
 
 def _bufs():
@@ -18,33 +17,32 @@ def _bufs():
         sb(name + "c", n, "float8_e4m3fn_x4")
         sb(name + "s", n, "uint8")
     sb("nbT", 48, "int32"); sb("xb", 1024, "bfloat16"); sb("wb", 512, "bfloat16")
-    mx("X", 256); mx("wq", 128); mx("E", 512); mx("Z", 256)
+    mx("X", 256); mx("wq", 128); mx("E", 512); mx("H", 256); mx("Z", 256)
     for t in range(R):
         mx("W%d" % t, 1024); mx("N%d" % t, 512); mx("M%d" % t, 256)
-        sb("fl%d" % t, 4); sb("m01_%d" % t, 2); sb("RC%d" % t, 256, "bfloat16"); sb("CD%d" % t, 1024, "bfloat16"); sb("CT%d" % t, 1024, "bfloat16")
-        sb("S%d" % t, 48); sb("Eq%d" % t, 48); sb("Fd%d" % t, 48); sb("F2%d" % t, 32); sb("L%d" % t, 16); sb("U%d" % t, 16, "uint16")
-        sb("pt%d" % t, 32); sb("pu%d" % t, 32); sb("e6_%d" % t, 6)
+        sb("fl%d" % t, 4); sb("m01_%d" % t, 2); sb("RC%d" % t, 272, "bfloat16"); sb("U%d" % t, 16, "uint16"); sb("V%d" % t, 16, "uint16")
+        for name in ("D0_", "D1_", "Ls"): sb("%s%d" % (name, t), 32)
+        for name in ("e1_", "e2_"): sb("%s%d" % (name, t), 16)
+        sb("PRp%d" % t, 256); sb("PRn%d" % t, 256)
     for k in range(3): sb("h%d" % k, 1024, "bfloat16")
-    sb("half", 512, "bfloat16"); sb("hE", 2048, "bfloat16")
-    for name, n in (("pI", 1), ("rI", 1), ("gI", 1), ("uI", 1), ("yI", 256), ("wI", 256), ("rhoI", 1), ("zI", 48), ("vI0", 16), ("aI0", 16),
-                    ("vI", 64), ("aI", 64), ("nbI", 48), ("vN", 64), ("aN", 64), ("kI", 16), ("kA", 16), ("kL", 16), ("kB", 16), ("pv", 16), ("pv0", 16), ("pv1", 16)): sb(name, n, "int32")
-    for name, n in (("one", 128), ("I", 128), ("mF", 256), ("ju", 256), ("rF", 1), ("g16", 1), ("gG", 1), ("me", 1), ("mo", 1), ("rho", 1), ("o48", 48), ("z48", 48), ("z3", 48), ("M48", 48), ("jR", 256),
-                    ("Fw", 1024), ("mk", 48), ("t2a", 16), ("T2", 16), ("RK", 256), ("dk", 256), ("nK", 2), ("sg", 2), ("jk", 512), ("Tn", 16), ("nd0", 16), ("nd", 16), ("md", 16), ("mn", 16),
-                    ("kh", 16), ("k1", 16), ("kap", 16), ("kapn", 16), ("kh2", 16), ("k12", 16), ("kap2", 16), ("hh", 16), ("hk", 16), ("u0", 8), ("u1", 8), ("p3", 16), ("hP", 48), ("kP", 48), ("lP", 48), ("lQ", 48), ("xP", 24), ("yP", 24), ("dP", 48),
-                    ("hN", 64), ("kN", 64), ("lN", 64), ("lO", 64), ("xN", 32), ("yN", 32), ("dN2", 64), ("posF", 16), ("lo", 16), ("lo1", 16), ("lo2", 16), ("df", 16), ("df2", 16), ("K2", 48), ("Bm", 48), ("c8", 48),
-                    ("MK", 4), ("mk0", 4), ("CP", 6), ("dg", 768), ("dh", 512), ("Sc", 6), ("sm", 4), ("ge", 2), ("c01", 2), ("m01c", 2), ("ncp", 2), ("mxa", 1), ("mxc", 2), ("Af", 2), ("Bf", 2),
-                    ("EB", 48), ("e24", 24), ("e12", 12), ("cpn", 6), ("io", 1024), ("Rn", 768), ("dR", 768), ("tR", 768), ("NB1", 48), ("NB2", 96), ("En", 96), ("fq", 96), ("g1", 32), ("g2", 32),
-                    ("fp", 48), ("f1", 16), ("f2", 16), ("yo", 256), ("q4", 6), ("q6", 6), ("qa", 2), ("qb", 2), ("qc", 2)): sb(name, n)
-    for name, n in (("TS", 64), ("TT", 64), ("Rp", 256), ("dA", 256), ("tA", 256), ("iJ", 256), ("Rpi", 256), ("dB", 256), ("tB", 256), ("Rpn", 256), ("Rq", 768), ("d2", 768), ("t2", 768),
-                    ("dn", 768), ("tn", 768), ("TC", 64), ("TD", 64), ("TP", 64), ("TQ", 64), ("RP", 256), ("dPr", 256), ("tPr", 256)): sb(name, n, "bfloat16")
-    for name, n in (("T2u", 16), ("lA", 16), ("lB", 16), ("lM", 16), ("posU", 16), ("piU", 16), ("nbL", 48), ("nbU", 48), ("lG", 48), ("lH", 48), ("nU", 32), ("n2U", 8), ("CLp", 64), ("CLn", 64)): sb(name, n, "uint16")
+    sb("hE", 516, "bfloat16"); sb("Ho", 1024, "bfloat16")
+    for name, n in (("pI", 1), ("rI", 1), ("gI", 1), ("uI", 1), ("aP", 1), ("yI", 256), ("wI", 256), ("rhoI", 1), ("zI", 48),
+                    ("vI", 48), ("aI", 48), ("nbI", 48), ("kI", 32), ("kA", 32)): sb(name, n, "int32")
+    for name, n in (("pF", 1), ("I", 128), ("mF", 256), ("rF", 1), ("g16", 1), ("gG", 1), ("rho", 1), ("o48", 48), ("z48", 48), ("z3", 48), ("M48", 48),
+                    ("Fw", 1024), ("mk", 48), ("t2a", 16), ("T2", 16), ("RK", 256), ("dk", 256), ("nK", 2), ("sg", 2), ("jk", 512), ("Tn", 16), ("c0", 32),
+                    ("kh", 32), ("k1", 32), ("kap", 32), ("hP", 48), ("kP", 48), ("lP", 48), ("lQ", 64), ("kP0", 1), ("mk0", 2), ("MS", 3), ("NP", 6), ("dN", 2), ("Bm", 48), ("c8", 48),
+                    ("dg", 792), ("dh", 792), ("Sc", 6), ("ge", 2), ("gd", 2), ("c01", 2), ("d2c", 2), ("gt", 2), ("ga", 2), ("A2", 2), ("A3", 1), ("Qf", 3), ("Tf", 3), ("ckB", 6), ("ngB", 2), ("mB", 16), ("mP", 2), ("ckm", 6),
+                    ("f1", 16), ("f2", 16), ("x1", 16), ("x2", 16), ("x3", 16), ("x4", 16), ("x5", 16), ("NBa", 16), ("NBd", 32), ("EB", 48), ("e24", 24), ("e12", 12), ("io", 1032), ("Rn", 768), ("dR", 768), ("tR", 768), ("yo", 256)): sb(name, n)
+    for name, n in (("TS", 64), ("TT", 64), ("Rp", 256), ("dA", 256), ("tA", 256), ("iJ", 256), ("Rpi", 256), ("tI", 256), ("dB", 256), ("tB", 256), ("Rpn", 256), ("Rq", 768), ("d2", 768), ("t2", 768),
+                    ("TC", 64), ("TD", 64), ("RO", 256), ("ROt", 256), ("RT", 256), ("RV", 256), ("RVt", 256)): sb(name, n, "bfloat16")
+    for name, n in (("T2u", 16), ("lA", 16), ("lB", 16), ("lM", 16), ("posU", 16), ("piU", 16), ("nbL", 48), ("nbU", 48), ("lG", 48), ("nU", 32), ("n2U", 8), ("LV", 16), ("CLd", 16)): sb(name, n, "uint16")
     for i in range(8): b["ps%d" % i] = ("psum", [128, 512], "float32")
     return b
 
 
 def _pack(b):
     out, place, fill = {}, {}, {"float32": 0, "int32": 0, "uint16": 0, "bfloat16": 0}
-    fixed = ("nbT", "xb", "wb", "hE", "half", "h0", "h1", "h2", "fl0", "fl1", "fl2", "m01_0", "m01_1", "m01_2")
+    fixed = ("nbT", "xb", "wb", "hE", "pF", "mF", "I", "Ho", "h0", "h1", "h2", "fl0", "fl1", "fl2", "m01_0", "m01_1", "m01_2")
     for name, (where, shape, d) in b.items():
         place[name] = (name, 0)
         if where != "sbuf" or d not in fill or name in fixed: out[name] = (where, shape, d)
@@ -57,7 +55,7 @@ def _pack(b):
 
 SCRATCH, PLACE = _pack(_bufs())
 WIDTH = {k: v[1][1] for k, v in _bufs().items()}
-SEMAPHORES = ["qv", "qs", "qt", "qg", "ldn", "ldx", "ldw", "ls", "st", "pst"] + ["x%s%d" % (k, t) for k in "csm" for t in range(R)]
+SEMAPHORES = ["qv", "qs", "qt", "qg", "ldn", "ldx", "ldw", "ls", "st"] + ["x%s%d" % (k, t) for k in "csm" for t in range(R)]
 
 
 def shares(T, topo, core):
@@ -85,7 +83,10 @@ def rank_program(g, core, T, topo):
 
     def clash(x, y):
         if x[2] <= y[1] or y[2] <= x[1]: return False
-        return not (x[3] == y[3] and x[3] > 1 and (x[1] - y[1]) % x[3])
+        if x[3] == y[3]: return x[3] == 1 or (x[1] - y[1]) % x[3] == 0
+        if x[3] > 1 and y[3] > 1: return True
+        (s, a, b), (c, e) = ((x[3], x[1], x[2]), y[1:3]) if x[3] > 1 else ((y[3], y[1], y[2]), x[1:3])
+        return a + max(0, -((a - c) // s)) * s < min(b, e)
 
     def need(q, rd, wr, acc=False):
         evs = []
@@ -134,9 +135,10 @@ def rank_program(g, core, T, topo):
     def cp(out, in_, q="v"):
         if q == "v": run("v", lambda e: e.tensor_copy(ap(out), ap(in_)), [in_], [out])
         else: run("s", lambda e: e.activation(ap(out), ap(in_), AF.Copy), [in_], [out])
+    def plus(out, in_, bias, scale=1.0): run("s", lambda e: e.activation(ap(out), ap(in_), AF.Identity, bias=bias, scale=scale), [in_], [out])
     def ms(out, c): run("v", lambda e: e.memset(ap(out), c), [], [out])
     def rsum(out, in_, negate=False): run("v", lambda e: e.tensor_reduce(ap(out), ap(in_), AxisListType.X, A.add, negate=negate), [in_], [out])
-    def tp(out, in_, p=None): run("v", lambda e: e.transpose(ap(out, p), ap(in_, p)), [in_], [out])
+    def tp(out, in_): run("v", lambda e: e.transpose(ap(out), ap(in_)), [in_], [out])
     def gather(out, win, off, q="v"):
         if q == "v": run("v", lambda e: e.tensor_copy(ap(out), ap(win).indirect(ap(off))), [win, off], [out])
         else: run("s", lambda e: e.activation(ap(out), ap(win).indirect(ap(off)), AF.Copy), [win, off], [out])
@@ -192,31 +194,15 @@ def rank_program(g, core, T, topo):
     iota(W("pI"), [[0, 1]], 0, 1)
     iota(W("o48"), [[0, 16], [1, 3]], 0, 0)
     iota(W("mF"), [[1, 256]], 0, 0)
-    iota(W("yI"), [[0, 16], [11, 16]], 10, 0)
-    iota(W("ju"), [[16, 16], [0, 16]], 0, 0)
-    ms(W("one"), 1.0)
+    iota(W("yI"), [[256, 16], [11, 16]], 10, 0)
+    iota(W("pF"), [[0, 1]], 0, 1)
+    iota(W("c8"), [[0, 6], [1, 8]], 0, 0)
+    ms(W("hE"), 0.0)
     for q in range(4):
         c, r = q ^ rank ^ 1, ("Fw", 256 * q, 256 * q + 256)
-        if q < rank: run("s", lambda e: e.activation(ap(r), ap(W("mF")), AF.Identity, bias=65536.0 * c, scale=256.0), [W("mF")], [r])
-        else: ms(r, 65536.0 * c)
+        if q < rank: plus(r, W("mF"), 1048576.0 * c, 4096.0)
+        else: ms(r, 1048576.0 * c)
     cp(W("iJ"), W("mF"), "s")
-    ms(W("TS"), 0.0)
-    ms(W("half"), 0.5)
-    run("g", lambda e: e.affine_select(ap(W("I")), ap(W("one")), [[-1, 128]], A.is_equal, 0.0, 0, 1), [W("one")], [W("I")])
-    def etile(b):
-        out = ("hE", 512 * b, 512 * b + 512)
-        settle()
-        run("g", lambda e: e.affine_select(ap(out), ap(W("half")), [[1, 512]], A.is_equal, 0.0, -b, -4), [W("half")], [out])
-    for b in range(2): etile(b)
-    ms(W("mk0"), 4e29)
-    def within(i, src, cm, base):
-        a, b = (src, i, i + 1), ("MK", i, i + 1)
-        run("g", lambda e: e.affine_select(ap(b), ap(a), [[0, 1]], A.is_ge, -4e29, base, cm), [a], [b])
-    within(0, "mk0", -1, 47)
-    within(2, "mk0", 1, -80)
-    within(1, "mk0", 1, -32)
-    settle()
-    within(1, "MK", -1, 79)
 
     def kappa(v, vi, ai, h, s, out):
         return [D(cp, vi, v), D(ts, h, v, 128.0, A.is_ge, 96.0, A.mult), D(ts, ai, vi, 96, A.bitwise_and), D(tt, s, v, ai, A.add), D(tt, out, s, h, A.subtract)]
@@ -227,37 +213,65 @@ def rank_program(g, core, T, topo):
     ts(W("uI"), W("gI"), 1, A.bitwise_and)
     weave([D(ts, W("z48"), W("o48"), W("rF"), A.add, 1.0, A.add), D(ts, W("zI"), W("z48"), 1.0 / 3.0, A.mult), D(ts, W("z3"), W("zI"), 3.0, A.mult), D(tt, W("M48"), W("z3"), W("z48"), A.is_equal)],
           [D(ts, W("rhoI"), W("rF"), 3.0, A.mult, 2.0, A.add), D(ts, W("rhoI"), W("rhoI"), 15, A.bitwise_and), D(cp, W("rho"), W("rhoI"))],
-          [D(ts, W("g16"), W("uI"), 16.0, A.mult)] + [D(ts, ("nd0", i, 16, 2), ("mF", 0, 256, 32), W("g16"), A.add) for i in range(2)] + [D(ts, W("md"), W("nd0"), W("rho"), A.add)]
-          + kappa(W("md"), W("kI"), W("kA"), W("kh"), W("k1"), W("kap")))
+          [D(ts, W("g16"), W("uI"), 16.0, A.mult), D(ms, W("TS"), 0.0), D(ms, W("TC"), 0.0)])
 
     weave([D(tt, W("mk"), W("nbT"), W("M48"), A.mult), D(tt, W("t2a"), ("mk", 0, 48, 3), ("mk", 1, 48, 3), A.add), D(tt, W("T2"), W("t2a"), ("mk", 2, 48, 3), A.add), D(cp, W("T2u"), W("T2"))],
-          [D(ts, W("wI"), W("yI"), 15, A.bitwise_and), D(tt, W("jR"), W("wI"), W("ju"), A.add)])
-    run("v", lambda e: e.tensor_tensor(ap(W("RK")), ap(W("Fw")).indirect(ap(W("T2u"))), ap(W("jR")), A.add), [W("Fw"), W("T2u"), W("jR")], [W("RK")])
+          [D(ts, W("wI"), W("yI"), 3855, A.bitwise_and), D(ts, W("I"), ("mF", 0, 128), W("pF"), A.is_equal)])
+    run("v", lambda e: e.tensor_tensor(ap(W("RK")), ap(W("Fw")).indirect(ap(W("T2u"))), ap(W("wI")), A.add), [W("Fw"), W("T2u"), W("wI")], [W("RK")])
+    cp(W("nbU"), W("nbT"))
+    for h in range(2): tt(("dk", 128 * h, 128 * h + 128), ("RK", 128 * h, 128 * h + 128), W("I"), A.mult)
     for h in range(2):
-        d = ("dk", 128 * h, 128 * h + 128)
-        tt(d, ("RK", 128 * h, 128 * h + 128), W("I"), A.mult)
-        rsum(("nK", h, h + 1), d, negate=True)
+        rsum(("nK", h, h + 1), ("dk", 128 * h, 128 * h + 128), negate=True)
         jk, b, o = ("jk", 256 * h, 256 * h + 256), ("nK", h, h + 1), ("sg", h, h + 1)
         run("s", lambda e: e.activation(ap(jk), ap(W("RK")), AF.Sign, bias=ap(b), accum_out=ap(o)), [W("RK"), b], [jk, o])
+    run("s", lambda e: e.activation(ap(("hE", 3, 515, 4)), ap(W("I")), AF.Copy, scale=0.5), [W("I")], [("hE", 3, 515, 4)])
+    for q in range(4): plus(("io", 256 * q, 256 * q + 256), W("mF"), 256.0 * q - 1.0)
+    plus(("io", 1024, 1032), ("mF", 0, 8), 1023.0)
     ts(W("nbI"), W("nbT"), 255, A.bitwise_and)
+    quant(("X", 0, 256), W("xb"))
+    cp(W("nbL"), W("nbI"))
     ts(("TS", 0, 64, 32), W("sg"), -0.5, A.mult, 127.5, A.add)
     tp(W("TT"), W("TS"))
     spread("Rp", "TT")
-    for b in range(2, 4): etile(b)
-    weave([D(ts, W("mn"), ("mF", 0, 256, 16), W("rho"), A.add)] + kappa(W("mn"), W("kL"), W("kB"), W("kh2"), W("k12"), W("kap2")) + [D(cp, W("lM"), W("kap2"))],
-          [D(cp, W("lA"), W("kap")), D(ts, W("nd"), W("nd0"), W("rF"), A.add), D(cp, W("nbL"), W("nbI")), D(cp, W("lB"), W("nd")), D(quant, ("X", 0, 256), W("xb")), D(cp, W("mo"), W("uI")), D(ts, W("me"), W("mo"), -1.0, A.mult, 1.0, A.add)])
-    weave(kappa(W("nd"), W("vI0"), W("aI0"), W("hh"), W("hk"), W("kapn")) + [D(cp, ("CLp", 0, 16), W("kapn"))],
-          [D(ms, ("K2", 16 * k, 16 * k + 16), 2 * CODE[k]) for k in range(3)] + [D(ms, W("CP"), BIG), D(ms, W("TC"), 0.0), D(ts, W("Tn"), ("mF", 0, 256, 16), W("rF"), A.add)])
-
+    cp(("c0", 0, 16), ("mF", 0, 256, 16))
+    for i in range(2): ts(("c0", 16 + i, 32, 2), ("mF", 0, 256, 32), W("g16"), A.add)
+    weave(kappa(W("c0"), W("kI"), W("kA"), W("kh"), W("k1"), W("kap")),
+          [D(quant, ("E", 128 * b, 128 * b + 128), ("hE", 3 - b, 515 - b)) for b in range(4)])
+    ts(W("aP"), W("pI"), 96, A.bitwise_and)
+    ts(W("lA"), ("kap", 16, 32), W("rho"), A.add)
+    ts(W("lM"), ("kap", 0, 16), W("rho"), A.add)
+    ts(W("lB"), ("c0", 16, 32), W("rF"), A.add)
+    tt(W("kP0"), W("pI"), W("aP"), A.add)
+    gather(W("Rn"), W("io"), W("nbU"), "s")
     gather(W("dA"), W("Rp"), W("lA"))
+    ts(("mk0", 0, 1), W("kP0"), -256.0, A.add)
     tp(W("tA"), W("dA"))
+    ts(("mk0", 1, 2), W("kP0"), -224.0, A.add)
     cp(W("posU"), ("tA", 0, 256, 16))
+    ts(W("CLd"), ("kap", 16, 32), W("rF"), A.add)
     run("v", lambda e: e.tensor_copy(ap(W("Rpi")).indirect(ap(W("posU"))), ap(W("iJ"))), [W("posU"), W("iJ")], [W("Rpi")])
+    def within(out, src, cm, base): run("g", lambda e: e.affine_select(ap(out), ap(src), [[0, 1]], A.is_ge, 0.0, base, cm), [src], [out])
+    settle()
+    within(("MS", 0, 1), ("mk0", 0, 1), -1, 47)
+    within(("MS", 2, 3), ("mk0", 1, 2), 1, -80)
+    within(("MS", 1, 2), ("mk0", 1, 2), 1, -32)
+    settle()
+    within(("MS", 1, 2), ("MS", 1, 2), -1, 79)
     gather(W("Rpn"), W("Rp"), W("lM"), "s")
     gather(W("Rq"), W("Rpn"), W("nbL"), "s")
-    gather(W("dB"), W("Rpi"), W("lB"))
+    ts(("lQ", 48, 64), ("kap", 0, 16), W("rF"), A.add)
+    tp(W("tI"), W("Rpi"))
+    gather(W("dB"), W("Rpi"), W("lB"), "s")
+    ts(W("Tn"), ("mF", 0, 256, 16), W("rF"), A.add)
+    def where(k, q):
+        for i in range(2): ts(("lG", 16 * k + i, 16 * k + 16, 2), ("tI", 0, 256, 32), 3.0, A.mult, float(k), A.add)
+        gather(("d2", 256 * k, 256 * k + 256), W("Rq"), ("lG", 16 * k, 16 * k + 16), q)
+    where(1, "s")
+    where(0, "v")
     tp(W("tB"), W("dB"))
+    tp(("t2", 0, 256), ("d2", 0, 256))
     cp(W("piU"), ("tB", 0, 256, 16))
+    cp(("nU", 0, 16), ("t2", 0, 256, 16))
     pick(("W0", 0, 256), ("X", 0, 256), W("piU"))
 
     def exchange(t):
@@ -272,184 +286,205 @@ def rank_program(g, core, T, topo):
 
     def neighbours2(t): pick(("M%d" % t,) + LOC, ("W%d" % t, 0, 256), ("n2U", 0, 7))
 
-    def score(t, k, h, bank):
+    def product(t, k, h, bank):
         mov = ("N%d" % t, 256 * k + 128 * h, 256 * k + 128 * h + 128) if k < 2 else ("M%d" % t, 128 * h, 128 * h + 128)
         mm(bank, 128, ("W%d" % t, 128 * h, 128 * h + 128), mov)
-        d = ("dg", 128 * (2 * k + h), 128 * (2 * k + h) + 128)
-        tt(d, ("ps%d" % bank, 0, 128), W("I"), A.mult)
-        return d, ("Sc", 2 * k + h, 2 * k + h + 1)
+
+    def score(k, h, bank, q):
+        i = 2 * k + h
+        d, s, j = ("dg", 132 * i, 132 * i + 129), ("Sc", i, i + 1), ("dh", 132 * i, 132 * i + 129)
+        tt(("dg", 132 * i, 132 * i + 128), ("ps%d" % bank, 0, 128), W("I"), A.mult)
+        if q == "s": run("s", lambda e: e.activation(ap(j), ap(d), AF.Copy, accum_out=ap(s)), [d], [j, s])
+        else: return D(rsum, s, d)
+
+    def halves(t, parts):
+        for b in parts: mm(BANKS[0][b], 256, ("E", 128 * b, 128 * b + 128), ("W%d" % t, 0, 256), True, b in VPARTS)
+
+    def keep():
+        for b in VPARTS: cp(("Ho", b, 1024, 4), ("ps%d" % BANKS[0][b], 0, 256), "s")
+
+    def unpack(t, k, parts=(0, 1, 2, 3)):
+        mov = ("N%d" % t, 256 * k, 256 * k + 256) if k < 2 else ("M%d" % t, 0, 256)
+        for b in parts:
+            e, bank, alone = ("E", 128 * b, 128 * b + 128), BANKS[k][b], k != 1 and b in VPARTS
+            if k and not alone: mm(bank, 256, e, ("W%d" % t, 0, 256), True, False)
+            mm(bank, 256, e, mov, alone, True)
+
+    def cast(k, parts=(0, 1, 2, 3)):
+        for b in parts:
+            out, bank = ("h%d" % k, b, 1024, 4), ("ps%d" % BANKS[k][b], 0, 256)
+            if k != 1 and b in VPARTS: tt(out, bank, ("Ho", b, 1024, 4), A.add)
+            else: cp(out, bank, "s")
+
+    def candidate(t, k): quant(("W%d" % t, 256 * (k + 1), 256 * (k + 2)), W("h%d" % k))
 
     def local(t):
-        for k in range(2):
-            for h in range(2):
-                d, s = score(t, k, h, 2 * k + h)
-                j = ("dh", 128 * h, 128 * h + 128)
-                if k == 0: run("s", lambda e: e.activation(ap(j), ap(d), AF.Copy, accum_out=ap(s)), [d], [j, s])
-                else: rsum(s, d)
-        tt(W("sm"), ("Sc", 0, 4), ("CP", 0, 4), A.min)
+        halves(t, (0, 1))
+        for h in range(2): product(t, 0, h, h)
+        halves(t, (2, 3))
+        for h in range(2): product(t, 1, h, 2 + h)
+        keep()
+        for h in range(2): score(0, h, h, "s")
+        score(1, 0, 2, "s")
+        score(1, 1, 3, "v")()
         m, fl = "m01_%d" % t, "fl%d" % t
-        tt(W(m), ("sm", 0, 2), ("sm", 2, 4), A.max)
+        tt(W(m), ("Sc", 0, 2), ("Sc", 2, 4), A.max)
         def what(d):
             r = (m, FAR[d][0] // 128, FAR[d][0] // 128 + 1)
             return ap(r), ap((fl, d, d + 1)), r
         send(what, "xm%d" % t)
         arrives("xm%d" % t, incoming, [W(fl)])
-        tt(W("ge"), ("sm", 0, 2), ("sm", 2, 4), A.is_ge)
-        ts(W("ncp"), ("CP", 4, 6), -1.0, A.mult)
-        ts(W("c01"), W("ge"), CODE[0] - CODE[1], A.mult, CODE[1], A.add)
-        tt(W("m01c"), W(m), W("ncp"), A.max)
+        unpack(t, 0)
+        cast(0)
+        unpack(t, 1, range(NB))
+        tt(W("ge"), ("Sc", 0, 2), ("Sc", 2, 4), A.is_ge)
 
-    def unpack(t, k, parts=(0, 1, 2, 3)):
-        mov = ("N%d" % t, 256 * k, 256 * k + 256) if k < 2 else ("M%d" % t, 0, 256)
-        for b in parts:
-            e = ("E", 128 * b, 128 * b + 128)
-            if (k, b) not in AHEAD or t == 0: mm(BANKS[k][b], 256, e, ("W%d" % t, 0, 256), True, False)
-            mm(BANKS[k][b], 256, e, mov, False, True)
-        for b in parts: cp(("h%d" % k, b, 1024, 4), ("ps%d" % BANKS[k][b], 0, 256), "s")
-
-    def candidate(t, k): quant(("W%d" % t, 256 * (k + 1), 256 * (k + 2)), W("h%d" % k))
+    def prefer():
+        return [D(tt, W("gd"), W("ge"), W("dN"), A.mult), D(tt, W("c01"), W("gd"), ("NP", 2, 4), A.add), D(tt, W("d2c"), ("NP", 4, 6), W("c01"), A.subtract)]
 
     def choose(t):
         fl = "fl%d" % t
-        for d, s in [score(t, 2, h, h) for h in range(2)]: rsum(s, d)
-        ts(("mxc", 0, 1), (fl, 1, 2), ("MK", 0, 1), A.min, ("m01c", 0, 1), A.max)
-        ts(W("mxa"), (fl, 3, 4), ("MK", 1, 2), A.min, ("m01c", 1, 2), A.max)
-        for h in range(2): ts(("Af", h, h + 1), ("Sc", 4 + h, 5 + h), ("m01c", h, h + 1), A.is_gt, ("c01", h, h + 1), A.max)
-        ts(("mxc", 1, 2), (fl, 2, 3), ("MK", 2, 3), A.min, W("mxa"), A.max)
-        for h in range(2): ts(("Bf", h, h + 1), ("Sc", 4 + h, 5 + h), ("mxc", h, h + 1), A.is_gt, CODE[2] - 1.0, A.mult)
-        tt(("TC", 0, 64, 32), W("Af"), W("Bf"), A.add)
+        for h in range(2): product(t, 2, h, h)
+        cast(1, range(NB))
+        for f in [score(2, h, h, "v") for h in range(2)]: f()
+        ms(("RC%d" % t, 256, 272), -1.0)
+        tt(W("gt"), ("Sc", 4, 6), W("m01_%d" % t), A.is_gt)
+        ms(W("D0_%d" % t), 0.0)
+        tt(W("ga"), W("gt"), W("d2c"), A.mult)
+        ts(("Qf", 0, 1), ("MS", 0, 1), ("gt", 0, 1), A.mult)
+        ts(("Qf", 1, 3), ("MS", 1, 3), ("gt", 1, 2), A.mult)
+        tt(W("A2"), W("ga"), W("c01"), A.add)
+        ts(("Tf", 2, 3), (fl, 2, 3), ("Sc", 5, 6), A.is_lt, ("Qf", 2, 3), A.mult)
+        ts(("Tf", 1, 2), (fl, 3, 4), ("Sc", 5, 6), A.is_lt, ("Qf", 1, 2), A.mult)
+        ts(("Tf", 0, 1), (fl, 1, 2), ("Sc", 4, 5), A.is_lt, ("Qf", 0, 1), A.mult)
+        tt(W("A3"), ("Tf", 2, 3), ("A2", 1, 2), A.add)
+        tt(("TC", 0, 1), ("Tf", 0, 1), ("A2", 0, 1), A.add)
+        tt(("TC", 32, 33), ("Tf", 1, 2), W("A3"), A.add)
         tp(W("TD"), W("TC"))
         spread("RC%d" % t, "TD")
-        candidate(t, 0)
+        unpack(t, 1, range(NB, 4))
+        cast(1, range(NB, 4))
+        unpack(t, 2)
+        cast(2)
+        for k in range(3): candidate(t, k)
 
-    def decide(t, cl, base):
-        cd, ct, s, f, f2, l = ["%s%d" % (n, t) for n in ("CD", "CT", "S", "Fd", "F2", "L")]
-        for i in range(4): gather((cd, 256 * i, 256 * i + 256), W("RC%d" % t), (cl, 16 * i, 16 * i + 16), "vvss"[i])
-        for i in range(4): tp((ct, 256 * i, 256 * i + 256), (cd, 256 * i, 256 * i + 256))
-        for k in range(3): tt((s, 16 * k, 16 * k + 16), (ct, 0, 256, 16), (ct, 256 * (k + 1), 256 * (k + 2), 16), A.add)
-        for k in range(3): ts((f, 16 * k, 16 * k + 16), (s, 16 * k, 16 * k + 16), 2 * CODE[k], A.is_equal, 256.0 * (k + 1), A.mult)
-        candidate(t, 1)
-        tt((f2, 0, 16), (f, 0, 16), (f, 16, 32), A.add)
-        tt((f2, 16, 32), (f, 32, 48), W(base), A.add)
-        tt(W(l), (f2, 0, 16), (f2, 16, 32), A.add)
-        cp(W("U%d" % t), W(l))
+    def decide(t):
+        rc, d0, d1, ls, e1, e2 = ["%s%d" % (n, t) for n in ("RC", "D0_", "D1_", "Ls", "e1_", "e2_")]
+        gather(W("RO"), (rc, 0, 256), W("CLd"), "s")
+        tp(W("RT"), (rc, 0, 256))
+        for h in range(2):
+            for s in range(2): cp(("LV", 8 * h + s, 8 * h + 8, 2), ("RT", 32 * h, 256, 64))
+        gather(W("RV"), (rc, 0, 272), W("LV"), "s")
+        if t < R - 1: numbers(t)
+        else:
+            rows(1, "s")
+            store(1)
+        tp(W("ROt"), W("RO"))
+        cp((d1, 1, 32, 2), W("Tn"))
+        v = ("ROt", 0, 256, 16)
+        tt(W(e1), v, ("lQ", 16, 32), A.is_equal)
+        tt(W(e2), v, ("lQ", 32, 48), A.is_equal)
+        ts(W("f1"), W(e1), 256.0, A.mult, 256.0, A.add)
+        ts(W("f2"), W(e2), 512.0, A.mult)
+        if t < R - 1: ts(("ckB", 4, 6), W("gt"), -BIG, A.mult)
+        tt((d1, 0, 32, 2), W("f1"), W("f2"), A.add)
+        if t < R - 1:
+            ts(W("ngB"), W("gt"), BIG, A.mult, -BIG, A.add)
+            tt(("ckB", 0, 2), W("ngB"), W("ge"), A.mult)
+            tt(("ckB", 2, 4), W("ngB"), ("ckB", 0, 2), A.subtract)
+        else:
+            for f in partner(t): f()
+        tp(W("RVt"), W("RV"))
+        tt((d0, 1, 32, 2), ("RVt", 0, 256, 16), ("lQ", 48, 64), A.is_equal)
+        run("v", lambda e: e.tensor_tensor_scan(ap(W(ls)), ap(W(d0)), ap(W(d1)), 0.0, A.mult, A.add), [W(d0), W(d1)], [W(ls)])
+        cp(W("U%d" % t), (ls, 1, 32, 2))
 
     def caps(t):
-        e6 = W("e6_%d" % t)
-        return [D(tt, W("Eq%d" % t), W("S%d" % t), W("K2"), A.is_equal), D(tt, W("EB"), W("Eq%d" % t), W("Bm"), A.mult), D(tt, W("e24"), ("EB", 0, 48, 2), ("EB", 1, 48, 2), A.add),
-                D(tt, W("e12"), ("e24", 0, 24, 2), ("e24", 1, 24, 2), A.add), D(tt, e6, ("e12", 0, 12, 2), ("e12", 1, 12, 2), A.add),
-                D(ts, W("cpn"), e6, -2 * BIG, A.mult, BIG, A.add), D(tt, W("CP"), W("CP"), W("cpn"), A.min)]
+        cl = ("dg", 128, 792, 132)
+        return [D(tt, W("mB"), ("D0_%d" % t, 1, 32, 2), ("Bm", 0, 16), A.mult)] + [D(rsum, ("mP", h, h + 1), ("mB", 8 * h, 8 * h + 8)) for h in range(2)] \
+            + [D(ts, ("ckm", h, 6, 2), ("ckB", h, 6, 2), ("mP", h, h + 1), A.mult) for h in range(2)] + [D(tt, cl, cl, W("ckm"), A.add)]
 
-    def pairs(t, e):
-        tt(W("fp"), W(e), W("NB1"), A.mult)
-        tt(W("f1"), ("fp", 0, 16), ("fp", 16, 32), A.add)
-        tt(W("f2"), W("f1"), ("fp", 32, 48), A.add)
-        ts(("pt%d" % t, 0, 16), W("f2"), -1.0, A.add)
-        tp(W("pu%d" % t), W("pt%d" % t), (0, 32))
-        need("y", [W("pu%d" % t)], [])
-        g.sync.dma_start(T.pr[t:t + 1, :], ap(("pu%d" % t, 0, 16), (0, 16))).then_inc(T.sem.pst, 16)
+    def numbers(k): gather(("dR", 256 * k, 256 * k + 256), W("Rn"), ("lG", 16 * k, 16 * k + 16), "s")
 
-    def dup(v, x, y, out, n):
-        return [D(ts, x, (v, 0, n, 2), W("me"), A.mult), D(ts, y, (v, 1, n, 2), W("mo"), A.mult)] + [D(tt, (out, i, n, 2), x, y, A.add) for i in range(2)]
+    def partner(t):
+        return [D(tt, W("x1"), W("e1_%d" % t), ("NBd", 0, 16), A.mult), D(tt, W("x2"), W("e2_%d" % t), ("NBd", 16, 32), A.mult), D(tt, W("x3"), W("x1"), W("NBa"), A.add), D(tt, W("x4"), W("x2"), W("x3"), A.add)]
+
+    def listed(t):
+        return [D(tt, W("x5"), ("D0_%d" % t, 1, 32, 2), W("x4"), A.mult), D(cp, W("V%d" % t), W("x5"))]
+
+    def rows(t, q):
+        gather(W("PRp%d" % t), W("io"), W("V%d" % t), q)
+        gather(W("PRn%d" % t), W("PRp%d" % t), W("posU"), q)
+
+    def store(t):
+        need("y", [W("PRn%d" % t)], [])
+        g.sync.dma_start(T.pr[t:t + 1, :], ap(W("PRn%d" % t), (0, 1))).then_inc(T.sem.st, 16)
 
     exchange(0)
-    ts(W("u0"), ("tB", 0, 256, 32), 3.0, A.mult, W("me"), A.mult)
-    ts(W("u1"), ("tB", 16, 256, 32), 3.0, A.mult, W("mo"), A.mult)
-    for i in range(2): tt(("p3", i, 16, 2), W("u0"), W("u1"), A.add)
-    def where(k, q):
-        ts(("lG", 16 * k, 16 * k + 16), W("p3"), float(k), A.add)
-        gather(("d2", 256 * k, 256 * k + 256), W("Rq"), ("lG", 16 * k, 16 * k + 16), q)
-    where(1, "s")
-    where(0, "v")
-    for k in (0, 1):
-        tp(("t2", 256 * k, 256 * k + 256), ("d2", 256 * k, 256 * k + 256))
-        cp(("nU", 16 * k, 16 * k + 16), ("t2", 256 * k, 256 * k + 256, 16))
-        neighbours(0, k)
-    where(2, "s")
-    quant(("E", 0, 512), W("hE"))
+    neighbours(0, 0)
+    tp(("t2", 256, 512), ("d2", 256, 512))
+    ts(("dg", 128, 792, 132), ("mF", 0, 6), 0.0, A.mult)
+    cp(("nU", 16, 32), ("t2", 256, 512, 16))
+    neighbours(0, 1)
+    for i in range(2): ts(("lG", 32 + i, 48, 2), ("tI", 0, 256, 32), 3.0, A.mult, 2.0, A.add)
     local(0)
-    tp(("t2", 512, 768), ("d2", 512, 768))
-    weave([D(cp, ("n2U", 0, 7), ("t2", 512 + LOC[0], 512 + LOC[1], 16)), D(neighbours2, 0)] + [D(ts, ("lH", 16 * k, 16 * k + 16), W("nd"), 3.0, A.mult, float(k), A.add) for k in range(3)],
-          [D(cp, W("lP"), ("t2", 0, 768, 16))] + [D(cp, ("lP", 32 + a, 32 + b), ("Tn", a, b)) for a, b in ((0, LOC[0] // 16), (LOC[1] // 16, 16))]
-          + kappa(W("lP"), ("vI", 0, 48), ("aI", 0, 48), W("hP"), W("kP"), W("lQ")) + dup("lQ", W("xP"), W("yP"), "dP", 48) + [D(cp, ("CLp", 16, 64), W("dP"))])
-    iota(W("io"), [[1, 1024]], 0, 0)
-    iota(W("c8"), [[0, 6], [1, 8]], 0, 0)
-    for k in range(3): gather(("dn", 256 * k, 256 * k + 256), W("Rq"), ("lH", 16 * k, 16 * k + 16), "s")
-    unpack(0, 0)
-    choose(0)
+    gather(("d2", 512, 768), W("Rq"), ("lG", 32, 48), "s")
+    cp(("lP", 0, 32), ("t2", 0, 512, 16))
     cp(W("gG"), W("gI"))
+    for a, b in ((0, LOC[0] // 16), (LOC[1] // 16, 16)): cp(("lP", 32 + a, 32 + b), ("Tn", a, b))
     ts(W("Bm"), W("c8"), W("gG"), A.is_equal)
+    tp(("t2", 512, 768), ("d2", 512, 768))
+    cp(("n2U", 0, 7), ("t2", 512 + LOC[0], 512 + LOC[1], 16))
+    cp(("lP", 32 + LOC[0] // 16, 32 + LOC[1] // 16), ("t2", 512 + LOC[0], 512 + LOC[1], 16))
+    weave(kappa(W("lP"), W("vI"), W("aI"), W("hP"), W("kP"), ("lQ", 0, 48)), [D(neighbours2, 0)])
+    tt(W("EB"), ("lQ", 0, 48), W("Bm"), A.mult)
+    tt(W("e24"), ("EB", 0, 48, 2), ("EB", 1, 48, 2), A.add)
+    tt(W("e12"), ("e24", 0, 24, 2), ("e24", 1, 24, 2), A.add)
+    tt(W("NP"), ("e12", 0, 12, 2), ("e12", 1, 12, 2), A.add)
+    tt(W("dN"), ("NP", 0, 2), ("NP", 2, 4), A.subtract)
+    tt(("NP", 4, 6), ("NP", 4, 6), ("MS", 0, 2), A.subtract)
+    weave(prefer()[:2], [D(tt, ("NP", 5, 6), ("NP", 5, 6), ("MS", 2, 3), A.subtract)])
+    prefer()[2]()
+    choose(0)
 
     for t in range(R):
-        last = t == R - 1
-        unpack(t, 1, range(NB if t else 0, 4))
-        decide(t, "CLn" if last else "CLp", "posF" if last else "Tn")
-        unpack(t, 2)
-        candidate(t, 2)
-        if last: break
+        decide(t)
+        if t == R - 1: break
         u = t + 1
         pick(("W%d" % u, 0, 256), ("W%d" % t, 0, 1024), W("U%d" % t))
         exchange(u)
-        for k, b in AHEAD: mm(BANKS[k][b], 256, ("E", 128 * b, 128 * b + 128), ("W%d" % u, 0, 256), True, False)
-        weave([D(neighbours, u, 0), D(neighbours, u, 1)], caps(t))
+        cl = caps(t)
+        weave([D(neighbours, u, 0), D(neighbours, u, 1)], cl[:1])
+        for f in cl[1:]: f()
         local(u)
-        neighbours2(u)
-        unpack(u, 0)
-        unpack(u, 1, range(NB))
-        if u == 1:
-            for i in range(R): ms(("pt%d" % i, 16, 32), 0.0)
-            cp(W("nbU"), W("nbT"))
-            gather(W("Rn"), W("io"), W("nbU"), "s")
-            for k in range(3): gather(("dR", 256 * k, 256 * k + 256), W("Rn"), ("lH", 16 * k, 16 * k + 16), "s")
-            weave([D(tp, ("tn", 256 * k, 256 * k + 256), ("dn", 256 * k, 256 * k + 256)) for k in range(3)] + [D(cp, ("lN", 16, 48), ("tn", 0, 512, 16)), D(tt, W("df"), ("tn", 512, 768, 16), W("posF"), A.subtract),
-                  D(tt, W("df2"), W("df"), W("lo"), A.mult), D(tt, ("lN", 48, 64), W("df2"), W("posF"), A.add)] + kappa(W("lN"), W("vN"), W("aN"), W("hN"), W("kN"), W("lO")) + dup("lO", W("xN"), W("yN"), "dN2", 64) + [D(cp, W("CLn"), W("dN2"))],
-                  [D(cp, W("posF"), ("tA", 0, 256, 16)), D(cp, ("lN", 0, 16), W("posF")), D(ts, W("lo1"), W("posF"), float(LOC[0]), A.is_ge), D(ts, W("lo2"), W("posF"), float(LOC[1]), A.is_lt), D(tt, W("lo"), W("lo1"), W("lo2"), A.mult)])
-            choose(u)
-            ms(W("TP"), 0.0)
+        weave(prefer(), [D(neighbours2, u)])
+        if u == 1: numbers(2)
+        else:
             quant(("wq", 0, 128), W("wb"))
             for k in range(3): tp(("tR", 256 * k, 256 * k + 256), ("dR", 256 * k, 256 * k + 256))
-            ts(W("NB1"), ("tR", 0, 768, 16), 1.0, A.add)
-        else:
-            for k in range(3):
-                for i in range(2): cp(("NB2", 32 * k + 16 * i, 32 * k + 16 * i + 16), ("NB1", 16 * k, 16 * k + 16), "s")
-            ts(W("q4"), W("e6_1"), 4.0, A.mult)
-            tt(W("q6"), W("q4"), W("e6_0"), A.add)
-            ts(W("qa"), ("q6", 2, 4), 2.0, A.mult)
-            ts(W("qc"), ("q6", 4, 6), 3.0, A.mult)
-            tt(W("qb"), ("q6", 0, 2), W("qa"), A.add)
-            tt(("TP", 0, 64, 32), W("qb"), W("qc"), A.add)
-            tp(W("TQ"), W("TP"))
-            spread("RP", "TQ")
-            choose(u)
-            gather(W("dPr"), W("RP"), ("CLn", 0, 16))
-            tp(W("tPr"), W("dPr"))
-            cp(W("pv"), ("tPr", 0, 256, 16))
-            ts(W("pv0"), W("pv"), 3, A.bitwise_and)
-            ts(W("pv1"), W("pv"), 2, A.logical_shift_right)
+            ts(W("NBa"), ("tR", 0, 256, 16), 2.0, A.add)
+            for k in (1, 2): tt(("NBd", 16 * k - 16, 16 * k), ("tR", 256 * k, 256 * k + 256, 16), ("tR", 0, 256, 16), A.subtract)
             for i in range(2):
-                for k in range(3): ts(("En", 32 * k + 16 * i, 32 * k + 16 * i + 16), W("pv%d" % i), float(k + 1), A.is_equal)
+                for f in partner(i) + listed(i): f()
+            rows(0, "s")
+            store(0)
+        choose(u)
 
     t = R - 1
-    pick(("Z", 0, 256), ("W%d" % t, 0, 1024), W("U%d" % t))
+    pick(("H", 0, 256), ("W%d" % t, 0, 1024), W("U%d" % t))
+    for f in listed(t): f()
+    pick(("Z", 0, 256), ("H", 0, 256), W("posU"))
+    rows(t, "v")
     need("y", [("Zc", 0, 256)], [])
     g.sync.dma_start(T.oc[:, :], octets(("Zc", 0, 256))).then_inc(T.sem.st, 16)
-    tt(W("Eq%d" % t), W("S%d" % t), W("K2"), A.is_equal)
-    pairs(t, "Eq%d" % t)
     mm(0, 256, ("wq", 0, 128), ("Z", 0, 256))
-    need("s", [("Zs", 0, 256)], [])
-    for k in range(4): g.scalar.dma_start(T.osc[4 * k:4 * k + 4, :], T.Zs[32 * k:32 * k + 4, 0:256]).then_inc(T.sem.st, 16)
-    cp(W("yo"), ("ps0", 0, 256))
-    tt(W("fq"), W("En"), W("NB2"), A.mult)
-    tt(W("g1"), ("fq", 0, 32), ("fq", 32, 64), A.add)
-    tt(W("g2"), W("g1"), ("fq", 64, 96), A.add)
-    ts(W("pt0"), W("g2"), -1.0, A.add)
-    tp(W("pu0"), W("pt0"), (0, 32))
-    need("s", [W("pu0")], [])
-    g.scalar.dma_start(T.pr[0:2, :], ap(("pu0", 0, 16), (0, 32))).then_inc(T.sem.pst, 16)
-    need("y", [W("yo")], [])
-    g.sync.dma_start(T.y[:, :], ap(W("yo"))).then_inc(T.sem.st, 16)
-    g.sync.wait_ge(T.sem.st, 16 * 6)
-    g.sync.wait_ge(T.sem.pst, 32)
+    need("y", [("Zs", 0, 256)], [])
+    for k in range(4): g.sync.dma_start(T.osc[4 * k:4 * k + 4, :], T.Zs[32 * k:32 * k + 4, 0:256]).then_inc(T.sem.st, 16)
+    cp(W("yo"), ("ps0", 0, 256), "s")
+    need("s", [W("yo")], [])
+    g.scalar.dma_start(T.y[:, :], ap(W("yo"))).then_inc(T.sem.st, 16)
+    store(t)
+    g.sync.wait_ge(T.sem.st, 16 * (6 + R))
     g.wait_ge(T.sem.ls, sent[0])
     for q, sem in qsem.items():
         if known["g"].get(sem, 0) < count[sem]: g.wait_ge(T.sem[sem], count[sem])

@@ -6,8 +6,10 @@ FAR = {1: (0, 48), 3: (160, 208), 2: (208, 256)}
 LOC = (48, 160)
 BIG = 1e29
 BANKS = ((4, 5, 6, 7), (4, 5, 6, 7), (2, 3, 0, 1))
-NB = 2
 VPARTS = (0, 1)
+AHEAD = (("u", 0, 0), ("u", 0, 1), ("u", 0, 2), ("u", 0, 3))
+BESIDE = (("q", 0), ("u", 2, 0), ("u", 2, 1), ("u", 1, 0), ("u", 1, 1), ("u", 1, 2), ("u", 1, 3), ("q", 1), ("l",), ("u", 2, 2), ("u", 2, 3))
+AFTER = (("f",), ("q", 2))
 
 
 def _bufs():
@@ -20,9 +22,8 @@ def _bufs():
     mx("X", 256); mx("wq", 128); mx("E", 512); mx("H", 256); mx("Z", 256)
     for t in range(R):
         mx("W%d" % t, 1024); mx("N%d" % t, 512); mx("M%d" % t, 256)
-        sb("fl%d" % t, 4); sb("m01_%d" % t, 2); sb("RC%d" % t, 272, "bfloat16"); sb("U%d" % t, 16, "uint16"); sb("V%d" % t, 16, "uint16")
-        for name in ("D0_", "D1_", "Ls"): sb("%s%d" % (name, t), 32)
-        for name in ("e1_", "e2_"): sb("%s%d" % (name, t), 16)
+        sb("fl%d" % t, 4); sb("m01_%d" % t, 3); sb("RC%d" % t, 272, "bfloat16"); sb("U%d" % t, 16, "uint16")
+        for name in ("S0_", "S1_", "Ls"): sb("%s%d" % (name, t), 64)
         sb("PRp%d" % t, 256); sb("PRn%d" % t, 256)
     for k in range(3): sb("h%d" % k, 1024, "bfloat16")
     sb("hE", 516, "bfloat16"); sb("Ho", 1024, "bfloat16")
@@ -31,11 +32,11 @@ def _bufs():
     for name, n in (("pF", 1), ("I", 128), ("mF", 256), ("rF", 1), ("g16", 1), ("gG", 1), ("rho", 1), ("o48", 48), ("z48", 48), ("z3", 48), ("M48", 48),
                     ("Fw", 1024), ("mk", 48), ("t2a", 16), ("T2", 16), ("RK", 256), ("dk", 256), ("nK", 2), ("sg", 2), ("jk", 512), ("Tn", 16), ("c0", 32),
                     ("kh", 32), ("k1", 32), ("kap", 32), ("hP", 48), ("kP", 48), ("lP", 48), ("lQ", 64), ("kP0", 1), ("mk0", 2), ("MS", 3), ("NP", 6), ("dN", 2), ("Bm", 48), ("c8", 48),
-                    ("dg", 792), ("dh", 792), ("Sc", 6), ("ge", 2), ("gd", 2), ("c01", 2), ("d2c", 2), ("gt", 2), ("ga", 2), ("A2", 2), ("A3", 1), ("Qf", 3), ("Tf", 3), ("ckB", 6), ("ngB", 2), ("mB", 16), ("mP", 2), ("ckm", 6),
-                    ("f1", 16), ("f2", 16), ("x1", 16), ("x2", 16), ("x3", 16), ("x4", 16), ("x5", 16), ("NBa", 16), ("NBd", 32), ("EB", 48), ("e24", 24), ("e12", 12), ("io", 1032), ("Rn", 768), ("dR", 768), ("tR", 768), ("yo", 256)): sb(name, n)
+                    ("dg", 792), ("dh", 792), ("Sc", 6), ("ge", 2), ("gd", 2), ("c01", 2), ("d2c", 2), ("gt", 2), ("ga", 2), ("mx", 3), ("x0", 1), ("Tf", 3), ("ckB", 6), ("ngB", 2), ("mB", 16), ("mP", 2), ("ckm", 6),
+                    ("EB", 48), ("e24", 24), ("e12", 12), ("io", 1032), ("Rn", 768), ("NR", 1024), ("yo", 256)): sb(name, n)
     for name, n in (("TS", 64), ("TT", 64), ("Rp", 256), ("dA", 256), ("tA", 256), ("iJ", 256), ("Rpi", 256), ("tI", 256), ("dB", 256), ("tB", 256), ("Rpn", 256), ("Rq", 768), ("d2", 768), ("t2", 768),
                     ("TC", 64), ("TD", 64), ("RO", 256), ("ROt", 256), ("RT", 256), ("RV", 256), ("RVt", 256)): sb(name, n, "bfloat16")
-    for name, n in (("T2u", 16), ("lA", 16), ("lB", 16), ("lM", 16), ("posU", 16), ("piU", 16), ("nbL", 48), ("nbU", 48), ("lG", 48), ("nU", 32), ("n2U", 8), ("LV", 16), ("CLd", 16)): sb(name, n, "uint16")
+    for name, n in (("T2u", 16), ("lA", 16), ("lB", 16), ("lM", 16), ("posU", 16), ("piU", 16), ("nbL", 48), ("nbU", 48), ("lG", 48), ("lN", 48), ("nU", 32), ("n2U", 8), ("LV", 16), ("CLd", 16)): sb(name, n, "uint16")
     for i in range(8): b["ps%d" % i] = ("psum", [128, 512], "float32")
     return b
 
@@ -193,16 +194,19 @@ def rank_program(g, core, T, topo):
 
     iota(W("pI"), [[0, 1]], 0, 1)
     iota(W("o48"), [[0, 16], [1, 3]], 0, 0)
+    iota(W("pF"), [[0, 1]], 0, 1)
     iota(W("mF"), [[1, 256]], 0, 0)
     iota(W("yI"), [[256, 16], [11, 16]], 10, 0)
-    iota(W("pF"), [[0, 1]], 0, 1)
     iota(W("c8"), [[0, 6], [1, 8]], 0, 0)
-    ms(W("hE"), 0.0)
-    for q in range(4):
+    for q in (3, 0, 1, 2):
         c, r = q ^ rank ^ 1, ("Fw", 256 * q, 256 * q + 256)
-        if q < rank: plus(r, W("mF"), 1048576.0 * c, 4096.0)
-        else: ms(r, 1048576.0 * c)
+        if q == 3: ms(r, 1048576.0 * c)
+        elif q < rank: plus(r, W("mF"), 1048576.0 * c, 4096.0)
+        else: plus(r, W("mF"), 1048576.0 * c, 0.0)
     cp(W("iJ"), W("mF"), "s")
+    for q in range(4): plus(("io", 256 * q, 256 * q + 256), W("mF"), 256.0 * q)
+    plus(("io", 1024, 1032), ("mF", 0, 8), 1024.0)
+    plus(("NR", 0, 256), W("mF"), -1.0, 0.0)
 
     def kappa(v, vi, ai, h, s, out):
         return [D(cp, vi, v), D(ts, h, v, 128.0, A.is_ge, 96.0, A.mult), D(ts, ai, vi, 96, A.bitwise_and), D(tt, s, v, ai, A.add), D(tt, out, s, h, A.subtract)]
@@ -224,9 +228,9 @@ def rank_program(g, core, T, topo):
         rsum(("nK", h, h + 1), ("dk", 128 * h, 128 * h + 128), negate=True)
         jk, b, o = ("jk", 256 * h, 256 * h + 256), ("nK", h, h + 1), ("sg", h, h + 1)
         run("s", lambda e: e.activation(ap(jk), ap(W("RK")), AF.Sign, bias=ap(b), accum_out=ap(o)), [W("RK"), b], [jk, o])
+    ms(W("hE"), 0.0)
     run("s", lambda e: e.activation(ap(("hE", 3, 515, 4)), ap(W("I")), AF.Copy, scale=0.5), [W("I")], [("hE", 3, 515, 4)])
-    for q in range(4): plus(("io", 256 * q, 256 * q + 256), W("mF"), 256.0 * q - 1.0)
-    plus(("io", 1024, 1032), ("mF", 0, 8), 1023.0)
+    gather(W("Rn"), W("io"), W("nbU"), "s")
     ts(W("nbI"), W("nbT"), 255, A.bitwise_and)
     quant(("X", 0, 256), W("xb"))
     cp(W("nbL"), W("nbI"))
@@ -242,7 +246,6 @@ def rank_program(g, core, T, topo):
     ts(W("lM"), ("kap", 0, 16), W("rho"), A.add)
     ts(W("lB"), ("c0", 16, 32), W("rF"), A.add)
     tt(W("kP0"), W("pI"), W("aP"), A.add)
-    gather(W("Rn"), W("io"), W("nbU"), "s")
     gather(W("dA"), W("Rp"), W("lA"))
     ts(("mk0", 0, 1), W("kP0"), -256.0, A.add)
     tp(W("tA"), W("dA"))
@@ -259,19 +262,22 @@ def rank_program(g, core, T, topo):
     within(("MS", 1, 2), ("MS", 1, 2), -1, 79)
     gather(W("Rpn"), W("Rp"), W("lM"), "s")
     gather(W("Rq"), W("Rpn"), W("nbL"), "s")
-    ts(("lQ", 48, 64), ("kap", 0, 16), W("rF"), A.add)
     tp(W("tI"), W("Rpi"))
     gather(W("dB"), W("Rpi"), W("lB"), "s")
-    ts(W("Tn"), ("mF", 0, 256, 16), W("rF"), A.add)
-    def where(k, q):
+    def where(k):
         for i in range(2): ts(("lG", 16 * k + i, 16 * k + 16, 2), ("tI", 0, 256, 32), 3.0, A.mult, float(k), A.add)
-        gather(("d2", 256 * k, 256 * k + 256), W("Rq"), ("lG", 16 * k, 16 * k + 16), q)
-    where(1, "s")
-    where(0, "v")
+    def find(k): gather(("d2", 256 * k, 256 * k + 256), W("Rq"), ("lG", 16 * k, 16 * k + 16), "s")
+    def turn(k):
+        tp(("t2", 256 * k, 256 * k + 256), ("d2", 256 * k, 256 * k + 256))
+        cp(("nU", 16 * k, 16 * k + 16), ("t2", 256 * k, 256 * k + 256, 16))
+    where(0)
+    find(0)
+    where(1)
+    quant(("wq", 0, 128), W("wb"))
     tp(W("tB"), W("dB"))
-    tp(("t2", 0, 256), ("d2", 0, 256))
+    ts(("lQ", 48, 64), ("kap", 0, 16), W("rF"), A.add)
     cp(W("piU"), ("tB", 0, 256, 16))
-    cp(("nU", 0, 16), ("t2", 0, 256, 16))
+    ts(W("Tn"), ("mF", 0, 256, 16), W("rF"), A.add)
     pick(("W0", 0, 256), ("X", 0, 256), W("piU"))
 
     def exchange(t):
@@ -290,12 +296,13 @@ def rank_program(g, core, T, topo):
         mov = ("N%d" % t, 256 * k + 128 * h, 256 * k + 128 * h + 128) if k < 2 else ("M%d" % t, 128 * h, 128 * h + 128)
         mm(bank, 128, ("W%d" % t, 128 * h, 128 * h + 128), mov)
 
-    def score(k, h, bank, q):
+    def mask(k, h, bank): tt(("dg", 132 * (2 * k + h), 132 * (2 * k + h) + 128), ("ps%d" % bank, 0, 128), W("I"), A.mult)
+
+    def total(k, h, q):
         i = 2 * k + h
         d, s, j = ("dg", 132 * i, 132 * i + 129), ("Sc", i, i + 1), ("dh", 132 * i, 132 * i + 129)
-        tt(("dg", 132 * i, 132 * i + 128), ("ps%d" % bank, 0, 128), W("I"), A.mult)
         if q == "s": run("s", lambda e: e.activation(ap(j), ap(d), AF.Copy, accum_out=ap(s)), [d], [j, s])
-        else: return D(rsum, s, d)
+        else: rsum(s, d)
 
     def halves(t, parts):
         for b in parts: mm(BANKS[0][b], 256, ("E", 128 * b, 128 * b + 128), ("W%d" % t, 0, 256), True, b in VPARTS)
@@ -303,117 +310,114 @@ def rank_program(g, core, T, topo):
     def keep():
         for b in VPARTS: cp(("Ho", b, 1024, 4), ("ps%d" % BANKS[0][b], 0, 256), "s")
 
-    def unpack(t, k, parts=(0, 1, 2, 3)):
+    def unpack(t, k, b):
         mov = ("N%d" % t, 256 * k, 256 * k + 256) if k < 2 else ("M%d" % t, 0, 256)
-        for b in parts:
-            e, bank, alone = ("E", 128 * b, 128 * b + 128), BANKS[k][b], k != 1 and b in VPARTS
-            if k and not alone: mm(bank, 256, e, ("W%d" % t, 0, 256), True, False)
-            mm(bank, 256, e, mov, alone, True)
-
-    def cast(k, parts=(0, 1, 2, 3)):
-        for b in parts:
-            out, bank = ("h%d" % k, b, 1024, 4), ("ps%d" % BANKS[k][b], 0, 256)
-            if k != 1 and b in VPARTS: tt(out, bank, ("Ho", b, 1024, 4), A.add)
-            else: cp(out, bank, "s")
+        e, bank, alone = ("E", 128 * b, 128 * b + 128), BANKS[k][b], b in VPARTS
+        if k and not alone: mm(bank, 256, e, ("W%d" % t, 0, 256), True, False)
+        mm(bank, 256, e, mov, alone, True)
+        out, half = ("h%d" % k, b, 1024, 4), ("ps%d" % bank, 0, 256)
+        if alone: tt(out, half, ("Ho", b, 1024, 4), A.add)
+        else: cp(out, half, "s")
 
     def candidate(t, k): quant(("W%d" % t, 256 * (k + 1), 256 * (k + 2)), W("h%d" % k))
 
-    def local(t):
+    def lists(t):
+        tp(W("RT"), ("RC%d" % t, 0, 256))
+        for h in range(2):
+            for s in range(2): cp(("LV", 8 * h + s, 8 * h + 8, 2), ("RT", 32 * h, 256, 64))
+
+    def shadow(t, items):
+        for i in items:
+            if i[0] == "u": unpack(t, i[1], i[2])
+            elif i[0] == "q": candidate(t, i[1])
+            elif i[0] == "f": tt(W("gt"), ("Sc", 4, 6), ("m01_%d" % t, 0, 2), A.is_gt)
+            else: lists(t)
+
+    def local(t, extra=(), middle=()):
         halves(t, (0, 1))
-        for h in range(2): product(t, 0, h, h)
+        for k in range(2):
+            for h in range(2): product(t, k, h, 2 * k + h)
         halves(t, (2, 3))
-        for h in range(2): product(t, 1, h, 2 + h)
         keep()
-        for h in range(2): score(0, h, h, "s")
-        score(1, 0, 2, "s")
-        score(1, 1, 3, "v")()
+        c = list(extra)
+        for h in range(2):
+            mask(0, h, h)
+            for f in c[2 * h:2 * h + 2]: f()
+        mask(1, 0, 2)
+        for f in c[4:]: f()
+        for h in range(2): total(0, h, "s")
+        total(1, 0, "s")
+        mask(1, 1, 3)
+        if t: neighbours2(t)
+        total(1, 1, "v")
+        for f in middle: f()
         m, fl = "m01_%d" % t, "fl%d" % t
-        tt(W(m), ("Sc", 0, 2), ("Sc", 2, 4), A.max)
+        tt((m, 0, 2), ("Sc", 0, 2), ("Sc", 2, 4), A.max)
         def what(d):
             r = (m, FAR[d][0] // 128, FAR[d][0] // 128 + 1)
             return ap(r), ap((fl, d, d + 1)), r
         send(what, "xm%d" % t)
         arrives("xm%d" % t, incoming, [W(fl)])
-        unpack(t, 0)
-        cast(0)
-        unpack(t, 1, range(NB))
         tt(W("ge"), ("Sc", 0, 2), ("Sc", 2, 4), A.is_ge)
+        tt((m, 2, 3), ("Sc", 1, 2), ("Sc", 3, 4), A.max)
 
     def prefer():
         return [D(tt, W("gd"), W("ge"), W("dN"), A.mult), D(tt, W("c01"), W("gd"), ("NP", 2, 4), A.add), D(tt, W("d2c"), ("NP", 4, 6), W("c01"), A.subtract)]
 
     def choose(t):
-        fl = "fl%d" % t
+        fl, m = "fl%d" % t, "m01_%d" % t
+        shadow(t, AHEAD)
         for h in range(2): product(t, 2, h, h)
-        cast(1, range(NB))
-        for f in [score(2, h, h, "v") for h in range(2)]: f()
-        ms(("RC%d" % t, 256, 272), -1.0)
-        tt(W("gt"), ("Sc", 4, 6), W("m01_%d" % t), A.is_gt)
-        ms(W("D0_%d" % t), 0.0)
-        tt(W("ga"), W("gt"), W("d2c"), A.mult)
-        ts(("Qf", 0, 1), ("MS", 0, 1), ("gt", 0, 1), A.mult)
-        ts(("Qf", 1, 3), ("MS", 1, 3), ("gt", 1, 2), A.mult)
-        tt(W("A2"), W("ga"), W("c01"), A.add)
-        ts(("Tf", 2, 3), (fl, 2, 3), ("Sc", 5, 6), A.is_lt, ("Qf", 2, 3), A.mult)
-        ts(("Tf", 1, 2), (fl, 3, 4), ("Sc", 5, 6), A.is_lt, ("Qf", 1, 2), A.mult)
-        ts(("Tf", 0, 1), (fl, 1, 2), ("Sc", 4, 5), A.is_lt, ("Qf", 0, 1), A.mult)
-        tt(W("A3"), ("Tf", 2, 3), ("A2", 1, 2), A.add)
-        tt(("TC", 0, 1), ("Tf", 0, 1), ("A2", 0, 1), A.add)
-        tt(("TC", 32, 33), ("Tf", 1, 2), W("A3"), A.add)
+        ready(t)
+        for h in range(2): mask(2, h, h)
+        for h in range(2): total(2, h, "v")
+        tt(W("mx"), (fl, 1, 4), W(m), A.max)
+        def above(out, x, h, then): ts(out, x, ("Sc", 4 + h, 5 + h), A.is_lt, then, A.mult)
+        for h in range(2): above(("ga", h, h + 1), (m, h, h + 1), h, ("d2c", h, h + 1))
+        above(("Tf", 1, 2), ("mx", 2, 3), 1, ("MS", 1, 2))
+        above(("Tf", 0, 1), ("mx", 0, 1), 0, ("MS", 0, 1))
+        above(("Tf", 2, 3), ("mx", 1, 2), 1, ("MS", 2, 3))
+        ts(W("x0"), ("c01", 1, 2), ("ga", 1, 2), A.add, ("Tf", 1, 2), A.add)
+        ts(("TC", 0, 1), ("c01", 0, 1), ("ga", 0, 1), A.add, ("Tf", 0, 1), A.add)
+        tt(("TC", 32, 33), W("x0"), ("Tf", 2, 3), A.add)
         tp(W("TD"), W("TC"))
         spread("RC%d" % t, "TD")
-        unpack(t, 1, range(NB, 4))
-        cast(1, range(NB, 4))
-        unpack(t, 2)
-        cast(2)
-        for k in range(3): candidate(t, k)
+        shadow(t, BESIDE)
+
+    def ready(t):
+        for i, c in enumerate((0.0, 0.5, 512.0)): plus(("S0_%d" % t, i, 64, 4), ("mF", 0, 16), c, 0.0)
+        plus(("S1_%d" % t, 2, 64, 4), ("mF", 0, 16), 256.0, 0.0)
+        cp(("S1_%d" % t, 3, 64, 4), W("Tn"), "s")
+        plus(("RC%d" % t, 256, 272), ("mF", 0, 16), -1.0, 0.0)
 
     def decide(t):
-        rc, d0, d1, ls, e1, e2 = ["%s%d" % (n, t) for n in ("RC", "D0_", "D1_", "Ls", "e1_", "e2_")]
+        rc, d0, d1, ls = ["%s%d" % (n, t) for n in ("RC", "S0_", "S1_", "Ls")]
         gather(W("RO"), (rc, 0, 256), W("CLd"), "s")
-        tp(W("RT"), (rc, 0, 256))
-        for h in range(2):
-            for s in range(2): cp(("LV", 8 * h + s, 8 * h + 8, 2), ("RT", 32 * h, 256, 64))
         gather(W("RV"), (rc, 0, 272), W("LV"), "s")
+        shadow(t, AFTER)
         if t < R - 1: numbers(t)
         else:
             rows(1, "s")
             store(1)
         tp(W("ROt"), W("RO"))
-        cp((d1, 1, 32, 2), W("Tn"))
         v = ("ROt", 0, 256, 16)
-        tt(W(e1), v, ("lQ", 16, 32), A.is_equal)
-        tt(W(e2), v, ("lQ", 32, 48), A.is_equal)
-        ts(W("f1"), W(e1), 256.0, A.mult, 256.0, A.add)
-        ts(W("f2"), W(e2), 512.0, A.mult)
-        if t < R - 1: ts(("ckB", 4, 6), W("gt"), -BIG, A.mult)
-        tt((d1, 0, 32, 2), W("f1"), W("f2"), A.add)
-        if t < R - 1:
-            ts(W("ngB"), W("gt"), BIG, A.mult, -BIG, A.add)
-            tt(("ckB", 0, 2), W("ngB"), W("ge"), A.mult)
-            tt(("ckB", 2, 4), W("ngB"), ("ckB", 0, 2), A.subtract)
-        else:
-            for f in partner(t): f()
+        tt((d1, 0, 64, 4), v, ("lQ", 16, 32), A.is_equal)
+        tt((d1, 1, 64, 4), v, ("lQ", 32, 48), A.is_equal)
         tp(W("RVt"), W("RV"))
-        tt((d0, 1, 32, 2), ("RVt", 0, 256, 16), ("lQ", 48, 64), A.is_equal)
+        tt((d0, 3, 64, 4), ("RVt", 0, 256, 16), ("lQ", 48, 64), A.is_equal)
         run("v", lambda e: e.tensor_tensor_scan(ap(W(ls)), ap(W(d0)), ap(W(d1)), 0.0, A.mult, A.add), [W(d0), W(d1)], [W(ls)])
-        cp(W("U%d" % t), (ls, 1, 32, 2))
+        cp(W("U%d" % t), (ls, 3, 64, 4))
 
     def caps(t):
         cl = ("dg", 128, 792, 132)
-        return [D(tt, W("mB"), ("D0_%d" % t, 1, 32, 2), ("Bm", 0, 16), A.mult)] + [D(rsum, ("mP", h, h + 1), ("mB", 8 * h, 8 * h + 8)) for h in range(2)] \
+        return [D(ts, W("ngB"), W("gt"), BIG, A.mult, -BIG, A.add), D(ts, ("ckB", 4, 6), W("gt"), -BIG, A.mult), D(tt, W("mB"), ("S0_%d" % t, 3, 64, 4), ("Bm", 0, 16), A.mult), D(tt, ("ckB", 0, 2), W("ngB"), W("ge"), A.mult)] \
+            + [D(rsum, ("mP", h, h + 1), ("mB", 8 * h, 8 * h + 8)) for h in range(2)] + [D(tt, ("ckB", 2, 4), W("ngB"), ("ckB", 0, 2), A.subtract)] \
             + [D(ts, ("ckm", h, 6, 2), ("ckB", h, 6, 2), ("mP", h, h + 1), A.mult) for h in range(2)] + [D(tt, cl, cl, W("ckm"), A.add)]
 
-    def numbers(k): gather(("dR", 256 * k, 256 * k + 256), W("Rn"), ("lG", 16 * k, 16 * k + 16), "s")
-
-    def partner(t):
-        return [D(tt, W("x1"), W("e1_%d" % t), ("NBd", 0, 16), A.mult), D(tt, W("x2"), W("e2_%d" % t), ("NBd", 16, 32), A.mult), D(tt, W("x3"), W("x1"), W("NBa"), A.add), D(tt, W("x4"), W("x2"), W("x3"), A.add)]
-
-    def listed(t):
-        return [D(tt, W("x5"), ("D0_%d" % t, 1, 32, 2), W("x4"), A.mult), D(cp, W("V%d" % t), W("x5"))]
+    def numbers(k): gather(("NR", 256 * k + 256, 256 * k + 512), W("Rn"), ("lN", 16 * k, 16 * k + 16), "s")
 
     def rows(t, q):
-        gather(W("PRp%d" % t), W("io"), W("V%d" % t), q)
+        gather(W("PRp%d" % t), W("NR"), W("U%d" % t), q)
         gather(W("PRn%d" % t), W("PRp%d" % t), W("posU"), q)
 
     def store(t):
@@ -421,21 +425,19 @@ def rank_program(g, core, T, topo):
         g.sync.dma_start(T.pr[t:t + 1, :], ap(W("PRn%d" % t), (0, 1))).then_inc(T.sem.st, 16)
 
     exchange(0)
+    find(1)
+    turn(0)
     neighbours(0, 0)
-    tp(("t2", 256, 512), ("d2", 256, 512))
-    ts(("dg", 128, 792, 132), ("mF", 0, 6), 0.0, A.mult)
-    cp(("nU", 16, 32), ("t2", 256, 512, 16))
+    turn(1)
     neighbours(0, 1)
-    for i in range(2): ts(("lG", 32 + i, 48, 2), ("tI", 0, 256, 32), 3.0, A.mult, 2.0, A.add)
-    local(0)
-    gather(("d2", 512, 768), W("Rq"), ("lG", 32, 48), "s")
-    cp(("lP", 0, 32), ("t2", 0, 512, 16))
-    cp(W("gG"), W("gI"))
-    for a, b in ((0, LOC[0] // 16), (LOC[1] // 16, 16)): cp(("lP", 32 + a, 32 + b), ("Tn", a, b))
+    where(2)
+    find(2)
+    ts(("dg", 128, 792, 132), ("mF", 0, 6), 0.0, A.mult)
+    for k in range(3): ts(("lN", 16 * k, 16 * k + 16), ("tB", 0, 256, 16), 3.0, A.mult, float(k), A.add)
+    l0, l1 = LOC[0] // 16, LOC[1] // 16
+    local(0, (), [D(tp, ("t2", 512, 768), ("d2", 512, 768)), D(cp, ("lP", 0, 32), ("t2", 0, 512, 16)), D(cp, W("gG"), W("gI")), D(cp, ("n2U", 0, 7), ("t2", 512 + LOC[0], 512 + LOC[1], 16)),
+        D(cp, ("lP", 32 + l0, 32 + l1), ("t2", 512 + LOC[0], 512 + LOC[1], 16)), D(cp, ("lP", 32, 32 + l0), ("Tn", 0, l0)), D(cp, ("lP", 32 + l1, 48), ("Tn", l1, 16))])
     ts(W("Bm"), W("c8"), W("gG"), A.is_equal)
-    tp(("t2", 512, 768), ("d2", 512, 768))
-    cp(("n2U", 0, 7), ("t2", 512 + LOC[0], 512 + LOC[1], 16))
-    cp(("lP", 32 + LOC[0] // 16, 32 + LOC[1] // 16), ("t2", 512 + LOC[0], 512 + LOC[1], 16))
     weave(kappa(W("lP"), W("vI"), W("aI"), W("hP"), W("kP"), ("lQ", 0, 48)), [D(neighbours2, 0)])
     tt(W("EB"), ("lQ", 0, 48), W("Bm"), A.mult)
     tt(W("e24"), ("EB", 0, 48, 2), ("EB", 1, 48, 2), A.add)
@@ -454,25 +456,17 @@ def rank_program(g, core, T, topo):
         pick(("W%d" % u, 0, 256), ("W%d" % t, 0, 1024), W("U%d" % t))
         exchange(u)
         cl = caps(t)
-        weave([D(neighbours, u, 0), D(neighbours, u, 1)], cl[:1])
-        for f in cl[1:]: f()
-        local(u)
-        weave(prefer(), [D(neighbours2, u)])
+        for f in [D(neighbours, u, 0)] + cl[:3] + [D(neighbours, u, 1)] + cl[3:5]: f()
+        local(u, cl[5:])
+        for f in prefer(): f()
         if u == 1: numbers(2)
         else:
-            quant(("wq", 0, 128), W("wb"))
-            for k in range(3): tp(("tR", 256 * k, 256 * k + 256), ("dR", 256 * k, 256 * k + 256))
-            ts(W("NBa"), ("tR", 0, 256, 16), 2.0, A.add)
-            for k in (1, 2): tt(("NBd", 16 * k - 16, 16 * k), ("tR", 256 * k, 256 * k + 256, 16), ("tR", 0, 256, 16), A.subtract)
-            for i in range(2):
-                for f in partner(i) + listed(i): f()
             rows(0, "s")
             store(0)
         choose(u)
 
     t = R - 1
     pick(("H", 0, 256), ("W%d" % t, 0, 1024), W("U%d" % t))
-    for f in listed(t): f()
     pick(("Z", 0, 256), ("H", 0, 256), W("posU"))
     rows(t, "v")
     need("y", [("Zc", 0, 256)], [])

@@ -9,7 +9,7 @@ BANKS = ((4, 5, 6, 7), (4, 5, 6, 7), (2, 3, 0, 1))
 VPARTS = (0, 1)
 AHEAD = (("u", 0, 0), ("u", 0, 1), ("u", 0, 2), ("u", 0, 3))
 BESIDE = (("q", 0), ("u", 2, 0), ("u", 2, 1), ("u", 1, 0), ("u", 1, 1), ("u", 1, 2), ("u", 1, 3), ("q", 1), ("l",), ("u", 2, 2), ("u", 2, 3))
-AFTER = (("f",), ("q", 2))
+AFTER = (("q", 2),)
 
 
 def _bufs():
@@ -22,18 +22,18 @@ def _bufs():
     mx("X", 256); mx("wq", 128); mx("E", 512); mx("H", 256); mx("Z", 256)
     for t in range(R):
         mx("W%d" % t, 1024); mx("N%d" % t, 512); mx("M%d" % t, 256)
-        sb("fl%d" % t, 4); sb("m01_%d" % t, 3); sb("RC%d" % t, 272, "bfloat16"); sb("U%d" % t, 16, "uint16")
+        sb("fl%d" % t, 4); sb("m01_%d" % t, 2); sb("RC%d" % t, 272, "bfloat16"); sb("U%d" % t, 16, "uint16")
         for name in ("S0_", "S1_", "Ls"): sb("%s%d" % (name, t), 64)
         sb("PRp%d" % t, 256); sb("PRn%d" % t, 256)
     for k in range(3): sb("h%d" % k, 1024, "bfloat16")
     sb("hE", 516, "bfloat16"); sb("Ho", 1024, "bfloat16")
     for name, n in (("pI", 1), ("rI", 1), ("gI", 1), ("uI", 1), ("aP", 1), ("yI", 256), ("wI", 256), ("rhoI", 1), ("zI", 48),
-                    ("vI", 48), ("aI", 48), ("nbI", 48), ("kI", 32), ("kA", 32)): sb(name, n, "int32")
+                    ("lP", 48), ("aI", 48), ("nbI", 48), ("kI", 32), ("kA", 32)): sb(name, n, "int32")
     for name, n in (("pF", 1), ("I", 128), ("mF", 256), ("rF", 1), ("g16", 1), ("gG", 1), ("rho", 1), ("o48", 48), ("z48", 48), ("z3", 48), ("M48", 48),
                     ("Fw", 1024), ("mk", 48), ("t2a", 16), ("T2", 16), ("RK", 256), ("dk", 256), ("nK", 2), ("sg", 2), ("jk", 512), ("Tn", 16), ("c0", 32),
-                    ("kh", 32), ("k1", 32), ("kap", 32), ("hP", 48), ("kP", 48), ("lP", 48), ("lQ", 64), ("kP0", 1), ("mk0", 2), ("MS", 3), ("NP", 6), ("dN", 2), ("Bm", 48), ("c8", 48),
-                    ("dg", 792), ("dh", 792), ("Sc", 6), ("ge", 2), ("gd", 2), ("c01", 2), ("d2c", 2), ("gt", 2), ("ga", 2), ("mx", 3), ("x0", 1), ("Tf", 3), ("ckB", 6), ("ngB", 2), ("mB", 16), ("mP", 2), ("ckm", 6),
-                    ("EB", 48), ("e24", 24), ("e12", 12), ("io", 1032), ("Rn", 768), ("NR", 1024), ("yo", 256)): sb(name, n)
+                    ("kh", 32), ("k1", 32), ("kap", 32), ("hP", 48), ("kP", 48), ("lQ", 64), ("kP0", 1), ("mk0", 2), ("MS", 3), ("NP", 6), ("dN", 2), ("Bm", 48), ("c8", 48),
+                    ("dg", 792), ("dh", 792), ("Sc", 6), ("ge", 2), ("c01", 2), ("d2c", 2), ("gt", 2), ("ga", 2), ("A2", 2), ("Qf", 3), ("Tf", 3), ("ckB", 6), ("ngB", 2), ("mB", 16), ("mP", 2), ("ckm", 6),
+                    ("EB", 48), ("io", 1032), ("Rn", 768), ("NR", 1024), ("yo", 256)): sb(name, n)
     for name, n in (("TS", 64), ("TT", 64), ("Rp", 256), ("dA", 256), ("tA", 256), ("iJ", 256), ("Rpi", 256), ("tI", 256), ("dB", 256), ("tB", 256), ("Rpn", 256), ("Rq", 768), ("d2", 768), ("t2", 768),
                     ("TC", 64), ("TD", 64), ("RO", 256), ("ROt", 256), ("RT", 256), ("RV", 256), ("RVt", 256)): sb(name, n, "bfloat16")
     for name, n in (("T2u", 16), ("lA", 16), ("lB", 16), ("lM", 16), ("posU", 16), ("piU", 16), ("nbL", 48), ("nbU", 48), ("lG", 48), ("lN", 48), ("nU", 32), ("n2U", 8), ("LV", 16), ("CLd", 16)): sb(name, n, "uint16")
@@ -136,17 +136,20 @@ def rank_program(g, core, T, topo):
     def cp(out, in_, q="v"):
         if q == "v": run("v", lambda e: e.tensor_copy(ap(out), ap(in_)), [in_], [out])
         else: run("s", lambda e: e.activation(ap(out), ap(in_), AF.Copy), [in_], [out])
-    def plus(out, in_, bias, scale=1.0): run("s", lambda e: e.activation(ap(out), ap(in_), AF.Identity, bias=bias, scale=scale), [in_], [out])
+    def plus(out, in_, bias, scale=1.0):
+        rd = [in_] + [x for x in (bias, scale) if isinstance(x, tuple)]
+        run("s", lambda e: e.activation(ap(out), ap(in_), AF.Identity, bias=sc(bias), scale=sc(scale)), rd, [out])
+    def times(out, in_, col): run("s", lambda e: e.activation(ap(out), ap(in_), AF.Copy, scale=ap(col)), [in_, col], [out])
     def ms(out, c): run("v", lambda e: e.memset(ap(out), c), [], [out])
     def rsum(out, in_, negate=False): run("v", lambda e: e.tensor_reduce(ap(out), ap(in_), AxisListType.X, A.add, negate=negate), [in_], [out])
     def tp(out, in_): run("v", lambda e: e.transpose(ap(out), ap(in_)), [in_], [out])
     def gather(out, win, off, q="v"):
         if q == "v": run("v", lambda e: e.tensor_copy(ap(out), ap(win).indirect(ap(off))), [win, off], [out])
         else: run("s", lambda e: e.activation(ap(out), ap(win).indirect(ap(off)), AF.Copy), [win, off], [out])
-    def pick(out, win, off):
+    def pick(out, win, off, what="cs"):
         oc, wc, os_, ws = [(r[0] + x, r[1], r[2]) for x in "cs" for r in (out, win)]
-        run("v", lambda e: e.tensor_copy(words(oc), words(wc).indirect(ap(off))), [wc, off], [oc])
-        run("s", lambda e: e.activation(ap(os_), ap(ws).indirect(ap(off)), AF.Copy), [ws, off], [os_])
+        if "c" in what: run("v", lambda e: e.tensor_copy(words(oc), words(wc).indirect(ap(off))), [wc, off], [oc])
+        if "s" in what: run("s", lambda e: e.activation(ap(os_), ap(ws).indirect(ap(off)), AF.Copy), [ws, off], [os_])
     def quant(out, in_):
         c, s = (out[0] + "c", out[1], out[2]), (out[0] + "s", out[1], out[2])
         run("v", lambda e: e.quantize_mx(ap(c), ap(s), ap(in_)), [in_], [c, s])
@@ -208,8 +211,8 @@ def rank_program(g, core, T, topo):
     plus(("io", 1024, 1032), ("mF", 0, 8), 1024.0)
     plus(("NR", 0, 256), W("mF"), -1.0, 0.0)
 
-    def kappa(v, vi, ai, h, s, out):
-        return [D(cp, vi, v), D(ts, h, v, 128.0, A.is_ge, 96.0, A.mult), D(ts, ai, vi, 96, A.bitwise_and), D(tt, s, v, ai, A.add), D(tt, out, s, h, A.subtract)]
+    def kappa(v, ai, h, s, out):
+        return [D(ts, h, v, 128.0, A.is_ge, 96.0, A.mult), D(ts, ai, v, 96, A.bitwise_and), D(tt, s, v, ai, A.add), D(tt, out, s, h, A.subtract)]
 
     ts(W("rI"), W("pI"), 15, A.bitwise_and)
     ts(W("gI"), W("pI"), 4, A.logical_shift_right)
@@ -239,7 +242,7 @@ def rank_program(g, core, T, topo):
     spread("Rp", "TT")
     cp(("c0", 0, 16), ("mF", 0, 256, 16))
     for i in range(2): ts(("c0", 16 + i, 32, 2), ("mF", 0, 256, 32), W("g16"), A.add)
-    weave(kappa(W("c0"), W("kI"), W("kA"), W("kh"), W("k1"), W("kap")),
+    weave([D(cp, W("kI"), W("c0"))] + kappa(W("kI"), W("kA"), W("kh"), W("k1"), W("kap")),
           [D(quant, ("E", 128 * b, 128 * b + 128), ("hE", 3 - b, 515 - b)) for b in range(4)])
     ts(W("aP"), W("pI"), 96, A.bitwise_and)
     ts(W("lA"), ("kap", 16, 32), W("rho"), A.add)
@@ -290,7 +293,7 @@ def rank_program(g, core, T, topo):
 
     def neighbours(t, k): pick(("N%d" % t, 256 * k, 256 * k + 256), ("W%d" % t, 0, 256), ("nU", 16 * k, 16 * k + 16))
 
-    def neighbours2(t): pick(("M%d" % t,) + LOC, ("W%d" % t, 0, 256), ("n2U", 0, 7))
+    def neighbours2(t, what="cs"): pick(("M%d" % t,) + LOC, ("W%d" % t, 0, 256), ("n2U", 0, 7), what)
 
     def product(t, k, h, bank):
         mov = ("N%d" % t, 256 * k + 128 * h, 256 * k + 128 * h + 128) if k < 2 else ("M%d" % t, 128 * h, 128 * h + 128)
@@ -330,56 +333,59 @@ def rank_program(g, core, T, topo):
         for i in items:
             if i[0] == "u": unpack(t, i[1], i[2])
             elif i[0] == "q": candidate(t, i[1])
-            elif i[0] == "f": tt(W("gt"), ("Sc", 4, 6), ("m01_%d" % t, 0, 2), A.is_gt)
             else: lists(t)
 
-    def local(t, extra=(), middle=()):
+    def local(t, middle=()):
         halves(t, (0, 1))
         for k in range(2):
             for h in range(2): product(t, k, h, 2 * k + h)
         halves(t, (2, 3))
         keep()
-        c = list(extra)
-        for h in range(2):
-            mask(0, h, h)
-            for f in c[2 * h:2 * h + 2]: f()
-        mask(1, 0, 2)
-        for f in c[4:]: f()
+        for h in range(2): mask(0, h, h)
+        if t:
+            cl = ("dg", 128, 792, 132)
+            tt(cl, cl, W("ckm"), A.add)
+            neighbours2(t, "c")
         for h in range(2): total(0, h, "s")
+        mask(1, 0, 2)
         total(1, 0, "s")
         mask(1, 1, 3)
-        if t: neighbours2(t)
+        if t: neighbours2(t, "s")
         total(1, 1, "v")
         for f in middle: f()
         m, fl = "m01_%d" % t, "fl%d" % t
-        tt((m, 0, 2), ("Sc", 0, 2), ("Sc", 2, 4), A.max)
+        tt(W(m), ("Sc", 0, 2), ("Sc", 2, 4), A.max)
         def what(d):
             r = (m, FAR[d][0] // 128, FAR[d][0] // 128 + 1)
             return ap(r), ap((fl, d, d + 1)), r
         send(what, "xm%d" % t)
         arrives("xm%d" % t, incoming, [W(fl)])
         tt(W("ge"), ("Sc", 0, 2), ("Sc", 2, 4), A.is_ge)
-        tt((m, 2, 3), ("Sc", 1, 2), ("Sc", 3, 4), A.max)
 
     def prefer():
-        return [D(tt, W("gd"), W("ge"), W("dN"), A.mult), D(tt, W("c01"), W("gd"), ("NP", 2, 4), A.add), D(tt, W("d2c"), ("NP", 4, 6), W("c01"), A.subtract)]
+        for h in range(2): plus(("c01", h, h + 1), ("ge", h, h + 1), ("NP", 2 + h, 3 + h), ("dN", h, h + 1))
+        for h in range(2): plus(("d2c", h, h + 1), ("c01", h, h + 1), ("NP", 4 + h, 5 + h), -1.0)
 
     def choose(t):
         fl, m = "fl%d" % t, "m01_%d" % t
-        shadow(t, AHEAD)
+        if t:
+            prefer()
+            shadow(t, AHEAD)
         for h in range(2): product(t, 2, h, h)
         ready(t)
+        if t == 0:
+            for k in range(3): numbers(k)
+            prefer()
         for h in range(2): mask(2, h, h)
         for h in range(2): total(2, h, "v")
-        tt(W("mx"), (fl, 1, 4), W(m), A.max)
-        def above(out, x, h, then): ts(out, x, ("Sc", 4 + h, 5 + h), A.is_lt, then, A.mult)
-        for h in range(2): above(("ga", h, h + 1), (m, h, h + 1), h, ("d2c", h, h + 1))
-        above(("Tf", 1, 2), ("mx", 2, 3), 1, ("MS", 1, 2))
-        above(("Tf", 0, 1), ("mx", 0, 1), 0, ("MS", 0, 1))
-        above(("Tf", 2, 3), ("mx", 1, 2), 1, ("MS", 2, 3))
-        ts(W("x0"), ("c01", 1, 2), ("ga", 1, 2), A.add, ("Tf", 1, 2), A.add)
-        ts(("TC", 0, 1), ("c01", 0, 1), ("ga", 0, 1), A.add, ("Tf", 0, 1), A.add)
-        tt(("TC", 32, 33), W("x0"), ("Tf", 2, 3), A.add)
+        tt(W("gt"), ("Sc", 4, 6), W(m), A.is_gt)
+        tt(W("ga"), W("gt"), W("d2c"), A.mult)
+        ts(("Qf", 1, 3), ("MS", 1, 3), ("gt", 1, 2), A.mult)
+        ts(("Qf", 0, 1), ("MS", 0, 1), ("gt", 0, 1), A.mult)
+        tt(W("A2"), W("ga"), W("c01"), A.add)
+        for i, d, h in ((1, 3, 1), (2, 2, 1), (0, 1, 0)): ts(("Tf", i, i + 1), (fl, d, d + 1), ("Sc", 4 + h, 5 + h), A.is_lt, ("Qf", i, i + 1), A.mult)
+        ts(("TC", 32, 33), ("A2", 1, 2), ("Tf", 1, 2), A.add, ("Tf", 2, 3), A.add)
+        tt(("TC", 0, 1), ("A2", 0, 1), ("Tf", 0, 1), A.add)
         tp(W("TD"), W("TC"))
         spread("RC%d" % t, "TD")
         shadow(t, BESIDE)
@@ -395,7 +401,7 @@ def rank_program(g, core, T, topo):
         gather(W("RO"), (rc, 0, 256), W("CLd"), "s")
         gather(W("RV"), (rc, 0, 272), W("LV"), "s")
         shadow(t, AFTER)
-        if t < R - 1: numbers(t)
+        if t < R - 1: bars()
         else:
             rows(1, "s")
             store(1)
@@ -407,12 +413,16 @@ def rank_program(g, core, T, topo):
         tt((d0, 3, 64, 4), ("RVt", 0, 256, 16), ("lQ", 48, 64), A.is_equal)
         run("v", lambda e: e.tensor_tensor_scan(ap(W(ls)), ap(W(d0)), ap(W(d1)), 0.0, A.mult, A.add), [W(d0), W(d1)], [W(ls)])
         cp(W("U%d" % t), (ls, 3, 64, 4))
+        if t < R - 1: tt(W("mB"), (d0, 3, 64, 4), ("Bm", 0, 16), A.mult)
 
-    def caps(t):
-        cl = ("dg", 128, 792, 132)
-        return [D(ts, W("ngB"), W("gt"), BIG, A.mult, -BIG, A.add), D(ts, ("ckB", 4, 6), W("gt"), -BIG, A.mult), D(tt, W("mB"), ("S0_%d" % t, 3, 64, 4), ("Bm", 0, 16), A.mult), D(tt, ("ckB", 0, 2), W("ngB"), W("ge"), A.mult)] \
-            + [D(rsum, ("mP", h, h + 1), ("mB", 8 * h, 8 * h + 8)) for h in range(2)] + [D(tt, ("ckB", 2, 4), W("ngB"), ("ckB", 0, 2), A.subtract)] \
-            + [D(ts, ("ckm", h, 6, 2), ("ckB", h, 6, 2), ("mP", h, h + 1), A.mult) for h in range(2)] + [D(tt, cl, cl, W("ckm"), A.add)]
+    def bars():
+        plus(("ckB", 4, 6), W("gt"), 0.0, -BIG)
+        plus(W("ngB"), W("gt"), -BIG, BIG)
+        for h in range(2): times(("ckB", h, h + 1), ("ge", h, h + 1), ("ngB", h, h + 1))
+        for h in range(2): plus(("ckB", 2 + h, 3 + h), ("ckB", h, h + 1), ("ngB", h, h + 1), -1.0)
+
+    def caps():
+        for h in range(2): times(("ckm", h, 6, 2), ("ckB", h, 6, 2), ("mP", h, h + 1))
 
     def numbers(k): gather(("NR", 256 * k + 256, 256 * k + 512), W("Rn"), ("lN", 16 * k, 16 * k + 16), "s")
 
@@ -435,18 +445,15 @@ def rank_program(g, core, T, topo):
     ts(("dg", 128, 792, 132), ("mF", 0, 6), 0.0, A.mult)
     for k in range(3): ts(("lN", 16 * k, 16 * k + 16), ("tB", 0, 256, 16), 3.0, A.mult, float(k), A.add)
     l0, l1 = LOC[0] // 16, LOC[1] // 16
-    local(0, (), [D(tp, ("t2", 512, 768), ("d2", 512, 768)), D(cp, ("lP", 0, 32), ("t2", 0, 512, 16)), D(cp, W("gG"), W("gI")), D(cp, ("n2U", 0, 7), ("t2", 512 + LOC[0], 512 + LOC[1], 16)),
+    local(0, [D(tp, ("t2", 512, 768), ("d2", 512, 768)), D(cp, ("lP", 0, 32), ("t2", 0, 512, 16)), D(cp, W("gG"), W("gI")), D(cp, ("n2U", 0, 7), ("t2", 512 + LOC[0], 512 + LOC[1], 16)),
         D(cp, ("lP", 32 + l0, 32 + l1), ("t2", 512 + LOC[0], 512 + LOC[1], 16)), D(cp, ("lP", 32, 32 + l0), ("Tn", 0, l0)), D(cp, ("lP", 32 + l1, 48), ("Tn", l1, 16))])
     ts(W("Bm"), W("c8"), W("gG"), A.is_equal)
-    weave(kappa(W("lP"), W("vI"), W("aI"), W("hP"), W("kP"), ("lQ", 0, 48)), [D(neighbours2, 0)])
+    weave(kappa(W("lP"), W("aI"), W("hP"), W("kP"), ("lQ", 0, 48)), [D(neighbours2, 0)] + [D(shadow, 0, (i,)) for i in AHEAD])
     tt(W("EB"), ("lQ", 0, 48), W("Bm"), A.mult)
-    tt(W("e24"), ("EB", 0, 48, 2), ("EB", 1, 48, 2), A.add)
-    tt(W("e12"), ("e24", 0, 24, 2), ("e24", 1, 24, 2), A.add)
-    tt(W("NP"), ("e12", 0, 12, 2), ("e12", 1, 12, 2), A.add)
-    tt(W("dN"), ("NP", 0, 2), ("NP", 2, 4), A.subtract)
+    for i in range(6): rsum(("NP", i, i + 1), ("EB", 8 * i, 8 * i + 8))
     tt(("NP", 4, 6), ("NP", 4, 6), ("MS", 0, 2), A.subtract)
-    weave(prefer()[:2], [D(tt, ("NP", 5, 6), ("NP", 5, 6), ("MS", 2, 3), A.subtract)])
-    prefer()[2]()
+    tt(W("dN"), ("NP", 0, 2), ("NP", 2, 4), A.subtract)
+    tt(("NP", 5, 6), ("NP", 5, 6), ("MS", 2, 3), A.subtract)
     choose(0)
 
     for t in range(R):
@@ -455,12 +462,12 @@ def rank_program(g, core, T, topo):
         u = t + 1
         pick(("W%d" % u, 0, 256), ("W%d" % t, 0, 1024), W("U%d" % t))
         exchange(u)
-        cl = caps(t)
-        for f in [D(neighbours, u, 0)] + cl[:3] + [D(neighbours, u, 1)] + cl[3:5]: f()
-        local(u, cl[5:])
-        for f in prefer(): f()
-        if u == 1: numbers(2)
-        else:
+        for h in range(2): rsum(("mP", h, h + 1), ("mB", 8 * h, 8 * h + 8))
+        neighbours(u, 0)
+        neighbours(u, 1)
+        caps()
+        local(u)
+        if u == R - 1:
             rows(0, "s")
             store(0)
         choose(u)
@@ -468,17 +475,20 @@ def rank_program(g, core, T, topo):
     t = R - 1
     pick(("H", 0, 256), ("W%d" % t, 0, 1024), W("U%d" % t))
     pick(("Z", 0, 256), ("H", 0, 256), W("posU"))
-    rows(t, "v")
+    gather(W("PRp%d" % t), W("NR"), W("U%d" % t))
     need("y", [("Zc", 0, 256)], [])
     g.sync.dma_start(T.oc[:, :], octets(("Zc", 0, 256))).then_inc(T.sem.st, 16)
-    mm(0, 256, ("wq", 0, 128), ("Z", 0, 256))
+    for h in range(2): mm(h, 128, ("wq", 0, 128), ("Z", 128 * h, 128 * h + 128))
     need("y", [("Zs", 0, 256)], [])
     for k in range(4): g.sync.dma_start(T.osc[4 * k:4 * k + 4, :], T.Zs[32 * k:32 * k + 4, 0:256]).then_inc(T.sem.st, 16)
-    cp(W("yo"), ("ps0", 0, 256), "s")
-    need("s", [W("yo")], [])
-    g.scalar.dma_start(T.y[:, :], ap(W("yo"))).then_inc(T.sem.st, 16)
+    for h in range(2):
+        half = ("yo", 128 * h, 128 * h + 128)
+        cp(half, ("ps%d" % h, 0, 128), "sv"[h])
+        need("sy"[h], [half], [])
+        queues["sy"[h]].dma_start(T.y[:, 128 * h:128 * h + 128], ap(half)).then_inc(T.sem.st, 16)
+    gather(W("PRn%d" % t), W("PRp%d" % t), W("posU"))
     store(t)
-    g.sync.wait_ge(T.sem.st, 16 * (6 + R))
+    g.sync.wait_ge(T.sem.st, 16 * (7 + R))
     g.wait_ge(T.sem.ls, sent[0])
     for q, sem in qsem.items():
         if known["g"].get(sem, 0) < count[sem]: g.wait_ge(T.sem[sem], count[sem])

from concourse.bass import DstId, RemoteDMATransfer
from concourse.mybir import dt, AluOpType as A, AxisListType, ActivationFunctionType as AF

P, F, R = 256, 48, 3
FAR = {1: (0, 48), 3: (160, 208), 2: (208, 256)}
LOC = (48, 160)
BIG = 1e29
BANKS = ((4, 5, 6, 7), (4, 5, 6, 7), (2, 3, 0, 1))
VPARTS = (0, 1)
AHEAD = (("u", 0, 0), ("u", 0, 1), ("u", 0, 2), ("u", 0, 3))
BESIDE = (("q", 0), ("u", 2, 0), ("u", 2, 1), ("u", 1, 0), ("u", 1, 1), ("u", 1, 2), ("u", 1, 3), ("q", 1), ("l",), ("u", 2, 2), ("u", 2, 3))
AFTER = (("q", 2),)


def _bufs():
    b = {}
    def sb(name, n, d="float32"): b[name] = ("sbuf", [128, n], d)
    def mx(name, n):
        sb(name + "c", n, "float8_e4m3fn_x4")
        sb(name + "s", n, "uint8")
    sb("nbT", 48, "int32"); sb("xb", 1024, "bfloat16"); sb("wb", 512, "bfloat16")
    mx("X", 256); mx("wq", 128); mx("E", 512); mx("H", 256); mx("Z", 256)
    for t in range(R):
        mx("W%d" % t, 1024); mx("N%d" % t, 512); mx("M%d" % t, 256)
        sb("fl%d" % t, 4); sb("m01_%d" % t, 2); sb("RC%d" % t, 272, "bfloat16"); sb("U%d" % t, 16, "uint16")
        for name in ("S0_", "S1_", "Ls"): sb("%s%d" % (name, t), 64)
        sb("PRp%d" % t, 256); sb("PRn%d" % t, 256)
    for k in range(3): sb("h%d" % k, 1024, "bfloat16")
    sb("hE", 516, "bfloat16"); sb("Ho", 1024, "bfloat16")
    for name, n in (("pI", 1), ("rI", 1), ("gI", 1), ("uI", 1), ("aP", 1), ("yI", 256), ("wI", 256), ("rhoI", 1), ("zI", 48),
                    ("lP", 48), ("aI", 48), ("nbI", 48), ("kI", 32), ("kA", 32)): sb(name, n, "int32")
    for name, n in (("pF", 1), ("I", 128), ("mF", 256), ("rF", 1), ("g16", 1), ("gG", 1), ("rho", 1), ("o48", 48), ("z48", 48), ("z3", 48), ("M48", 48),
                    ("Fw", 1024), ("mk", 48), ("t2a", 16), ("T2", 16), ("RK", 256), ("dk", 256), ("nK", 2), ("sg", 2), ("jk", 512), ("Tn", 16), ("c0", 32),
                    ("kh", 32), ("k1", 32), ("kap", 32), ("hP", 48), ("kP", 48), ("lQ", 64), ("kP0", 1), ("mk0", 2), ("MS", 3), ("NP", 6), ("dN", 2), ("Bm", 48), ("c8", 48),
                    ("dg", 792), ("dh", 792), ("Sc", 6), ("ge", 2), ("c01", 2), ("d2c", 2), ("gt", 2), ("ga", 2), ("A2", 2), ("Qf", 3), ("Tf", 3), ("ckB", 6), ("ngB", 2), ("mB", 16), ("mP", 2), ("ckm", 6),
                    ("EB", 48), ("io", 1032), ("Rn", 768), ("NR", 1024), ("yo", 256)): sb(name, n)
    for name, n in (("TS", 64), ("TT", 64), ("Rp", 256), ("dA", 256), ("tA", 256), ("iJ", 256), ("Rpi", 256), ("tI", 256), ("dB", 256), ("tB", 256), ("Rpn", 256), ("Rq", 768), ("d2", 768), ("t2", 768),
                    ("TC", 64), ("TD", 64), ("RO", 256), ("ROt", 256), ("RT", 256), ("RV", 256), ("RVt", 256)): sb(name, n, "bfloat16")
    for name, n in (("T2u", 16), ("lA", 16), ("lB", 16), ("lM", 16), ("posU", 16), ("piU", 16), ("nbL", 48), ("nbU", 48), ("lG", 48), ("lN", 48), ("nU", 32), ("n2U", 8), ("LV", 16), ("CLd", 16)): sb(name, n, "uint16")
    for i in range(8): b["ps%d" % i] = ("psum", [128, 512], "float32")
    return b


def _pack(b):
    out, place, fill = {}, {}, {"float32": 0, "int32": 0, "uint16": 0, "bfloat16": 0}
    fixed = ("nbT", "xb", "wb", "hE", "pF", "mF", "I", "Ho", "h0", "h1", "h2", "fl0", "fl1", "fl2", "m01_0", "m01_1", "m01_2")
    for name, (where, shape, d) in b.items():
        place[name] = (name, 0)
        if where != "sbuf" or d not in fill or name in fixed: out[name] = (where, shape, d)
        else:
            place[name] = ("pool_" + d, fill[d])
            fill[d] += (shape[1] + 31) // 32 * 32
    for d, n in fill.items(): out["pool_" + d] = ("sbuf", [128, n], d)
    return out, place


SCRATCH, PLACE = _pack(_bufs())
WIDTH = {k: v[1][1] for k, v in _bufs().items()}
SEMAPHORES = ["qv", "qs", "qt", "qg", "ldn", "ldx", "ldw", "ls", "st"] + ["x%s%d" % (k, t) for k in "csm" for t in range(R)]


def shares(T, topo, core):
    peer = {d: T.cores[T.rank_of(core) ^ d] for d in FAR}
    may = {d: topo.engines(core, c) for d, c in peer.items()}
    away = [d for d in FAR if topo.chip(peer[d]) != topo.chip(core)]
    eng, used = {}, []
    for d in sorted(FAR, key=lambda d: (d not in away, d)):
        free = [e for e in may[d] if e not in used]
        eng[d] = free[:len(may[d]) // len(away)] if d in away else free[::2][:4]
        used += eng[d]
    return peer, eng


def rank_program(g, core, T, topo):
    rank = T.rank_of(core)
    if rank is None: return
    queues = {"v": g.vector, "s": g.scalar, "t": g.tensor, "g": g, "y": g.sync}
    qsem = {"v": "qv", "s": "qs", "t": "qt", "g": "qg"}
    count = {k: 0 for k in qsem.values()}
    known = {q: {} for q in queues}
    writes, reads = {}, {}

    def norm(r): return (r[0], r[1], r[2], r[3] if len(r) > 3 else 1)

    def clash(x, y):
        if x[2] <= y[1] or y[2] <= x[1]: return False
        if x[3] == y[3]: return x[3] == 1 or (x[1] - y[1]) % x[3] == 0
        if x[3] > 1 and y[3] > 1: return True
        (s, a, b), (c, e) = ((x[3], x[1], x[2]), y[1:3]) if x[3] > 1 else ((y[3], y[1], y[2]), x[1:3])
        return a + max(0, -((a - c) // s)) * s < min(b, e)

    def need(q, rd, wr, acc=False):
        evs = []
        for r in map(norm, rd): evs += [e for w, e in writes.get(r[0], []) if clash(w, r)]
        for r in map(norm, wr):
            evs += [e for w, e in writes.get(r[0], []) if clash(w, r) and not (acc and e[3] == "t")]
            evs += [e for w, e in reads.get(r[0], []) if clash(w, r)]
        evs.sort(key=lambda e: -e[1])
        for sem, val, snap, _q in evs:
            if known[q].get(sem, 0) >= val: continue
            queues[q].wait_ge(T.sem[sem], val)
            known[q][sem] = val
            for k, v in snap.items(): known[q][k] = max(known[q].get(k, 0), v)

    def note(ev, rd, wr):
        for r in rd: reads.setdefault(r[0], []).append((norm(r), ev))
        for r in map(norm, wr):
            inside = lambda w: w[1] >= r[1] and w[2] <= r[2] and r[3] == 1
            writes[r[0]] = [(w, e) for w, e in writes.get(r[0], []) if not inside(w)] + [(r, ev)]
            reads[r[0]] = [(w, e) for w, e in reads.get(r[0], []) if not inside(w)]

    def run(q, fn, rd, wr, acc=False):
        need(q, rd, wr, acc)
        sem = qsem[q]
        count[sem] += 1
        fn(queues[q]).then_inc(T.sem[sem], 1)
        note((sem, count[sem], dict(known[q]), q), rd, wr)

    def arrives(sem, val, wr): note((sem, val, {}, "d"), [], wr)

    def ap(r, p=None):
        name, a, b, st = norm(r)
        buf, o = PLACE[name]
        rows = slice(p[0], p[1]) if p else slice(None)
        return T[buf][rows, o + a:o + b:st] if st != 1 else T[buf][rows, o + a:o + b]

    def words(r): return ap(r).bitcast(dt.uint32)
    def octets(r): return ap(r).bitcast(dt.uint8)
    def W(n): return (n, 0, WIDTH[n])
    def sc(s): return ap(s) if isinstance(s, tuple) else s
    def tt(out, in0, in1, op): run("v", lambda e: e.tensor_tensor(ap(out), ap(in0), ap(in1), op), [in0, in1], [out])
    def ts(out, in0, s1, op0, s2=None, op1=None):
        rd = [in0] + [s for s in (s1, s2) if isinstance(s, tuple)]
        if op1 is None: run("v", lambda e: e.tensor_scalar(ap(out), ap(in0), sc(s1), None, op0), rd, [out])
        else: run("v", lambda e: e.tensor_scalar(ap(out), ap(in0), sc(s1), sc(s2), op0, op1), rd, [out])
    def cp(out, in_, q="v"):
        if q == "v": run("v", lambda e: e.tensor_copy(ap(out), ap(in_)), [in_], [out])
        else: run("s", lambda e: e.activation(ap(out), ap(in_), AF.Copy), [in_], [out])
    def plus(out, in_, bias, scale=1.0):
        rd = [in_] + [x for x in (bias, scale) if isinstance(x, tuple)]
        run("s", lambda e: e.activation(ap(out), ap(in_), AF.Identity, bias=sc(bias), scale=sc(scale)), rd, [out])
    def times(out, in_, col): run("s", lambda e: e.activation(ap(out), ap(in_), AF.Copy, scale=ap(col)), [in_, col], [out])
    def ms(out, c): run("v", lambda e: e.memset(ap(out), c), [], [out])
    def rsum(out, in_, negate=False): run("v", lambda e: e.tensor_reduce(ap(out), ap(in_), AxisListType.X, A.add, negate=negate), [in_], [out])
    def tp(out, in_): run("v", lambda e: e.transpose(ap(out), ap(in_)), [in_], [out])
    def gather(out, win, off, q="v"):
        if q == "v": run("v", lambda e: e.tensor_copy(ap(out), ap(win).indirect(ap(off))), [win, off], [out])
        else: run("s", lambda e: e.activation(ap(out), ap(win).indirect(ap(off)), AF.Copy), [win, off], [out])
    def pick(out, win, off, what="cs"):
        oc, wc, os_, ws = [(r[0] + x, r[1], r[2]) for x in "cs" for r in (out, win)]
        if "c" in what: run("v", lambda e: e.tensor_copy(words(oc), words(wc).indirect(ap(off))), [wc, off], [oc])
        if "s" in what: run("s", lambda e: e.activation(ap(os_), ap(ws).indirect(ap(off)), AF.Copy), [ws, off], [os_])
    def quant(out, in_):
        c, s = (out[0] + "c", out[1], out[2]), (out[0] + "s", out[1], out[2])
        run("v", lambda e: e.quantize_mx(ap(c), ap(s), ap(in_)), [in_], [c, s])
    def mm(bank, n, w, x, start=True, stop=True):
        wc, ws, xc, xs = (w[0] + "c", w[1], w[2]), (w[0] + "s", w[1], w[2]), (x[0] + "c", x[1], x[2]), (x[0] + "s", x[1], x[2])
        run("t", lambda e: e.matmul_mx(ap(("ps%d" % bank, 0, n)), ap(wc), ap(ws), ap(xc), ap(xs), start, stop), [wc, ws, xc, xs], [("ps%d" % bank, 0, 512)], acc=not start)
    def iota(out, pattern, base, cm):
        if PLACE[out[0]][0] == "pool_int32": run("g", lambda e: e.iota(ap(out), pattern, base, cm), [], [out])
        else: run("g", lambda e: e.iota(ap(out), pattern, base, cm, allow_small_or_imprecise_dtypes=True), [], [out])
    def settle():
        if known["g"].get("qg", 0) < count["qg"]: g.wait_ge(T.sem.qg, count["qg"])
        known["g"]["qg"] = count["qg"]
    def pb(out, in_, p): run("g", lambda e: e.partition_broadcast(ap(out), ap(in_, (p, p + 1)), 128), [in_], [out])
    def spread(row, col):
        settle()
        for a in range(4): pb((row, 64 * a, 64 * a + 64), (col, 0, 64), 32 * a)
    def D(f, *a): return lambda: f(*a)
    def weave(*chains):
        for i in range(max(map(len, chains))):
            for c in chains:
                if i < len(c): c[i]()

    peer, eng = shares(T, topo, core)
    incoming = sum(len(shares(T, topo, c)[1][d]) for d, c in peer.items())
    sent = [0]

    def send(what, sem):
        tr = []
        for d in eng:
            src, dst, region = what(d)
            need("g", [region], [])
            rid, pid, _s = topo.addr(peer[d])
            tr.append(RemoteDMATransfer(dst_ids=[DstId(rid=rid, pnc=pid)], dma_engine_mask=sum(1 << e for e in eng[d]), remote_sem=T.sem[sem], src=src, dst=dst))
            sent[0] += len(eng[d])
        g.remote_dma_fused(tr, local_sem=T.sem.ls)

    for i in range(8):
        q = g.sync if i % 2 == 0 else g.scalar
        q.dma_start(T.nbT[16 * i:16 * i + 16, :], T.nb[:, :]).then_inc(T.sem.ldn, 16)
    arrives("ldn", 128, [W("nbT")])
    g.sync.dma_start(T.xb[:, :], T.x[:, :]).then_inc(T.sem.ldx, 16)
    arrives("ldx", 16, [W("xb")])
    g.sync.dma_start(T.wb[:, :], T.w[:, :]).then_inc(T.sem.ldw, 16)
    arrives("ldw", 16, [W("wb")])

    iota(W("pI"), [[0, 1]], 0, 1)
    iota(W("o48"), [[0, 16], [1, 3]], 0, 0)
    iota(W("pF"), [[0, 1]], 0, 1)
    iota(W("mF"), [[1, 256]], 0, 0)
    iota(W("yI"), [[256, 16], [11, 16]], 10, 0)
    iota(W("c8"), [[0, 6], [1, 8]], 0, 0)
    for q in (3, 0, 1, 2):
        c, r = q ^ rank ^ 1, ("Fw", 256 * q, 256 * q + 256)
        if q == 3: ms(r, 1048576.0 * c)
        elif q < rank: plus(r, W("mF"), 1048576.0 * c, 4096.0)
        else: plus(r, W("mF"), 1048576.0 * c, 0.0)
    cp(W("iJ"), W("mF"), "s")
    for q in range(4): plus(("io", 256 * q, 256 * q + 256), W("mF"), 256.0 * q)
    plus(("io", 1024, 1032), ("mF", 0, 8), 1024.0)
    plus(("NR", 0, 256), W("mF"), -1.0, 0.0)

    def kappa(v, ai, h, s, out):
        return [D(ts, h, v, 128.0, A.is_ge, 96.0, A.mult), D(ts, ai, v, 96, A.bitwise_and), D(tt, s, v, ai, A.add), D(tt, out, s, h, A.subtract)]

    ts(W("rI"), W("pI"), 15, A.bitwise_and)
    ts(W("gI"), W("pI"), 4, A.logical_shift_right)
    cp(W("rF"), W("rI"))
    ts(W("uI"), W("gI"), 1, A.bitwise_and)
    weave([D(ts, W("z48"), W("o48"), W("rF"), A.add, 1.0, A.add), D(ts, W("zI"), W("z48"), 1.0 / 3.0, A.mult), D(ts, W("z3"), W("zI"), 3.0, A.mult), D(tt, W("M48"), W("z3"), W("z48"), A.is_equal)],
          [D(ts, W("rhoI"), W("rF"), 3.0, A.mult, 2.0, A.add), D(ts, W("rhoI"), W("rhoI"), 15, A.bitwise_and), D(cp, W("rho"), W("rhoI"))],
          [D(ts, W("g16"), W("uI"), 16.0, A.mult), D(ms, W("TS"), 0.0), D(ms, W("TC"), 0.0)])

    weave([D(tt, W("mk"), W("nbT"), W("M48"), A.mult), D(tt, W("t2a"), ("mk", 0, 48, 3), ("mk", 1, 48, 3), A.add), D(tt, W("T2"), W("t2a"), ("mk", 2, 48, 3), A.add), D(cp, W("T2u"), W("T2"))],
          [D(ts, W("wI"), W("yI"), 3855, A.bitwise_and), D(ts, W("I"), ("mF", 0, 128), W("pF"), A.is_equal)])
    run("v", lambda e: e.tensor_tensor(ap(W("RK")), ap(W("Fw")).indirect(ap(W("T2u"))), ap(W("wI")), A.add), [W("Fw"), W("T2u"), W("wI")], [W("RK")])
    cp(W("nbU"), W("nbT"))
    for h in range(2): tt(("dk", 128 * h, 128 * h + 128), ("RK", 128 * h, 128 * h + 128), W("I"), A.mult)
    for h in range(2):
        rsum(("nK", h, h + 1), ("dk", 128 * h, 128 * h + 128), negate=True)
        jk, b, o = ("jk", 256 * h, 256 * h + 256), ("nK", h, h + 1), ("sg", h, h + 1)
        run("s", lambda e: e.activation(ap(jk), ap(W("RK")), AF.Sign, bias=ap(b), accum_out=ap(o)), [W("RK"), b], [jk, o])
    ms(W("hE"), 0.0)
    run("s", lambda e: e.activation(ap(("hE", 3, 515, 4)), ap(W("I")), AF.Copy, scale=0.5), [W("I")], [("hE", 3, 515, 4)])
    gather(W("Rn"), W("io"), W("nbU"), "s")
    ts(W("nbI"), W("nbT"), 255, A.bitwise_and)
    quant(("X", 0, 256), W("xb"))
    cp(W("nbL"), W("nbI"))
    ts(("TS", 0, 64, 32), W("sg"), -0.5, A.mult, 127.5, A.add)
    tp(W("TT"), W("TS"))
    spread("Rp", "TT")
    cp(("c0", 0, 16), ("mF", 0, 256, 16))
    for i in range(2): ts(("c0", 16 + i, 32, 2), ("mF", 0, 256, 32), W("g16"), A.add)
    weave([D(cp, W("kI"), W("c0"))] + kappa(W("kI"), W("kA"), W("kh"), W("k1"), W("kap")),
          [D(quant, ("E", 128 * b, 128 * b + 128), ("hE", 3 - b, 515 - b)) for b in range(4)])
    ts(W("aP"), W("pI"), 96, A.bitwise_and)
    ts(W("lA"), ("kap", 16, 32), W("rho"), A.add)
    ts(W("lM"), ("kap", 0, 16), W("rho"), A.add)
    ts(W("lB"), ("c0", 16, 32), W("rF"), A.add)
    tt(W("kP0"), W("pI"), W("aP"), A.add)
    gather(W("dA"), W("Rp"), W("lA"))
    ts(("mk0", 0, 1), W("kP0"), -256.0, A.add)
    tp(W("tA"), W("dA"))
    ts(("mk0", 1, 2), W("kP0"), -224.0, A.add)
    cp(W("posU"), ("tA", 0, 256, 16))
    ts(W("CLd"), ("kap", 16, 32), W("rF"), A.add)
    run("v", lambda e: e.tensor_copy(ap(W("Rpi")).indirect(ap(W("posU"))), ap(W("iJ"))), [W("posU"), W("iJ")], [W("Rpi")])
    def within(out, src, cm, base): run("g", lambda e: e.affine_select(ap(out), ap(src), [[0, 1]], A.is_ge, 0.0, base, cm), [src], [out])
    settle()
    within(("MS", 0, 1), ("mk0", 0, 1), -1, 47)
    within(("MS", 2, 3), ("mk0", 1, 2), 1, -80)
    within(("MS", 1, 2), ("mk0", 1, 2), 1, -32)
    settle()
    within(("MS", 1, 2), ("MS", 1, 2), -1, 79)
    gather(W("Rpn"), W("Rp"), W("lM"), "s")
    gather(W("Rq"), W("Rpn"), W("nbL"), "s")
    tp(W("tI"), W("Rpi"))
    gather(W("dB"), W("Rpi"), W("lB"), "s")
    def where(k):
        for i in range(2): ts(("lG", 16 * k + i, 16 * k + 16, 2), ("tI", 0, 256, 32), 3.0, A.mult, float(k), A.add)
    def find(k): gather(("d2", 256 * k, 256 * k + 256), W("Rq"), ("lG", 16 * k, 16 * k + 16), "s")
    def turn(k):
        tp(("t2", 256 * k, 256 * k + 256), ("d2", 256 * k, 256 * k + 256))
        cp(("nU", 16 * k, 16 * k + 16), ("t2", 256 * k, 256 * k + 256, 16))
    where(0)
    find(0)
    where(1)
    quant(("wq", 0, 128), W("wb"))
    tp(W("tB"), W("dB"))
    ts(("lQ", 48, 64), ("kap", 0, 16), W("rF"), A.add)
    cp(W("piU"), ("tB", 0, 256, 16))
    ts(W("Tn"), ("mF", 0, 256, 16), W("rF"), A.add)
    pick(("W0", 0, 256), ("X", 0, 256), W("piU"))

    def exchange(t):
        for kind in "cs":
            def what(d):
                own, far = [("%s%d%s" % (n, t, kind),) + FAR[d] for n in "WM"]
                return (octets(own), octets(far), own) if kind == "c" else (ap(own), ap(far), own)
            send(what, "x%s%d" % (kind, t))
            arrives("x%s%d" % (kind, t), incoming, [("M%d%s" % (t, kind), a, b) for a, b in FAR.values()])

    def neighbours(t, k): pick(("N%d" % t, 256 * k, 256 * k + 256), ("W%d" % t, 0, 256), ("nU", 16 * k, 16 * k + 16))

    def neighbours2(t, what="cs"): pick(("M%d" % t,) + LOC, ("W%d" % t, 0, 256), ("n2U", 0, 7), what)

    def product(t, k, h, bank):
        mov = ("N%d" % t, 256 * k + 128 * h, 256 * k + 128 * h + 128) if k < 2 else ("M%d" % t, 128 * h, 128 * h + 128)
        mm(bank, 128, ("W%d" % t, 128 * h, 128 * h + 128), mov)

    def mask(k, h, bank): tt(("dg", 132 * (2 * k + h), 132 * (2 * k + h) + 128), ("ps%d" % bank, 0, 128), W("I"), A.mult)

    def total(k, h, q):
        i = 2 * k + h
        d, s, j = ("dg", 132 * i, 132 * i + 129), ("Sc", i, i + 1), ("dh", 132 * i, 132 * i + 129)
        if q == "s": run("s", lambda e: e.activation(ap(j), ap(d), AF.Copy, accum_out=ap(s)), [d], [j, s])
        else: rsum(s, d)

    def halves(t, parts):
        for b in parts: mm(BANKS[0][b], 256, ("E", 128 * b, 128 * b + 128), ("W%d" % t, 0, 256), True, b in VPARTS)

    def keep():
        for b in VPARTS: cp(("Ho", b, 1024, 4), ("ps%d" % BANKS[0][b], 0, 256), "s")

    def unpack(t, k, b):
        mov = ("N%d" % t, 256 * k, 256 * k + 256) if k < 2 else ("M%d" % t, 0, 256)
        e, bank, alone = ("E", 128 * b, 128 * b + 128), BANKS[k][b], b in VPARTS
        if k and not alone: mm(bank, 256, e, ("W%d" % t, 0, 256), True, False)
        mm(bank, 256, e, mov, alone, True)
        out, half = ("h%d" % k, b, 1024, 4), ("ps%d" % bank, 0, 256)
        if alone: tt(out, half, ("Ho", b, 1024, 4), A.add)
        else: cp(out, half, "s")

    def candidate(t, k): quant(("W%d" % t, 256 * (k + 1), 256 * (k + 2)), W("h%d" % k))

    def lists(t):
        tp(W("RT"), ("RC%d" % t, 0, 256))
        for h in range(2):
            for s in range(2): cp(("LV", 8 * h + s, 8 * h + 8, 2), ("RT", 32 * h, 256, 64))

    def shadow(t, items):
        for i in items:
            if i[0] == "u": unpack(t, i[1], i[2])
            elif i[0] == "q": candidate(t, i[1])
            else: lists(t)

    def local(t, middle=()):
        halves(t, (0, 1))
        for k in range(2):
            for h in range(2): product(t, k, h, 2 * k + h)
        halves(t, (2, 3))
        keep()
        for h in range(2): mask(0, h, h)
        if t:
            cl = ("dg", 128, 792, 132)
            tt(cl, cl, W("ckm"), A.add)
            neighbours2(t, "c")
        for h in range(2): total(0, h, "s")
        mask(1, 0, 2)
        total(1, 0, "s")
        mask(1, 1, 3)
        if t: neighbours2(t, "s")
        total(1, 1, "v")
        for f in middle: f()
        m, fl = "m01_%d" % t, "fl%d" % t
        tt(W(m), ("Sc", 0, 2), ("Sc", 2, 4), A.max)
        def what(d):
            r = (m, FAR[d][0] // 128, FAR[d][0] // 128 + 1)
            return ap(r), ap((fl, d, d + 1)), r
        send(what, "xm%d" % t)
        arrives("xm%d" % t, incoming, [W(fl)])
        tt(W("ge"), ("Sc", 0, 2), ("Sc", 2, 4), A.is_ge)

    def prefer():
        for h in range(2): plus(("c01", h, h + 1), ("ge", h, h + 1), ("NP", 2 + h, 3 + h), ("dN", h, h + 1))
        for h in range(2): plus(("d2c", h, h + 1), ("c01", h, h + 1), ("NP", 4 + h, 5 + h), -1.0)

    def choose(t):
        fl, m = "fl%d" % t, "m01_%d" % t
        if t:
            prefer()
            shadow(t, AHEAD)
        for h in range(2): product(t, 2, h, h)
        ready(t)
        if t == 0:
            for k in range(3): numbers(k)
            prefer()
        for h in range(2): mask(2, h, h)
        for h in range(2): total(2, h, "v")
        tt(W("gt"), ("Sc", 4, 6), W(m), A.is_gt)
        tt(W("ga"), W("gt"), W("d2c"), A.mult)
        ts(("Qf", 1, 3), ("MS", 1, 3), ("gt", 1, 2), A.mult)
        ts(("Qf", 0, 1), ("MS", 0, 1), ("gt", 0, 1), A.mult)
        tt(W("A2"), W("ga"), W("c01"), A.add)
        for i, d, h in ((1, 3, 1), (2, 2, 1), (0, 1, 0)): ts(("Tf", i, i + 1), (fl, d, d + 1), ("Sc", 4 + h, 5 + h), A.is_lt, ("Qf", i, i + 1), A.mult)
        ts(("TC", 32, 33), ("A2", 1, 2), ("Tf", 1, 2), A.add, ("Tf", 2, 3), A.add)
        tt(("TC", 0, 1), ("A2", 0, 1), ("Tf", 0, 1), A.add)
        tp(W("TD"), W("TC"))
        spread("RC%d" % t, "TD")
        shadow(t, BESIDE)

    def ready(t):
        for i, c in enumerate((0.0, 0.5, 512.0)): plus(("S0_%d" % t, i, 64, 4), ("mF", 0, 16), c, 0.0)
        plus(("S1_%d" % t, 2, 64, 4), ("mF", 0, 16), 256.0, 0.0)
        cp(("S1_%d" % t, 3, 64, 4), W("Tn"), "s")
        plus(("RC%d" % t, 256, 272), ("mF", 0, 16), -1.0, 0.0)

    def decide(t):
        rc, d0, d1, ls = ["%s%d" % (n, t) for n in ("RC", "S0_", "S1_", "Ls")]
        gather(W("RO"), (rc, 0, 256), W("CLd"), "s")
        gather(W("RV"), (rc, 0, 272), W("LV"), "s")
        shadow(t, AFTER)
        if t < R - 1: bars()
        else:
            rows(1, "s")
            store(1)
        tp(W("ROt"), W("RO"))
        v = ("ROt", 0, 256, 16)
        tt((d1, 0, 64, 4), v, ("lQ", 16, 32), A.is_equal)
        tt((d1, 1, 64, 4), v, ("lQ", 32, 48), A.is_equal)
        tp(W("RVt"), W("RV"))
        tt((d0, 3, 64, 4), ("RVt", 0, 256, 16), ("lQ", 48, 64), A.is_equal)
        run("v", lambda e: e.tensor_tensor_scan(ap(W(ls)), ap(W(d0)), ap(W(d1)), 0.0, A.mult, A.add), [W(d0), W(d1)], [W(ls)])
        cp(W("U%d" % t), (ls, 3, 64, 4))
        if t < R - 1: tt(W("mB"), (d0, 3, 64, 4), ("Bm", 0, 16), A.mult)

    def bars():
        plus(("ckB", 4, 6), W("gt"), 0.0, -BIG)
        plus(W("ngB"), W("gt"), -BIG, BIG)
        for h in range(2): times(("ckB", h, h + 1), ("ge", h, h + 1), ("ngB", h, h + 1))
        for h in range(2): plus(("ckB", 2 + h, 3 + h), ("ckB", h, h + 1), ("ngB", h, h + 1), -1.0)

    def caps():
        for h in range(2): times(("ckm", h, 6, 2), ("ckB", h, 6, 2), ("mP", h, h + 1))

    def numbers(k): gather(("NR", 256 * k + 256, 256 * k + 512), W("Rn"), ("lN", 16 * k, 16 * k + 16), "s")

    def rows(t, q):
        gather(W("PRp%d" % t), W("NR"), W("U%d" % t), q)
        gather(W("PRn%d" % t), W("PRp%d" % t), W("posU"), q)

    def store(t):
        need("y", [W("PRn%d" % t)], [])
        g.sync.dma_start(T.pr[t:t + 1, :], ap(W("PRn%d" % t), (0, 1))).then_inc(T.sem.st, 16)

    exchange(0)
    find(1)
    turn(0)
    neighbours(0, 0)
    turn(1)
    neighbours(0, 1)
    where(2)
    find(2)
    ts(("dg", 128, 792, 132), ("mF", 0, 6), 0.0, A.mult)
    for k in range(3): ts(("lN", 16 * k, 16 * k + 16), ("tB", 0, 256, 16), 3.0, A.mult, float(k), A.add)
    l0, l1 = LOC[0] // 16, LOC[1] // 16
    local(0, [D(tp, ("t2", 512, 768), ("d2", 512, 768)), D(cp, ("lP", 0, 32), ("t2", 0, 512, 16)), D(cp, W("gG"), W("gI")), D(cp, ("n2U", 0, 7), ("t2", 512 + LOC[0], 512 + LOC[1], 16)),
        D(cp, ("lP", 32 + l0, 32 + l1), ("t2", 512 + LOC[0], 512 + LOC[1], 16)), D(cp, ("lP", 32, 32 + l0), ("Tn", 0, l0)), D(cp, ("lP", 32 + l1, 48), ("Tn", l1, 16))])
    ts(W("Bm"), W("c8"), W("gG"), A.is_equal)
    weave(kappa(W("lP"), W("aI"), W("hP"), W("kP"), ("lQ", 0, 48)), [D(neighbours2, 0)] + [D(shadow, 0, (i,)) for i in AHEAD])
    tt(W("EB"), ("lQ", 0, 48), W("Bm"), A.mult)
    for i in range(6): rsum(("NP", i, i + 1), ("EB", 8 * i, 8 * i + 8))
    tt(("NP", 4, 6), ("NP", 4, 6), ("MS", 0, 2), A.subtract)
    tt(W("dN"), ("NP", 0, 2), ("NP", 2, 4), A.subtract)
    tt(("NP", 5, 6), ("NP", 5, 6), ("MS", 2, 3), A.subtract)
    choose(0)

    for t in range(R):
        decide(t)
        if t == R - 1: break
        u = t + 1
        pick(("W%d" % u, 0, 256), ("W%d" % t, 0, 1024), W("U%d" % t))
        exchange(u)
        for h in range(2): rsum(("mP", h, h + 1), ("mB", 8 * h, 8 * h + 8))
        neighbours(u, 0)
        neighbours(u, 1)
        caps()
        local(u)
        if u == R - 1:
            rows(0, "s")
            store(0)
        choose(u)

    t = R - 1
    pick(("H", 0, 256), ("W%d" % t, 0, 1024), W("U%d" % t))
    pick(("Z", 0, 256), ("H", 0, 256), W("posU"))
    gather(W("PRp%d" % t), W("NR"), W("U%d" % t))
    need("y", [("Zc", 0, 256)], [])
    g.sync.dma_start(T.oc[:, :], octets(("Zc", 0, 256))).then_inc(T.sem.st, 16)
    for h in range(2): mm(h, 128, ("wq", 0, 128), ("Z", 128 * h, 128 * h + 128))
    need("y", [("Zs", 0, 256)], [])
    for k in range(4): g.sync.dma_start(T.osc[4 * k:4 * k + 4, :], T.Zs[32 * k:32 * k + 4, 0:256]).then_inc(T.sem.st, 16)
    for h in range(2):
        half = ("yo", 128 * h, 128 * h + 128)
        cp(half, ("ps%d" % h, 0, 128), "sv"[h])
        need("sy"[h], [half], [])
        queues["sy"[h]].dma_start(T.y[:, 128 * h:128 * h + 128], ap(half)).then_inc(T.sem.st, 16)
    gather(W("PRn%d" % t), W("PRp%d" % t), W("posU"))
    store(t)
    g.sync.wait_ge(T.sem.st, 16 * (7 + R))
    g.wait_ge(T.sem.ls, sent[0])
    for q, sem in qsem.items():
        if known["g"].get(sem, 0) < count[sem]: g.wait_ge(T.sem[sem], count[sem])
